import numpy as np, ml_dtypes
CORES = [8,136,40,168]
N = 4
BF = ml_dtypes.bfloat16
def gentries(a):
    return np.ascontiguousarray(a.reshape(8, 16, -1).transpose(0, 2, 1)).reshape(8, -1)
def gtable(e):
    e = np.asarray(e); return np.ascontiguousarray(e.reshape(8, -1, 16).transpose(0, 2, 1)).reshape(128, -1).astype(np.int32)
W, SB, P, HOPS, STEP, GAIN = 2048, 11, 192, 5, 3, 8
def parts(rng):
    x = rng.integers(0, 64, (N, 8, 16, W)); n = rng.integers(0, W, (N, 8, 16, W))
    s = rng.integers(0, rng.integers(2, 9, (N, 8, 1, W)) + 1, (N, 8, 16, W))
    return x, n, s, rng.integers(0, W, (N, 8, P)), rng.integers(0, 64, (N, 8, 16, P)), rng.integers(1, 256, (N, 8, 16, 1))
def lonely(rng, n, s, v, old, few, start):
    for q in range(N):
        for g in range(8):
            o = rng.permutation(W); a = o[:old]; b = o[old:old + few]
            s[q, g][:, a] = 0; n[q, g][:, b] = a[rng.integers(0, old, (16, few))]
            v[q, g, rng.permutation(P)[:start]] = b[rng.integers(0, few, start)]
def scarce(rng, n, s, v):
    lone = np.zeros((N, 8), np.int64); sh = int(rng.integers(0, 4))
    for q in range(N):
        for g in range(8):
            a, b = [int(m) for m in rng.permutation(W)[:2]]
            n[q, g][:, a] = b; s[q, g][:, b] = 0; lone[q, g] = a
    live = np.any(np.take_along_axis(s, n, 3) > 0, axis=2)
    for q in range(N):
        for g in range(8):
            c = np.flatnonzero(live[q, g])
            v[q, g] = np.where(live[q, g, v[q, g]], v[q, g], c[rng.integers(0, len(c), P)])
        for m in rng.permutation(8 * P)[:(q + sh) & 3]:
            g = int(m) // P; v[q, g, int(m) - g * P] = lone[q, g]
def plant(rng, x, n, s, v, z):
    for q in range(N):
        for g in range(8):
            o = [int(m) for m in 1 + rng.permutation(W - 1)[:25]]; X, M, S, Z = x[q, g], n[q, g], s[q, g], z[q, g]
            a, b, c = o[:3]
            M[:, 0] = c; S[:, c] = 0; Z[:, 0] = 0; v[q, g, 0] = 0
            M[:, a] = b; M[:, b] = 0; S[:, b] = rng.integers(1, 9, 16); v[q, g, 1] = a
            for p, j in ((2, 3), (P - 1, 9)):
                a, b, c, d1, d2, d3 = o[j:j + 6]; r = 63 * rng.integers(0, 2, 16)
                Z[:, p] = r; v[q, g, p] = a; M[:, a] = c; M[0, a] = b
                S[:, b] = rng.integers(1, 9, 16); S[15, b] = 0; M[0, b] = d3
                S[:, c] = rng.integers(1, 9, 16); M[:, c] = d1; M[15, c] = d2
                X[:, d1] = r; X[:, d2] = r; X[:, d3] = r; X[15, d1] = r[15] ^ 1
            for p, j in ((3, 15), (P - 2, 20)):
                a, b, c, d, h = o[j:j + 5]; r = 63 * rng.integers(0, 2, 16); k = int(rng.integers(1, 16))
                Z[:, p] = r; v[q, g, p] = a; M[:, a] = c; M[0, a] = b
                S[:, b] = rng.integers(1, 9, 16); S[0, b] = 0; M[0, b] = d; X[:, d] = r
                S[:, c] = 0; S[k, c] = int(rng.integers(1, 9)); M[k, c] = h; X[:, h] = 63 - r
def pack(x, e, v, z, w):
    return {"xs": np.ascontiguousarray(x.reshape(N, 128, W)).astype(np.float32).astype(BF), "en": np.ascontiguousarray(e.reshape(N, 128, W)).astype(np.int32),
            "v0": np.stack([gtable(a) for a in v]), "z0": np.ascontiguousarray(z.reshape(N, 128, P)).astype(np.float32).astype(BF), "wt": np.ascontiguousarray(w.reshape(N, 128, 1)).astype(np.int32)}
def setup_inputs(rng):
    x, n, s, v, z, w = parts(rng)
    lonely(rng, n, s, v, W // 8, W // 16, P // 8)
    return pack(x, n + W * s, v, z, w)
def setup_inputs_spread(rng):
    x, n, s, v, z, w = parts(rng)
    ex = rng.choice(np.array([0.25, 1.0, 4.0]), (N, 8, 1, W)); es = rng.choice(np.array([0.25, 1.0, 4.0]), (N, 8, 1, W)); en = rng.choice(np.array([1.0, 3.0]), (N, 8, 1, W))
    x = (64 * rng.random(x.shape) ** ex).astype(np.int64); s = (9 * rng.random(x.shape) ** es).astype(np.int64); n = (W * rng.random(x.shape) ** en).astype(np.int64)
    x = np.minimum(x, 63); s = np.minimum(s, 8); n = np.minimum(n, W - 1)
    v = np.minimum((W * rng.random(v.shape) ** 2).astype(np.int64), W - 1)
    z = np.minimum((64 * rng.random(z.shape) ** rng.choice(np.array([0.25, 1.0, 4.0]), (N, 8, 1, P))).astype(np.int64), 63)
    w = np.minimum(1 + (255 * rng.random(w.shape) ** 4).astype(np.int64), 255)
    scarce(rng, n, s, v)
    return pack(x, n + W * s, v, z, w)
def setup_inputs_ends(rng):
    x, n, s, v, z, w = parts(rng); hi = 9 * W - 1
    x = 63 * rng.integers(0, 2, x.shape); z = 63 * rng.integers(0, 2, z.shape); w = 1 + 254 * rng.integers(0, 2, w.shape); v = (W - 1) * rng.integers(0, 2, v.shape)
    e = np.where(rng.random(x.shape) < 0.8, hi * rng.integers(0, 2, x.shape), rng.choice(np.array([1, W - 2, 8 * W, 8 * W + 1, 9 * W - 2]), x.shape))
    e[..., W - 1] = rng.choice(np.array([hi, hi, 8 * W + 1, 9 * W - 2]), (N, 8, 16)); e[:, :, 15, W - 1] = hi
    e[..., W - 3] = 0; e[:, 7, :, W - 4] = hi
    one = rng.integers(0, 16, (N, 8)); one[:, 7] = 15; one[N - 1] = 15
    e[..., 0] = np.where(np.arange(16) == one[..., None], hi, 0)
    full = 63 * rng.integers(0, 2, (N, 8, 1)); full[:, 7] = 63
    for c in (1, W - 2, W - 1): x[..., c] = full
    for p in (0, P - 1): z[..., p] = full
    for p in (1, P - 2, P - 3): z[..., p] = 63 - full
    for p in (0, 1, P - 2, P - 1): v[..., p] = W - 1
    v[..., 2] = 0; v[..., P - 3] = W - 3; w[:, 7] = 255; w[:, 0, 0] = 1
    return pack(x, e, v, z, w)
def setup_inputs_corners(rng):
    x, n, s, v, z, w = parts(rng); o = [int(a) for a in rng.permutation(8)]; col = np.arange(W); i = np.arange(16)[:, None]
    n[:, o[0]] = col
    k = rng.integers(0, 4, (N, 16, W))
    n[:, o[1]] = np.where(k == 0, 0, np.where(k == 1, W - 1, np.where(k == 2, col, (col + 1) & (W - 1))))
    h = P // 2; s[:, o[2]] = 0; w[:, o[2], 0] = 255; w[:, o[2], 1] = W // 256 - 1
    z[:, o[2], :, :h] = 0; z[:, o[2], 0, :h] = W // 256; z[:, o[2], 1, :h] = 1
    s[:, o[3]] = np.where(i < 8, i + 1, 0)
    s[:, o[4]] = np.where(i == 0, 4, np.where(i == 12, 6, np.where(i == 13, 8, 0)))
    s[:, o[5]] = np.where(i == 0, 4, np.where(i == 13, 8, 0))
    for c in (3, 4, 5): x[:, o[c]] = np.repeat(x[:, o[c], :, :1], W, axis=2)
    s[::2, o[6]] = 8; s[1::2, o[6]] = 0
    v[..., 0] = W - 1; v[..., 1] = 0; v[..., P - 1] = W - 1
    for q in range(N):
        m = rng.permutation(W - 1); a = np.append(m[:P - 1], W - 1); b = m[P - 1:2 * P - 1]
        n[q, o[7]][:, a] = b; n[q, o[7]][:, b] = b; s[q, o[7]][:, b] = rng.integers(1, 9, (16, P)); v[q, o[7]] = a
    return pack(x, n + W * s, v, z, w)
def setup_inputs_crowd(rng):
    x, n, s, v, z, w = parts(rng)
    lonely(rng, n, s, v, W // 4, W // 4, 1)
    want = (8 * P, 8 * P - 1, 255, 256); sh = int(rng.integers(0, 4))
    for q in range(N):
        bad = np.zeros(8 * P, bool); bad[rng.permutation(8 * P)[:want[(q + sh) % 4]]] = True; bad = bad.reshape(8, P)
        for g in range(8):
            a, b, c, d, hub = [int(m) for m in rng.permutation(W)[:5]]
            n[q, g, :, a] = b; s[q, g, :, b] = 8
            if g % 3 == 0: n[q, g, :, b] = a
            if g % 3 == 1: n[q, g, :, b] = hub
            n[q, g, :, c] = d; s[q, g, :, d] = 0
            v[q, g] = np.where(bad[g], c, a)
    z[:, ::2] = np.repeat(z[:, ::2, :, :1], P, axis=3)
    return pack(x, n + W * s, v, z, w)
def setup_inputs_ties(rng):
    x, n, s, v, z, w = parts(rng)
    base = rng.integers(0, 16, (N, 8, 16, 1)); proto = rng.integers(0, 4, (N, 8, W))
    x = np.repeat(base, W, axis=3); x[:, :, 0] = base[:, :, 0] + GAIN * proto
    i = np.arange(16)[:, None]; s = (i + rng.integers(0, 8, (N, 8, 1, W))) & 7
    s = np.where((rng.random((N, 8, 1, W)) < 0.5) & (s == 0) & (i < 8), 8, s)
    n = np.where(rng.random((N, 8, 1, W)) < 0.3, rng.integers(0, W, (N, 8, 1, W)), n)
    z[:, :, 0] = 63 * (rng.random((N, 8, P)) < 0.25)
    plant(rng, x, n, s, v, z)
    return pack(x, n + W * s, v, z, w)
def check_inputs(d):
    bad = []
    for k, lo, hi in (("xs", 0, 63), ("en", 0, 9 * W - 1), ("v0", 0, W - 1), ("z0", 0, 63), ("wt", 1, 255)):
        a = np.asarray(d[k]).astype(np.float64)
        if not (np.min(a) >= lo and np.max(a) <= hi): bad.append("range of " + k)
        elif np.any(a != np.floor(a)): bad.append("whole numbers of " + k)
    return bad
def reference(xs, en, v0, z0, wt):
    x = xs.astype(np.float32).astype(np.int64).reshape(N, 8, 16, W); e = en.astype(np.int64).reshape(N, 8, 16, W); w = wt.astype(np.int64).reshape(N, 8, 16, 1)
    v = np.stack([gentries(a) for a in v0]).astype(np.int64); z = z0.astype(np.float32).astype(np.int64).reshape(N, 8, 16, P)
    tau = np.zeros((N, 8, P), np.int64); A = np.zeros(N, np.int64); k16 = np.arange(16); pn = np.arange(P)
    qi = np.arange(N)[:, None, None]; gi = np.arange(8)[None, :, None]
    for t in range(HOPS):
        if t > 0: v = np.roll(v, STEP, axis=0); tau = np.roll(tau, STEP, axis=0); z = np.roll(z, STEP, axis=0)
        ring = np.take_along_axis(e, v[:, :, None, :], 3) & (W - 1)
        F = np.take_along_axis(e, ring.reshape(N, 8, 1, 16 * P), 3).reshape(N, 8, 16, 16, P)
        newer = np.count_nonzero((F >> SB) > tau[:, :, None, None, :], axis=2)
        fk = F[:, :, (k16 + t) & 15, k16]
        rec = np.take_along_axis(x, (fk & (W - 1)).reshape(N, 8, 1, 16 * P), 3).reshape(N, 8, 16, 16, P)
        score = np.add.reduce(np.abs(rec - z[:, :, :, None, :]), axis=2) - GAIN * newer
        ok = (k16[:, None] < 16 - tau[:, :, None, :]) & ((fk >> SB) > tau[:, :, None, :])
        best = np.argmin(np.where(ok, score, 2 ** 20), axis=2); found = np.any(ok, axis=2)
        fa = np.take_along_axis(fk, best[:, :, None, :], 2)[:, :, 0]
        u = np.add.reduce(w * z, axis=2) & (W - 1)
        f = np.where(found, fa & (W - 1), ((u * u >> 5) + 37 * u + A[:, None, None]) & (W - 1))
        tau = np.where(found, fa >> SB, 0)
        z = np.where(found[:, :, None, :], z, np.abs(z - np.take_along_axis(x, f[:, :, None, :], 3)))
        A = np.count_nonzero(np.logical_not(found), axis=(1, 2)) & 255
        first = np.full((N, 8, W), P, np.int64)
        np.minimum.at(first, (qi, gi, np.concatenate([v, f], axis=2)), np.concatenate([pn, pn])[None, None, :])
        stands = (f != v) & (np.take_along_axis(first, v, 2) == pn) & (np.take_along_axis(first, f, 2) == pn)
        q, g, p = np.nonzero(stands); a = v[q, g, p]; b = f[q, g, p]
        ca = e[q, g, :, a]; cb = e[q, g, :, b]
        na = np.where(k16 % 2 == 0, cb, ca); nb = np.where(k16 % 2 == 0, ca, cb)
        na[:, 15] = b + W * (9 + t); nb[:, 15] = a + W * (9 + t)
        e[q, g, :, a] = na; e[q, g, :, b] = nb
        v = f
    return {"ys": np.add.reduce(e * (k16[:, None] + 1), axis=2).astype(np.float32), "yp": (v + W * tau).astype(np.float32), "yz": z.reshape(N, 128, P).astype(np.float32).astype(BF)}

@@ -1,0 +1,576 @@
+import numpy as np
+from concourse.mybir import AluOpType as A, ActivationFunctionType as F, AxisListType as AX
+
+HOPS = 5
+HR = 128
+HX = 1536 + 16 * (HR - 96)
+G1, V1, G0 = 8, 8, 12
+CH = (1, 0)
+RB = ("pb5", "pb7")
+f4, f2, b2, i4, u2 = "float32", "float16", "bfloat16", "int32", "uint16"
+SCRATCH = {}
+OWNBUF = ("enS", "tmpB", "NT", "ST", "XS", "FV", "FF", "NTh", "YS", "YP", "YZ", "v0s", "z0s", "wts", "ZI", "X", "S", "M", "D", "AB", "ZE",
+          "VAL", "VV", "OWN", "MM", "Zz", "MO", "ZO", "RT", "OT", "RL", "AL", "POS", "NNs", "NSs")
+PLACE = {}
+
+
+def declare(name, w, t):
+    if name in OWNBUF:
+        SCRATCH[name] = ("sbuf", [128, w], t)
+        PLACE[name] = (name, 0, w)
+        return
+    pool = "pool" + t
+    a = SCRATCH[pool][1][1] if pool in SCRATCH else 0
+    SCRATCH[pool] = ("sbuf", [128, a + w + w % 2], t)
+    PLACE[name] = (pool, a, w)
+
+
+for n_, w_, t_ in (
+        ("enS", 2048, i4), ("tmpB", 2048, b2), ("NT", 2432, f4), ("ST", 2432, b2), ("XS", 2048, b2),
+        ("FV", 2064, f4), ("FF", 2064, f4), ("NTh", 2048, f2), ("YS", 2048, f4), ("YP", 192, f4), ("YZ", 192, b2),
+        ("v0s", 12, i4), ("v0f", 12, f4), ("z0s", 192, b2), ("wts", 1, i4), ("wtf", 1, f4),
+        ("ones", 192, f2), ("onef", 32, f4), ("o32", 136, f2), ("ID", 128, f2), ("NID", 128, f2), ("P64", 128, f2), ("N64", 128, f2),
+        ("I2K", 128, f2), ("IDb", 128, b2), ("I22", 128, b2), ("INK", 128, b2), ("BDt", 128, f2), ("BD", 128, f2), ("GBt", 8, f4), ("GB", 8, f4), ("GBs", 8, f4), ("GBy", 8, f4),
+        ("BAND", 160, f2), ("ZI", 2560, f2), ("qI", 1, i4), ("qJ", 1, i4), ("qK", 1, i4), ("qi", 1, f4), ("qe", 1, f4), ("q15", 1, f4),
+        ("qo", 1, f4), ("q24", 1, f4), ("qs1", 1, f4), ("TC", 1, f4), ("w1", 1, f4),
+        ("CI", 192, f4), ("RM16", 16, f4), ("WC", 16, f4), ("selB", 128, b2), ("WN", 128, b2), ("SELT", 136, f2),
+        ("W16", 8, b2), ("WD", 8, f2), ("YWn", 8, f2), ("YWs", 8, b2), ("EXPT", 136, f2), ("KTHR", 136, f4), ("BK", 136, b2),
+        ("RST", 136, f4), ("NEG", 192, f4), ("EQD", 192, f4), ("OFFD", 192, f4), ("HOLD", 192, f4), ("SEG", 192, f4), ("TR", 24, f4), ("TRb", 24, f4),
+        ("DO", 128, f2), ("DE", 128, f2), ("D15", 128, f2), ("DOb", 128, b2), ("DEb", 128, b2), ("BT", 5, f4),
+        ("GFt", 128, f2), ("GTt", 128, f2), ("GF", 128, f2), ("GT", 128, f2), ("LM", 192, f2),
+        ("vlf", 12, f4), ("FL", 192, f4), ("CN", 192, f2), ("RL", 192, u2), ("X", 3072, f2), ("S", 3072, b2), ("M", 3072, b2), ("D", 3072, b2), ("AB", 3072, b2), ("ZE", 3072, f2),
+        ("AL", 192, u2), ("TBc", 272, b2), ("ui", 16, i4), ("ua", 16, i4), ("ub", 16, i4), ("uc", 16, i4), ("ud", 16, i4), ("ue", 16, i4), ("uf", 16, i4), ("ff", 16, f2),
+        ("Af", 1, f4), ("Ai", 1, i4), ("Aj", 1, i4), ("Ac", 1, f4), ("FC", 16, f2), ("TPs", 192, f2),
+        ("Rv", 192, f2), ("Sv", 192, b2), ("Rf", 192, f2), ("Sf", 192, b2), ("G0", 192, f4), ("pre", 192, f4),
+        ("ma", 192, f4), ("mb", 192, f4), ("nd", 192, f4), ("ns", 192, f4), ("nT", 24, f4), ("nP", 24, f4), ("POS", 24, u2),
+        ("NNs", 384, f4), ("NSs", 384, b2), ("XF", 192, f2), ("AZ", 192, f2), ("FM", 192, f2), ("R1", 192, f2), ("R2", 192, f2),
+        ("VAL", 960, f4), ("VV", 960, f4), ("OWN", 960, f4),
+        ("MM", 1920, f2), ("Zz", 960, f2), ("MO", 1920, f2), ("ZO", 960, f2), ("RT", 200, u2), ("OT", 200, u2)):
+    declare(n_, w_, t_)
+for c_ in (0, 1):
+    for n_, w_, t_ in (("Mn", 136, f4), ("dd", 136, f4), ("ee", 136, f4), ("oo", 136, f4), ("WT", 16, f2), ("RMk", 96, f4),
+                       ("eq", 96, f4), ("dup", 96, f4), ("pT", 6, f4), ("pQ", 6, f4)):
+        declare(n_ + str(c_), w_, t_)
+for b_ in range(8):
+    SCRATCH["pb%d" % b_] = ("psum", [128, 512], f4)
+    PLACE["pb%d" % b_] = ("pb%d" % b_, 0, 512)
+SEMAPHORES = ["cV", "cS", "cP", "cG", "sent"] + ["ld%d" % k for k in range(8)] + ["st%d" % k for k in range(3)] + \
+    ["a%s%d" % (m, t) for m in ("M", "L", "Z0", "Z1") for t in range(1, HOPS)]
+
+
+def meet(x, y):
+    return x[1] < y[2] and y[1] < x[2] and not (x[3] == y[3] and (x[1] - y[1]) % x[3])
+
+
+def make(g, T):
+    eng = {"V": g.vector, "S": g.scalar, "P": g.tensor, "G": g, "Y": g.sync}
+    cnt = {"V": 0, "S": 0, "P": 0, "G": 0}
+    clk = {q: {} for q in eng}
+    snap, acc = {}, {}
+
+    def semof(r):
+        return T.sem["c" + r] if r in cnt else T.sem[r]
+
+    def B(name, a=None, b=None, step=1, r0=0, r1=128):
+        name, o, w = PLACE[name]
+        a, b = (o, o + w) if a is None else (o + a, o + b)
+        return (T[name][r0:r1, a:b:step] if step != 1 else T[name][r0:r1, a:b], [(name, a, b, step)])
+
+    def I(win, off):
+        return (win[0].indirect(off[0]), win[1] + off[1])
+
+    def learn(q, r, n):
+        c = clk[q]
+        c[r] = max(c.get(r, 0), n)
+        for k, v in snap.get((r, n), {}).items():
+            if c.get(k, 0) < v:
+                c[k] = v
+
+    def sync(q, reads, writes):
+        need = {}
+        for regs, w in ((reads, False), (writes, True)):
+            for reg in regs:
+                ps = reg[0].startswith("pb")
+                for (rq, rn, old, rw) in acc.get(reg[0], ()):
+                    hit = meet(reg, old)
+                    if rq == q:
+                        if q == "P" or not rw or not hit:
+                            continue
+                    elif not (ps or (hit and (w or rw))):
+                        continue
+                    if need.get(rq, 0) < rn:
+                        need[rq] = rn
+        order = sorted(need, key=lambda r: (r not in cnt, -need[r]))
+        for final in (False, True):
+            for r in order:
+                if clk[q].get(r, 0) >= need[r]:
+                    continue
+                if not final and any(o != r and clk[q].get(o, 0) < need[o] and snap[(o, need[o])].get(r, 0) >= need[r] for o in order):
+                    continue
+                eng[q].wait_ge(semof(r), need[r])
+                learn(q, r, need[r])
+
+    def note(ev, n, reads, writes):
+        for reg in writes:
+            acc[reg[0]] = [x for x in acc.get(reg[0], []) if not (x[2][1] >= reg[1] and x[2][2] <= reg[2] and (reg[3] == 1 or (x[2][3] == reg[3] and x[2][1] == reg[1])))] + [(ev, n, reg, True)]
+        for reg in reads:
+            acc[reg[0]] = [x for x in acc.get(reg[0], []) if not (x[0] == ev and not x[3] and x[2] == reg)] + [(ev, n, reg, False)]
+
+    def op(q, fn, outs, ins):
+        reads = [r for i in ins for r in i[1]]
+        writes = [r for o in outs for r in o[1]]
+        sync(q, reads, writes)
+        call = fn()
+        cnt[q] += 1
+        n = cnt[q]
+        call.then_inc(semof(q), 1)
+        snap[(q, n)] = dict(clk[q])
+        snap[(q, n)][q] = n - 1
+        note(q, n, reads, writes)
+
+    def sc(x):
+        return x[0] if isinstance(x, tuple) else x
+
+    def tl(*xs):
+        return [x for x in xs if isinstance(x, tuple)]
+
+    def tt(o, a, b, f): op("V", lambda: eng["V"].tensor_tensor(o[0], a[0], b[0], f), [o], [a, b])
+    def ts(o, a, s1, s2, f0, f1=None):
+        if f1 is None:
+            op("V", lambda: eng["V"].tensor_scalar(o[0], a[0], sc(s1), None, f0), [o], [a] + tl(s1))
+        else:
+            op("V", lambda: eng["V"].tensor_scalar(o[0], a[0], sc(s1), sc(s2), f0, f1), [o], [a] + tl(s1, s2))
+    def cp(o, a): op("V", lambda: eng["V"].tensor_copy(o[0], a[0]), [o], [a])
+    def scat(tab, off, a): op("V", lambda: eng["V"].tensor_copy(tab[0].indirect(off[0]), a[0]), [tab], [a, off])
+    def scan(o, a, b, i, f0, f1): op("V", lambda: eng["V"].tensor_tensor_scan(o[0], a[0], b[0], i, f0, f1), [o], [a, b])
+    def red(o, a): op("V", lambda: eng["V"].tensor_reduce(o[0], a[0], AX.X, A.add), [o], [a])
+    def fill(o, c): op("V", lambda: eng["V"].memset(o[0], c), [o], [])
+    def act(o, a, f=F.Copy, scale=1.0, bias=0.0):
+        op("S", lambda: eng["S"].activation(o[0], a[0], f, bias=sc(bias), scale=sc(scale)), [o], [a] + tl(bias, scale))
+    def mm(o, l, r, st=True, sp=True): op("P", lambda: eng["P"].matmul(o[0], l[0], r[0], st, sp), [o], [l, r])
+    def iota(o, pat, base, cm, whole=False):
+        if whole:
+            op("G", lambda: g.iota(o[0], pat, base, cm), [o], [])
+        else:
+            op("G", lambda: g.iota(o[0], pat, base, cm, allow_small_or_imprecise_dtypes=True), [o], [])
+    def asel(o, a, pat, cop, fv, base, cm): op("G", lambda: g.affine_select(o[0], a[0], pat, cop, fv, base, cm), [o], [a])
+
+    def dma(q, sem, out, in_, outs, ins):
+        reads, writes = [r for i in ins for r in i[1]], [r for o in outs for r in o[1]]
+        sync(q, reads, writes)
+        eng[q].dma_start(out, in_).then_inc(T.sem[sem], 16)
+        snap[(sem, 16)] = dict(clk[q])
+        note(sem, 16, reads, writes)
+
+    def arrive(sem, n, b):
+        snap[(sem, n)] = {}
+        note(sem, n, [], b[1])
+
+    def send(core, dst, topo, o, i, rsem):
+        sync("G", i[1], [])
+        rid, pid = topo.addr(dst, core)
+        g.remote_dma(o[0], i[0], T.sem[rsem], T.sem.sent, pid, rid, topo.mask(core, dst))
+        return len(topo.engines(core, dst))
+
+    return dict(B=B, I=I, tt=tt, ts=ts, cp=cp, scat=scat, scan=scan, red=red, fill=fill, act=act, mm=mm, iota=iota, asel=asel, dma=dma,
+                arrive=arrive, send=send, cnt=cnt)
+
+
+def weave(*lists):
+    lists = [list(x) for x in lists]
+    while any(lists):
+        for x in lists:
+            if x:
+                x.pop(0)()
+
+
+def rank_program(g, core, T, topo):
+    rank = T.rank_of(core)
+    if rank is None:
+        return
+    K = make(g, T)
+    B, I, tt, ts, cp, scat, scan, red, fill, act, mm, iota, asel, dma = (K[k] for k in (
+        "B", "I", "tt", "ts", "cp", "scat", "scan", "red", "fill", "act", "mm", "iota", "asel", "dma"))
+    nxt = T.cores[(rank + 3) % len(T.cores)]
+    prv_eng = len(topo.engines(T.cores[(rank + 1) % len(T.cores)], core))
+
+    def dedupe(c, bank, a, flist, fpos):
+        s = str(c)
+        own = B("FL", 96 * c + 15, 96 * c + 96, 16)
+        return [lambda: tt(B("RMk" + s), B(bank, a, a + 96), B("NEG", 0, 96), A.add),
+                lambda: scan(B("FL", 96 * c, 96 * c + 96), B("HOLD", 0, 96), B("RMk" + s), 0.0, A.add, A.max),
+                lambda: tt(B("eq" + s, 0, 95), B(bank, a + 1, a + 96), B("FL", 96 * c, 96 * c + 95), A.is_equal),
+                lambda: cp(flist, own),
+                lambda: scan(B("dup" + s, 0, 95), B("SEG", 0, 95), B("eq" + s, 0, 95), 0.0, A.mult, A.max),
+                lambda: ts(B("pT" + s), B("dup" + s, 14, 95, 16), B("TC"), None, A.mult),
+                lambda: tt(B("pQ" + s), B("pT" + s), own, A.max),
+                lambda: cp(fpos, B("pQ" + s))]
+
+    def marks(tab, val, pos, p0, t, c):
+        return [lambda b=b: scat(B(tab), B(pos, p0 + 2 * b, p0 + 2 * b + 1), B(val, 192 * t + 16 * b, 192 * t + 16 * b + 16))
+                for b in range(6 * c + 5, 6 * c - 1, -1)]
+
+    dma("Y", "ld0", T.v0s[:], T.v0[:], [B("v0s")], [])
+    QW = 512
+    for j in range(4):
+        dma("Y", "ld%d" % (3 + j), T.enS[:, j * QW:(j + 1) * QW], T.en[:, j * QW:(j + 1) * QW], [B("enS", j * QW, (j + 1) * QW)], [])
+    dma("S", "ld1", T.z0s[:], T.z0[:], [B("z0s")], [])
+    dma("S", "ld2", T.wts[:], T.wt[:], [B("wts")], [])
+    dma("S", "ld7", T.XS[:], T.xs[:], [B("XS")], [])
+
+    fill(B("ones"), 1.0); fill(B("onef"), 1.0); fill(B("GFt"), 32.0); fill(B("GTt"), 1024.0); fill(B("o32"), 1.0 / 32)
+    iota(B("qI"), [[0, 1]], 0, 1, True)
+    iota(B("CI"), [[0, 12], [1, 16]], 0, 0)
+    asel(B("BDt"), B("ones", 0, 128), [[-16, 8], [0, 16]], A.is_ge, 0.0, 0, 1)
+    asel(B("BD"), B("BDt"), [[16, 8], [0, 16]], A.is_ge, 0.0, 15, -1)
+    asel(B("BAND"), B("ones", 0, 160), [[1, 160]], A.is_equal, 0.0, -16, -1)
+    asel(B("GBt"), B("onef", 0, 8), [[-16, 8]], A.is_ge, 0.0, 0, 1)
+    asel(B("GB"), B("GBt"), [[16, 8]], A.is_ge, 0.0, 15, -1)
+    asel(B("ID"), B("ones", 0, 128), [[-1, 128]], A.is_equal, 0.0, 0, 1)
+    iota(B("VAL", 0, 192), [[32, 12], [-2, 16]], 30, 0)
+    iota(B("VV", 0, 192), [[32, 12], [-2, 16]], 29, 0)
+    asel(B("EXPT"), B("ones", 0, 136), [[-16, 8], [0, 17]], A.is_equal, 0.0, 0, 1)
+    iota(B("FV"), [[0, 2064]], 9999, 0)
+    ts(B("qJ"), B("qI"), 15, None, A.bitwise_and)
+    cp(B("qi"), B("qJ"))
+    ts(B("RM16"), B("CI", 0, 16), B("qi"), None, A.is_equal)
+    ts(B("WC"), B("RM16"), -2097152.0 + 8192.0, -8192.0, A.mult, A.add)
+    act(B("GBs"), B("GB"), scale=2.0 ** -10)
+    for i in range(16):
+        act(B("selB", 8 * i, 8 * i + 8), B("GBs"), scale=B("RM16", i, i + 1))
+        act(B("WN", 8 * i, 8 * i + 8), B("GB"), scale=B("WC", i, i + 1))
+    act(B("INK"), B("ID"), scale=-2048.0)
+    ts(B("EQD"), B("CI"), B("qi"), None, A.is_equal)
+    ts(B("NEG"), B("EQD"), 4096.0, -4096.0, A.mult, A.add)
+    fill(B("HOLD"), 0.0); fill(B("SEG"), 1.0); fill(B("OT"), 0); fill(B("MM", 192, 384), 0.0)
+    fill(B("HOLD", 0, 192, 16), -8192.0); fill(B("SEG", 0, 192, 16), 0.0)
+    cp(B("v0f"), B("v0s"))
+    for i in range(16):
+        act(B("LM", i, 192, 16), B("v0f"), scale=B("RM16", 15 - i, 16 - i))
+    mm(B("pb7", 0, 192), B("BD"), B("LM"))
+    act(B("MM", 0, 192), B("pb7", 0, 192))
+    ts(B("TC"), B("qi"), 2048.0, None, A.add)
+    for i in range(16):
+        ts(B("ZI", 160 * i, 160 * i + 160), B("BAND"), B("RM16", i, i + 1), None, A.mult)
+    fill(B("NT", 2048, 2432), 0.0); fill(B("ST", 2048, 2432), 0.0)
+    for j in range(4):
+        a, b = j * QW, (j + 1) * QW
+        ts(B("tmpB", a, b), B("enS", a, b), 1.0 / 2048, 159.5 + 1.0 / 8192, A.mult, A.add)
+        act(B("ST", a, b), B("tmpB", a, b), bias=-160.0)
+        mm(B("pb%d" % j), B("INK"), B("ST", a, b))
+    for i in range(16):
+        act(B("Zz", i, 192, 16), B("z0s", 15 - i, 192, 16))
+    weave(*[dedupe(c, "pb7", 96 * c, B("RT", 6 * c, 6 * c + 6), B("RT", 12 + 12 * c, 24 + 12 * c, 2)) for c in CH])
+    ts(B("qs1"), B("qi"), 1.0, None, A.add)
+    cp(B("wtf"), B("wts"))
+    ts(B("q15"), B("qi"), 15.0, None, A.is_equal)
+    ts(B("qK"), B("qJ"), 1, None, A.bitwise_and)
+    ts(B("qe"), B("qK"), -1.0, 1.0, A.mult, A.add)
+    tt(B("w1"), B("qe"), B("q15"), A.add)
+    ts(B("qo"), B("w1"), -1.0, 1.0, A.mult, A.add)
+    act(B("W16"), B("GB"), scale=1024.0)
+    act(B("WD"), B("GB"), scale=B("wtf"))
+    act(B("IDb"), B("ID")); act(B("I22"), B("ID"), scale=4194304.0)
+    for j in range(4):
+        a, b = j * QW, (j + 1) * QW
+        tt(B("NT", a, b), B("enS", a, b), B("pb%d" % j), A.add)
+
+    def consts_late(part):
+        if part:
+            iota(B("FF"), [[0, 2064]], 9999, 0)
+            for t in range(1, HOPS):
+                iota(B("VAL", 192 * t, 192 * t + 192), [[32, 12], [-2, 16]], 30 - 512 * t, 0)
+                iota(B("VV", 192 * t, 192 * t + 192), [[32, 12], [-2, 16]], 29 - 512 * t, 0)
+            return
+        asel(B("SELT"), B("o32"), [[-16, 8], [-1, 17]], A.is_equal, 0.0, 1, 1)
+        iota(B("KTHR"), [[0, 8], [-1, 17]], 17, 0)
+        iota(B("BK"), [[0, 8], [64, 17]], -64, 0)
+        asel(B("GF", 0, 128, 1, 0, 16), B("GFt", 0, 128, 1, 0, 16), [[-1, 8], [0, 16]], A.is_equal, 0.0, 0, 1)
+        asel(B("GT", 0, 128, 1, 0, 16), B("GTt", 0, 128, 1, 0, 16), [[-1, 8], [0, 16]], A.is_equal, 0.0, -8, 1)
+        iota(B("TRb"), [[1, 24]], 2048, 0)
+
+    def consts_v1():
+        return [lambda: fill(B("SELT", 0, 136, 17), 0.0), lambda: fill(B("BK", 0, 136, 17), -524288.0),
+                lambda: fill(B("RST"), -1.0e7), lambda: fill(B("RST", 0, 136, 17), 1.0e7)]
+
+    def consts_v2():
+        return [lambda: ts(B("q24"), B("qi"), 24.0, None, A.mult), lambda: ts(B("TR"), B("TRb"), B("q24"), None, A.add),
+                lambda: ts(B("OFFD"), B("EQD"), 1.0e6, -1.0e6, A.mult, A.add),
+                lambda: tt(B("OWN", 0, 192), B("VAL", 0, 192), B("OFFD"), A.add)]
+
+    def consts_s():
+        act(B("NID"), B("ID"), scale=-1.0); act(B("P64"), B("ID"), scale=64.0); act(B("N64"), B("ID"), scale=-64.0)
+        act(B("DE"), B("ID"), scale=B("qe")); act(B("DO"), B("ID"), scale=B("qo")); act(B("D15"), B("ID"), scale=B("q15"))
+        act(B("DEb"), B("ID"), scale=B("qe")); act(B("DOb"), B("ID"), scale=B("qo"))
+        for t in range(HOPS):
+            act(B("BT", t, t + 1), B("q15"), scale=9.0 + t)
+        act(B("I2K"), B("ID"), scale=2048.0)
+        act(B("GBy"), B("GB"), scale=2048.0)
+        act(B("YWn"), B("GB"), scale=B("qs1")); act(B("YWs"), B("GBy"), scale=B("qs1"))
+
+    sent = 0
+    held = []
+    for t in range(HOPS):
+        last = t == HOPS - 1
+        zc, mc, rc = 192 * t, 384 * t, 40 * t
+        if t > 0:
+            K["arrive"]("aL%d" % t, prv_eng, B("RT", rc, rc + 36))
+            K["arrive"]("aM%d" % t, prv_eng, B("MM", mc, mc + 384))
+            for c in CH:
+                K["arrive"]("aZ%d%d" % (c, t), prv_eng, B("Zz", zc + 96 * c, zc + 96 * c + 96))
+        vl, fl = B("RT", rc, rc + 12), B("OT", rc, rc + 12)
+
+        def W(n, a=0, b=16, st=1):
+            return B(n, a, b, st, 0, 96)
+
+        def bc(name, c, k):
+            return B(name, 1536 * c + k, 1536 * c + 1536, 16)
+
+        def gat(c, what):
+            act(B(what, 1536 * c, 1536 * c + 1536), I(B("NT" if what == "X" else "ST"), B("RL", 96 * c, 96 * c + 96)))
+
+        def selx(c):
+            for k in range(16):
+                i = (k + t) % 16
+                off = 160 * i + 16 - (k - i)
+                mm(B("pb4", 96 * c, 96 * c + 96), B("ZI", off, off + 128), bc("X", c, k), k == 0, k == 15)
+
+        def lists(c):
+            cp(B("AL", 96 * c, 96 * c + 96), B("pb4", 96 * c, 96 * c + 96))
+            cp(B("CN", 96 * c, 96 * c + 96), B("AL", 96 * c, 96 * c + 96))
+
+        def rec(c):
+            tt(B("D", 1536 * c, 1536 * c + 1536), I(B("XS"), B("AL", 96 * c, 96 * c + 96)), B("ZE", 1536 * c, 1536 * c + 1536), A.subtract)
+
+        def size(c):
+            act(B("AB", 1536 * c, 1536 * c + 1536), B("D", 1536 * c, 1536 * c + 1536), F.Abs)
+
+        def newer(c):
+            return [lambda k=k: tt(bc("M", c, k), bc("S", c, k), B("pb5", 96 * c, 96 * c + 96), A.is_gt) for k in range(16)]
+
+        def pay(c):
+            mm(W("pb%d" % (2 + c), 0, 136), B("CN", 96 * c, 96 * c + 96), B("SELT"), True, False)
+            for k in range(16):
+                i = (k + t) % 16
+                mm(W("pb%d" % (2 + c), 1 + k, 136, 17), bc("S", c, k), B("selB", 8 * i, 8 * i + 8), False, False)
+
+        def failcol(c):
+            mm(W("pb%d" % (2 + c), 0, 136, 17), W("ID", 0, 96), W("ff", 8 * c, 8 * c + 8), False, True)
+
+        def key0(c):
+            mm(W("pb%d" % c, 0, 136), W("IDb", 0, 96), W("BK", 0, 136), True, False)
+            mm(W("pb%d" % c, 0, 136), W("I22", 0, 96), W("TBc", 136 * c, 136 * c + 136), False, False)
+
+        def keyA(c):
+            for k in range(16):
+                mm(W("pb%d" % c, 1 + k, 136, 17), bc("AB", c, k), B("W16"), False, False)
+
+        def keyM(c):
+            for k in range(16):
+                i = (k + t) % 16
+                mm(W("pb%d" % c, 1 + k, 136, 17), bc("M", c, k), B("WN", 8 * i, 8 * i + 8), False, k == 15)
+
+        def zexp(c, q, k0, k1):
+            for k in range(k0, k1):
+                z = B("Zz", zc + 96 * c, zc + 96 * c + 96)
+                if q == "G":
+                    asel(bc("ZE", c, k), z, [[0, 96]], A.is_equal, 0.0, 0, 0)
+                elif q == "S":
+                    act(bc("ZE", c, k), z)
+                else:
+                    cp(bc("ZE", c, k), z)
+
+        def tail(c):
+            s = str(c)
+            kk, pp = W("pb%d" % c, 0, 136), W("pb%d" % (2 + c), 0, 136)
+            mn, dd, ee, oo = (W(n + s, 0, 136) for n in ("Mn", "dd", "ee", "oo"))
+            o16 = W("oo" + s, 16, 136, 17)
+            return [lambda: scan(mn, W("RST", 0, 136), kk, 0.0, A.max, A.min), lambda: tt(dd, kk, mn, A.subtract),
+                    lambda: tt(ee, pp, dd, A.subtract), lambda: scan(oo, dd, ee, 0.0, A.min, A.max),
+                    lambda: ts(W("WT" + s, 0, 8), o16, 393216.0, 393216.0, A.add, A.subtract),
+                    lambda: tt(W("WT" + s, 8, 16), o16, W("WT" + s, 0, 8), A.subtract)]
+
+        def turn(c):
+            q = B("pb6", 320 + 96 * c, 416 + 96 * c, 1, 0, 16)
+            tp = B("TPs", 96 * c, 96 * c + 96, 1, 0, 16)
+            mm(q, W("WT%d" % c, 0, 16), W("ID", 0, 96))
+            act(tp, q)
+            mm(B(RB[c], 0, 96), B("GF", 0, 128, 1, 0, 16), tp)
+            mm(B(RB[c], 96, 192), B("GT", 0, 128, 1, 0, 16), tp)
+
+        def share(c):
+            for k in (0, 1):
+                act(B("MO", mc + 192 * k + 96 * c, mc + 192 * k + 96 * c + 96), B(RB[c], 96 * k, 96 * k + 96))
+
+        def zproc(c):
+            a, b = 96 * c, 96 * c + 96
+            zt = B("Zz", zc + a, zc + b)
+            act(B("FM", a, b), B(RB[c], 96, 192), F.Relu, scale=-1.0, bias=1.0)
+            act(B("XF", a, b), I(B("XS"), B("OT", rc + 6 * c, rc + 6 * c + 6)))
+            mm(B("pb1", a, b), B("ID"), zt, True, False)
+            mm(B("pb1", a, b), B("NID"), B("XF", a, b), False, True)
+            mm(B("pb3", a, b), B("ID"), zt, True, False)
+            mm(B("pb3", a, b), B("N64"), B("FM", a, b), False, True)
+            act(B("AZ", a, b), B("pb1", a, b), F.Abs)
+            act(B("R1", a, b), B("pb3", a, b), F.Relu)
+            mm(B("pb3", 192 + a, 192 + b), B("ID"), B("AZ", a, b), True, False)
+            mm(B("pb3", 192 + a, 192 + b), B("P64"), B("FM", a, b), False, True)
+            act(B("R2", a, b), B("pb3", 192 + a, 192 + b), F.Relu, bias=-64.0)
+            mm(B("pb1", 192 + a, 192 + b), B("ID"), B("R1", a, b), True, False)
+            mm(B("pb1", 192 + a, 192 + b), B("ID"), B("R2", a, b), False, True)
+            if not last:
+                act(B("ZO", zc + a, zc + b), B("pb1", 192 + a, 192 + b))
+
+        def out(o, src, n, a, b, sem):
+            if last:
+                return 0
+            return K["send"](core, nxt, topo, B(o, n * (t + 1) + a, n * (t + 1) + b), B(src, n * t + a, n * t + b), sem + str(t + 1))
+
+        for c in CH:
+            cp(B("RL", 96 * c, 96 * c + 96), I(B("NT"), B("RT", rc + 6 * c, rc + 6 * c + 6)))
+        act(B("X", 1536, HX), I(B("NT"), B("RL", 96, HR)))
+        cp(B("X", HX, 3072), I(B("NT"), B("RL", HR, 192)))
+        for f_ in held:
+            f_()
+        zexp(1, "S", G1 + V1, 16)
+        gat(0, "X"); gat(1, "S")
+        zexp(0, "S", G0, 16)
+        mm(B("pb5", 0, 192), B("ID"), B("MM", mc + 192, mc + 384))
+        for c in (0, 1):
+            mm(W("pb6", 136 * c, 136 * c + 136), B("MM", mc + 192 + 96 * c, mc + 288 + 96 * c), B("EXPT"))
+        selx(1)
+        zexp(1, "G", 0, G1)
+        if t == 0:
+            consts_late(0)
+        zexp(0, "G", 0, G0)
+        if t == 0:
+            consts_late(1)
+        e1, e2 = [], []
+        for c in (0, 1):
+            e1.append(lambda c=c: tt(W("TBc", 136 * c, 136 * c + 136), W("pb6", 136 * c, 136 * c + 136), W("KTHR", 0, 136), A.is_ge))
+        e1.append(lambda: cp(B("vlf"), vl))
+        if t > 0:
+            e1.append(lambda: red(W("Af", 0, 1), W("pb3", 480, 496)))
+            e1.append(lambda: cp(W("Ai", 0, 1), W("Af", 0, 1)))
+            e1.append(lambda: ts(W("Aj", 0, 1), W("Ai", 0, 1), 255, None, A.bitwise_and))
+            e1.append(lambda: cp(W("Ac", 0, 1), W("Aj", 0, 1)))
+        else:
+            e1.append(lambda: fill(B("Ac"), 0.0))
+        e2.append(lambda: cp(W("ui"), W("pb6", 288, 304)))
+        e2.append(lambda: ts(W("ua"), W("ui"), 2047, None, A.bitwise_and))
+        e2.append(lambda: tt(W("ub"), W("ua"), W("ua"), A.mult))
+        e2.append(lambda: ts(W("ud"), W("ua"), 37.0, W("Ac", 0, 1), A.mult, A.add))
+        e2.append(lambda: ts(W("uc"), W("ub"), 5, None, A.arith_shift_right))
+        e2.append(lambda: tt(W("ue"), W("uc"), W("ud"), A.add))
+        e2.append(lambda: ts(W("uf"), W("ue"), 2047, None, A.bitwise_and))
+        e2.append(lambda: ts(W("ff"), W("uf"), 1.0 / 32, None, A.mult))
+        weave([lambda k=k: zexp(1, "V", k, k + 1) for k in range(G1, G1 + V1)], consts_v1() if t == 0 else [])
+        lists(1); rec(1)
+        size(1)
+        gat(0, "S")
+        pay(1)
+        n1 = newer(1)
+        weave(n1[:8], e1)
+        for c in (0, 1):
+            mm(W("pb6", 288 + 8 * c, 296 + 8 * c), B("Zz", zc + 96 * c, zc + 96 * c + 96), B("WD"))
+        weave(n1[8:], e2)
+        selx(0)
+        key0(1); keyA(1); keyM(1)
+        failcol(1)
+        lists(0); rec(0)
+        pay(0); key0(0); failcol(0)
+        weave(consts_v2() if t == 0 else [])
+        size(0)
+        n0 = newer(0)
+        weave(n0[:6], tail(1))
+        turn(1)
+        weave(n0[6:], marks("FV", "VV", "RT", rc + 12, t, 1) + marks("FV", "VV", "RT", rc + 12, t, 0))
+        keyA(0); keyM(0)
+        act(B("Rv"), I(B("NT"), vl))
+        act(B("Sv"), I(B("ST"), vl))
+        if t > 0:
+            act(B("OWN", zc, zc + 192), B("OWN", 0, 192), bias=-512.0 * t)
+        else:
+            consts_s()
+        share(1)
+        act(B("G0"), I(B("FV"), vl), bias=1.0)
+        weave(tail(0), dedupe(1, RB[1], 0, B("OT", rc + 6, rc + 12), B("OT", rc + 24, rc + 36, 2)))
+        turn(0)
+        share(0)
+        zproc(1)
+        sent += out("Zz", "ZO", 192, 96, 192, "aZ1")
+        m1 = marks("FF", "VAL", "OT", rc + 12, t, 1)
+        weave(m1[:3], [lambda c=c: ts(W("FC", 8 * c, 8 * c + 8), W("WT%d" % c, 8, 16), 0.0, None, A.is_equal) for c in (0, 1)])
+        weave(dedupe(0, RB[0], 0, B("OT", rc, rc + 6), B("OT", rc + 12, rc + 24, 2)), m1[3:])
+        sent += out("MM", "MO", 384, 0, 384, "aM")
+        sent += out("RT", "OT", 40, 0, 36, "aL")
+        act(B("Rf"), I(B("NT"), fl))
+        act(B("Sf"), I(B("ST"), fl))
+        weave(marks("FF", "VAL", "OT", rc + 12, t, 0), [lambda: tt(B("pre"), I(B("FV"), fl), B("G0"), A.min)])
+        vr, fr = B("MM", mc, mc + 192), B("MO", mc, mc + 192)
+        for h, (own, oth, new) in enumerate((("Rv", "Rf", fr), ("Rf", "Rv", vr))):
+            o = B("pb0", 192 * h, 192 * h + 192)
+            mm(o, B("DO"), B(own), True, False)
+            mm(o, B("D15"), new, False, False)
+            mm(o, B("DE"), B(oth), False, True)
+        act(B("NNs"), B("pb0", 0, 384))
+        for h, (own, oth) in enumerate((("Sv", "Sf"), ("Sf", "Sv"))):
+            o = B("pb2", 192 * h, 192 * h + 192)
+            mm(o, B("DOb"), B(own), True, False)
+            mm(o, B("DEb"), B(oth), False, True)
+        act(B("NSs"), B("pb2", 0, 384), F.Identity, bias=B("BT", t, t + 1))
+        tt(B("ma"), I(B("FF"), vl), B("pre"), A.min)
+        tt(B("mb"), I(B("FF"), fl), B("ma"), A.min)
+        tt(B("nd"), B("mb"), B("OWN", zc, zc + 192), A.is_lt)
+        scan(B("ns"), B("SEG"), B("nd"), 0.0, A.mult, A.max)
+        nl = B("ns", 15, 192, 16)
+        tt(B("nT", 0, 12), nl, B("TR", 0, 12), A.mult)
+        tt(B("nT", 12, 24), nl, B("TR", 12, 24), A.mult)
+        tt(B("nP", 0, 12), B("nT", 0, 12), B("vlf"), A.max)
+        tt(B("nP", 12, 24), B("nT", 12, 24), B("FL", 15, 192, 16), A.max)
+        cp(B("POS"), B("nP"))
+        held = [lambda: scat(B("ST"), B("POS"), B("NSs"))]
+        if last:
+            held[0]()
+        scat(B("NT"), B("POS"), B("NNs"))
+        zproc(0)
+        if not last:
+            sent += out("Zz", "ZO", 192, 0, 96, "aZ0")
+            mm(W("pb3", 480, 496), W("ones", 0, 96), W("FC"))
+
+    mc = 384 * (HOPS - 1)
+    mm(B("pb7", 256, 448), B("ID"), B("MO", mc, mc + 192), True, False)
+    mm(B("pb7", 256, 448), B("I2K"), B("MO", mc + 192, mc + 384), False, True)
+    YB = ("pb2", "pb5", "pb4", "pb0")
+    for j in range(4):
+        mm(B(YB[j], 0, 512, 1, 0, 8), B("YWs"), B("ST", 512 * j, 512 * j + 512), True, False)
+    for i in range(16):
+        act(B("YP", 15 - i, 192, 16), B("pb7", 256 + i, 448, 16))
+    dma("Y", "st1", T.yp[:], T.YP[0:128:16, :], [], [B("YP")])
+    for j in range(4):
+        a, b = 512 * j, 512 * j + 512
+        if j % 2:
+            act(B("NTh", a, b), B("NT", a, b))
+        else:
+            cp(B("NTh", a, b), B("NT", a, b))
+    for j in range(4):
+        mm(B(YB[j], 0, 512, 1, 0, 8), B("YWn"), B("NTh", 512 * j, 512 * j + 512), False, True)
+    for j in range(4):
+        a, b = 512 * j, 512 * j + 512
+        o = B(YB[j], 0, 512, 1, 0, 8)
+        if j % 2:
+            act(B("YS", a, b, 1, 0, 8), o)
+        else:
+            cp(B("YS", a, b, 1, 0, 8), o)
+    dma("Y", "st2", T.ys[:], T.YS[0:8, :], [], [B("YS")])
+    for i in range(16):
+        act(B("YZ", 15 - i, 192, 16), B("pb1", 192 + i, 384, 16))
+    dma("Y", "st0", T.yz[:], T.YZ[:], [], [B("YZ")])
+
+    for q in ("V", "S", "P", "G"):
+        g.wait_ge(T.sem["c" + q], K["cnt"][q])
+    for j in range(8):
+        g.wait_ge(T.sem["ld%d" % j], 16)
+    for j in range(3):
+        g.wait_ge(T.sem["st%d" % j], 16)
+    g.wait_ge(T.sem.sent, sent)

@@ -1,16 +1,23 @@
-import numpy as np
-from concourse.mybir import AluOpType as A, ActivationFunctionType as F, AxisListType as AX
+from concourse.mybir import AluOpType as A, ActivationFunctionType as F
 
 HOPS = 5
-HR = 128
-HX = 1536 + 16 * (HR - 96)
-G1, V1, G0 = 8, 8, 12
-CH = (1, 0)
-RB = ("pb5", "pb7")
+NA = 128
+CHUNK = ((0, NA), (NA, 192 - NA))
+PC = 64
+EV, RV, RW = 64, 64, 0
+MQ = "SS"
+ONS = ("av", "sb", "Ax")
+DB = ("pb7", "pb7")
+SP = 384
+B0 = 2.0 ** 18 + 4096
+T0 = B0 / 2048 + 1
+U = 2.0 ** 19
+PE, GATHER, SCATTER, FIX, OWN, CROSS, LAG, FAR = 0.6, 1.5, 3.5, 30, 60, 100, 1800, 2800
+SLACK, ROUNDS = 0, 4
 f4, f2, b2, i4, u2 = "float32", "float16", "bfloat16", "int32", "uint16"
 SCRATCH = {}
-OWNBUF = ("enS", "tmpB", "NT", "ST", "XS", "FV", "FF", "NTh", "YS", "YP", "YZ", "v0s", "z0s", "wts", "ZI", "X", "S", "M", "D", "AB", "ZE",
-          "VAL", "VV", "OWN", "MM", "Zz", "MO", "ZO", "RT", "OT", "RL", "AL", "POS", "NNs", "NSs")
+OWNBUF = ("enS", "ET", "YS", "XS", "FT", "YP", "YQ", "YZ", "ZL", "v0s", "v0f", "z0s", "wts", "X", "M", "R", "MX", "VAL", "VV", "MM", "MO",
+          "RT", "OT", "RL", "AL", "POS", "NN", "PRE", "LP", "LC")
 PLACE = {}
 
 
@@ -26,47 +33,49 @@ def declare(name, w, t):
 
 
 for n_, w_, t_ in (
-        ("enS", 2048, i4), ("tmpB", 2048, b2), ("NT", 2432, f4), ("ST", 2432, b2), ("XS", 2048, b2),
-        ("FV", 2064, f4), ("FF", 2064, f4), ("NTh", 2048, f2), ("YS", 2048, f4), ("YP", 192, f4), ("YZ", 192, b2),
-        ("v0s", 12, i4), ("v0f", 12, f4), ("z0s", 192, b2), ("wts", 1, i4), ("wtf", 1, f4),
-        ("ones", 192, f2), ("onef", 32, f4), ("o32", 136, f2), ("ID", 128, f2), ("NID", 128, f2), ("P64", 128, f2), ("N64", 128, f2),
-        ("I2K", 128, f2), ("IDb", 128, b2), ("I22", 128, b2), ("INK", 128, b2), ("BDt", 128, f2), ("BD", 128, f2), ("GBt", 8, f4), ("GB", 8, f4), ("GBs", 8, f4), ("GBy", 8, f4),
-        ("BAND", 160, f2), ("ZI", 2560, f2), ("qI", 1, i4), ("qJ", 1, i4), ("qK", 1, i4), ("qi", 1, f4), ("qe", 1, f4), ("q15", 1, f4),
-        ("qo", 1, f4), ("q24", 1, f4), ("qs1", 1, f4), ("TC", 1, f4), ("w1", 1, f4),
-        ("CI", 192, f4), ("RM16", 16, f4), ("WC", 16, f4), ("selB", 128, b2), ("WN", 128, b2), ("SELT", 136, f2),
-        ("W16", 8, b2), ("WD", 8, f2), ("YWn", 8, f2), ("YWs", 8, b2), ("EXPT", 136, f2), ("KTHR", 136, f4), ("BK", 136, b2),
-        ("RST", 136, f4), ("NEG", 192, f4), ("EQD", 192, f4), ("OFFD", 192, f4), ("HOLD", 192, f4), ("SEG", 192, f4), ("TR", 24, f4), ("TRb", 24, f4),
-        ("DO", 128, f2), ("DE", 128, f2), ("D15", 128, f2), ("DOb", 128, b2), ("DEb", 128, b2), ("BT", 5, f4),
-        ("GFt", 128, f2), ("GTt", 128, f2), ("GF", 128, f2), ("GT", 128, f2), ("LM", 192, f2),
-        ("vlf", 12, f4), ("FL", 192, f4), ("CN", 192, f2), ("RL", 192, u2), ("X", 3072, f2), ("S", 3072, b2), ("M", 3072, b2), ("D", 3072, b2), ("AB", 3072, b2), ("ZE", 3072, f2),
-        ("AL", 192, u2), ("TBc", 272, b2), ("ui", 16, i4), ("ua", 16, i4), ("ub", 16, i4), ("uc", 16, i4), ("ud", 16, i4), ("ue", 16, i4), ("uf", 16, i4), ("ff", 16, f2),
-        ("Af", 1, f4), ("Ai", 1, i4), ("Aj", 1, i4), ("Ac", 1, f4), ("FC", 16, f2), ("TPs", 192, f2),
-        ("Rv", 192, f2), ("Sv", 192, b2), ("Rf", 192, f2), ("Sf", 192, b2), ("G0", 192, f4), ("pre", 192, f4),
-        ("ma", 192, f4), ("mb", 192, f4), ("nd", 192, f4), ("ns", 192, f4), ("nT", 24, f4), ("nP", 24, f4), ("POS", 24, u2),
-        ("NNs", 384, f4), ("NSs", 384, b2), ("XF", 192, f2), ("AZ", 192, f2), ("FM", 192, f2), ("R1", 192, f2), ("R2", 192, f2),
-        ("VAL", 960, f4), ("VV", 960, f4), ("OWN", 960, f4),
-        ("MM", 1920, f2), ("Zz", 960, f2), ("MO", 1920, f2), ("ZO", 960, f2), ("RT", 200, u2), ("OT", 200, u2)):
+        ("enS", 2048, i4), ("ET", SP + 2048, f4), ("YS", SP + 2048, f4), ("XS", 2048, b2), ("FT", 2064, f4),
+        ("YP", 192, f4), ("YQ", 192, f4), ("YZ", 192, b2), ("ZL", 192, b2),
+        ("v0s", 12, i4), ("v0f", 16, f4), ("z0s", 192, b2), ("wts", 1, i4), ("wtf", 1, f4), ("LP", 12, u2), ("LC", 12, u2),
+        ("ones", 128, f2), ("onef", 128, f4), ("oneb", 192, b2), ("ID", 128, f2), ("NID", 128, f2), ("N64", 128, f2), ("I2K", 128, f2),
+        ("I4K", 128, f2), ("IDb", 128, b2), ("I37", 128, b2), ("ITH", 128, b2), ("BDt", 128, f2), ("BD", 128, f2), ("GBt", 8, f4), ("GB", 8, f4),
+        ("SEL", 128, f4), ("WNa", 128, b2), ("WNb", 128, b2), ("WN", 128, b2), ("WX", 8, b2), ("WR", 8, b2), ("WA", 8, b2), ("WD", 8, f2), ("C32", 128, f4),
+        ("qI", 1, i4), ("qJ", 1, i4), ("qK", 1, i4), ("qi", 1, f4), ("qr", 1, f4), ("qe", 1, f4), ("q15", 1, f4), ("qo", 1, f4), ("qs1", 1, f4),
+        ("w1", 1, f4), ("qa", 1, f4), ("qb", 1, f4), ("qy15", 1, f4), ("qp", 1, f4), ("qh", 1, f4), ("SCq", 1, f4), ("BIq", 1, f4),
+        ("CI", 256, f4), ("EQD", 256, f4), ("EQR", 192, f4), ("LI", 12, f4), ("CKt", 384, f4), ("CKu", 256, f4), ("CK", 384, f2), ("CB", 384, f2),
+        ("RST", 128, f4), ("HOLD", 128, f4), ("RSP", 256, f4), ("RSi", 16, f4),
+        ("DO", 128, f4), ("DE", 128, f4), ("D15", 128, f2), ("YO", 128, f4), ("YE", 128, f4), ("Y15", 128, f2), ("YW", 128, f4), ("BT", 5, f4),
+        ("GF", 128, f2), ("GT", 128, f2), ("LM", 192, f2),
+        ("RI", 192, i4), ("RJ", 192, i4), ("RL", 192, u2), ("X", 3072, f4), ("M", 3072, b2), ("R", 3072, b2), ("MX", 3072, b2), ("AL", 192, u2),
+        ("PEN", 192, b2), ("ui", 16, i4), ("ua", 16, i4), ("ub", 16, f4), ("uc", 16, f4), ("ud", 16, i4), ("ue", 16, i4), ("ff", 16, f4),
+        ("Ax", 1, b2), ("Ay", 1, f4), ("FC", 16, f4), ("FA", 2, f4), ("TPs", 192, f2), ("Rv", 192, f4), ("Rf", 192, f4), ("PRE", 192, f4),
+        ("av", 192, f2), ("af", 192, f2), ("POS", 24, u2), ("NN", 384, f4), ("XF", 192, f2), ("R1", 192, f2),
+        ("VAL", 960, f4), ("VV", 960, f4), ("MM", 2880, f2), ("MO", 2880, f2), ("RT", 320, u2), ("OT", 320, u2)):
     declare(n_, w_, t_)
 for c_ in (0, 1):
-    for n_, w_, t_ in (("Mn", 136, f4), ("dd", 136, f4), ("ee", 136, f4), ("oo", 136, f4), ("WT", 16, f2), ("RMk", 96, f4),
-                       ("eq", 96, f4), ("dup", 96, f4), ("pT", 6, f4), ("pQ", 6, f4)):
+    for n_, w_, t_ in (("sb", 128, b2), ("nm", 128, f2), ("Mn", 128, f4), ("dd", 128, f4), ("ee", 128, f4), ("oo", 128, f4), ("t1", 8, f4), ("t2", 8, f4),
+                       ("fin", 8, f4), ("WF", 16, f2), ("WS", 16, b2), ("FL", 128, f4), ("ne", 128, f4), ("dup", 128, f4), ("ys", 256, f4)):
         declare(n_ + str(c_), w_, t_)
 for b_ in range(8):
     SCRATCH["pb%d" % b_] = ("psum", [128, 512], f4)
     PLACE["pb%d" % b_] = ("pb%d" % b_, 0, 512)
 SEMAPHORES = ["cV", "cS", "cP", "cG", "sent"] + ["ld%d" % k for k in range(8)] + ["st%d" % k for k in range(3)] + \
-    ["a%s%d" % (m, t) for m in ("M", "L", "Z0", "Z1") for t in range(1, HOPS)]
+    ["a%s%d" % (m, t) for m in ("L0", "L1", "M0", "M1") for t in range(1, HOPS)]
+ORDER = []
 
 
 def meet(x, y):
     return x[1] < y[2] and y[1] < x[2] and not (x[3] == y[3] and (x[1] - y[1]) % x[3])
 
 
+def covers(x, y):
+    return y[1] >= x[1] and y[2] <= x[2] and (x[3] == 1 or (y[3] == x[3] and y[1] == x[1]))
+
+
 def make(g, T):
     eng = {"V": g.vector, "S": g.scalar, "P": g.tensor, "G": g, "Y": g.sync}
     cnt = {"V": 0, "S": 0, "P": 0, "G": 0}
     clk = {q: {} for q in eng}
-    snap, acc = {}, {}
+    snap, acc, plan, sends = {}, {}, [], {}
 
     def semof(r):
         return T.sem["c" + r] if r in cnt else T.sem[r]
@@ -94,39 +103,61 @@ def make(g, T):
                 for (rq, rn, old, rw) in acc.get(reg[0], ()):
                     hit = meet(reg, old)
                     if rq == q:
-                        if q == "P" or not rw or not hit:
+                        if q == "P" or not hit or not (w or rw):
                             continue
                     elif not (ps or (hit and (w or rw))):
                         continue
                     if need.get(rq, 0) < rn:
                         need[rq] = rn
-        order = sorted(need, key=lambda r: (r not in cnt, -need[r]))
+        turn = sorted(need, key=lambda r: (r not in cnt, -need[r]))
         for final in (False, True):
-            for r in order:
+            for r in turn:
                 if clk[q].get(r, 0) >= need[r]:
                     continue
-                if not final and any(o != r and clk[q].get(o, 0) < need[o] and snap[(o, need[o])].get(r, 0) >= need[r] for o in order):
+                if not final and any(o != r and clk[q].get(o, 0) < need[o] and snap[(o, need[o])].get(r, 0) >= need[r] for o in turn):
                     continue
                 eng[q].wait_ge(semof(r), need[r])
                 learn(q, r, need[r])
 
     def note(ev, n, reads, writes):
         for reg in writes:
-            acc[reg[0]] = [x for x in acc.get(reg[0], []) if not (x[2][1] >= reg[1] and x[2][2] <= reg[2] and (reg[3] == 1 or (x[2][3] == reg[3] and x[2][1] == reg[1])))] + [(ev, n, reg, True)]
+            acc[reg[0]] = [x for x in acc.get(reg[0], []) if not covers(reg, x[2])] + [(ev, n, reg, True)]
         for reg in reads:
             acc[reg[0]] = [x for x in acc.get(reg[0], []) if not (x[0] == ev and not x[3] and x[2] == reg)] + [(ev, n, reg, False)]
 
-    def op(q, fn, outs, ins):
+    def size(x):
+        return len(range(*x[1][0][1:]))
+
+    def narrow(*xs):
+        return all(SCRATCH[x[1][0][0]][2] in (f2, b2, u2) for x in xs)
+
+    def cycles(q, o, ins, kind):
+        if q == "P":
+            return max(min(64, size(ins[0])), size(ins[1])) * (PE if narrow(ins[0]) else 4 * PE)
+        if q == "G":
+            return 150 + 2 * size(o)
+        if kind == "scatter":
+            return 60 + SCATTER * size(ins[0])
+        if ins and len(ins[0][1]) > 1:
+            return 60 + GATHER * size(o)
+        if kind == "two":
+            return FIX + max(64, size(o) * (1 if any(x[1][0][0].startswith("pb") for x in ins) else 2))
+        return FIX + max(64, size(o) * (0.5 if q == "V" and narrow(o, *ins[:1]) else 1))
+
+    def op(q, fn, outs, ins, kind=None):
         reads = [r for i in ins for r in i[1]]
         writes = [r for o in outs for r in o[1]]
-        sync(q, reads, writes)
-        call = fn()
-        cnt[q] += 1
-        n = cnt[q]
-        call.then_inc(semof(q), 1)
-        snap[(q, n)] = dict(clk[q])
-        snap[(q, n)][q] = n - 1
-        note(q, n, reads, writes)
+
+        def emit():
+            sync(q, reads, writes)
+            call = fn()
+            cnt[q] += 1
+            n = cnt[q]
+            call.then_inc(semof(q), 1)
+            snap[(q, n)] = dict(clk[q])
+            snap[(q, n)][q] = n - 1
+            note(q, n, reads, writes)
+        plan.append((q, cycles(q, outs[0], ins, kind), 0, reads, writes, emit, None))
 
     def sc(x):
         return x[0] if isinstance(x, tuple) else x
@@ -134,20 +165,27 @@ def make(g, T):
     def tl(*xs):
         return [x for x in xs if isinstance(x, tuple)]
 
-    def tt(o, a, b, f): op("V", lambda: eng["V"].tensor_tensor(o[0], a[0], b[0], f), [o], [a, b])
+    def tt(o, a, b, f): op("V", lambda: eng["V"].tensor_tensor(o[0], a[0], b[0], f), [o], [a, b], "two")
     def ts(o, a, s1, s2, f0, f1=None):
         if f1 is None:
             op("V", lambda: eng["V"].tensor_scalar(o[0], a[0], sc(s1), None, f0), [o], [a] + tl(s1))
         else:
             op("V", lambda: eng["V"].tensor_scalar(o[0], a[0], sc(s1), sc(s2), f0, f1), [o], [a] + tl(s1, s2))
     def cp(o, a): op("V", lambda: eng["V"].tensor_copy(o[0], a[0]), [o], [a])
-    def scat(tab, off, a): op("V", lambda: eng["V"].tensor_copy(tab[0].indirect(off[0]), a[0]), [tab], [a, off])
+    def scat(q, tab, off, a):
+        if q == "V":
+            op("V", lambda: eng["V"].tensor_copy(tab[0].indirect(off[0]), a[0]), [tab], [a, off], "scatter")
+        else:
+            op("S", lambda: eng["S"].activation(tab[0].indirect(off[0]), a[0], F.Silu), [tab], [a, off], "scatter")
     def scan(o, a, b, i, f0, f1): op("V", lambda: eng["V"].tensor_tensor_scan(o[0], a[0], b[0], i, f0, f1), [o], [a, b])
-    def red(o, a): op("V", lambda: eng["V"].tensor_reduce(o[0], a[0], AX.X, A.add), [o], [a])
     def fill(o, c): op("V", lambda: eng["V"].memset(o[0], c), [o], [])
-    def act(o, a, f=F.Copy, scale=1.0, bias=0.0):
-        op("S", lambda: eng["S"].activation(o[0], a[0], f, bias=sc(bias), scale=sc(scale)), [o], [a] + tl(bias, scale))
-    def mm(o, l, r, st=True, sp=True): op("P", lambda: eng["P"].matmul(o[0], l[0], r[0], st, sp), [o], [l, r])
+    def act(o, a, f=F.Copy, scale=1.0, bias=0.0, total=None):
+        if total is None:
+            op("S", lambda: eng["S"].activation(o[0], a[0], f, bias=sc(bias), scale=sc(scale)), [o], [a] + tl(bias, scale))
+        else:
+            op("S", lambda: eng["S"].activation(o[0], a[0], f, bias=sc(bias), scale=sc(scale), accum_out=total[0]), [o, total], [a] + tl(bias, scale))
+    def mm(o, l, r, st=True, sp=True):
+        op("P", lambda: eng["P"].matmul(o[0], l[0], r[0], st, sp), [o if st and sp else B(o[1][0][0])], [l, r])
     def iota(o, pat, base, cm, whole=False):
         if whole:
             op("G", lambda: g.iota(o[0], pat, base, cm), [o], [])
@@ -157,31 +195,94 @@ def make(g, T):
 
     def dma(q, sem, out, in_, outs, ins):
         reads, writes = [r for i in ins for r in i[1]], [r for o in outs for r in o[1]]
-        sync(q, reads, writes)
-        eng[q].dma_start(out, in_).then_inc(T.sem[sem], 16)
-        snap[(sem, 16)] = dict(clk[q])
-        note(sem, 16, reads, writes)
+
+        def emit():
+            sync(q, reads, writes)
+            eng[q].dma_start(out, in_).then_inc(T.sem[sem], 16)
+            snap[(sem, 16)] = dict(clk[q])
+            note(sem, 16, reads, writes)
+        plan.append((q, 100, LAG + sum(size(x) for x in outs + ins), reads, writes, emit, None))
 
     def arrive(sem, n, b):
-        snap[(sem, n)] = {}
-        note(sem, n, [], b[1])
+        def emit():
+            snap[(sem, n)] = {}
+            note(sem, n, [], b[1])
+        plan.append((sem, 0, 0, [], b[1], emit, sends[sem]))
 
     def send(core, dst, topo, o, i, rsem):
-        sync("G", i[1], [])
-        rid, pid = topo.addr(dst, core)
-        g.remote_dma(o[0], i[0], T.sem[rsem], T.sem.sent, pid, rid, topo.mask(core, dst))
+        def emit():
+            sync("G", i[1], [])
+            rid, pid = topo.addr(dst, core)
+            g.remote_dma(o[0], i[0], T.sem[rsem], T.sem.sent, pid, rid, topo.mask(core, dst))
+        sends[rsem] = len(plan)
+        plan.append(("G", 600, FAR + 3 * size(i), i[1], [], emit, None))
         return len(topo.engines(core, dst))
 
-    return dict(B=B, I=I, tt=tt, ts=ts, cp=cp, scat=scat, scan=scan, red=red, fill=fill, act=act, mm=mm, iota=iota, asel=asel, dma=dma,
-                arrive=arrive, send=send, cnt=cnt)
+    def issue():
+        if not ORDER:
+            ORDER.extend(order(plan))
+        for i in ORDER:
+            plan[i][5]()
+
+    return dict(B=B, I=I, tt=tt, ts=ts, cp=cp, scat=scat, scan=scan, fill=fill, act=act, mm=mm, iota=iota, asel=asel, dma=dma,
+                arrive=arrive, send=send, issue=issue, cnt=cnt)
 
 
-def weave(*lists):
-    lists = [list(x) for x in lists]
-    while any(lists):
-        for x in lists:
-            if x:
-                x.pop(0)()
+def order(plan):
+    n = len(plan)
+    pred, acc, bank = [], {}, {}
+    for i, (q, cost, lag, reads, writes, emit, after) in enumerate(plan):
+        p = {}
+        for regs, w in ((reads, False), (writes, True)):
+            for reg in regs:
+                for (j, old, rw) in acc.get(reg[0], ()):
+                    if (w or rw) and meet(reg, old):
+                        d = (0 if q == "P" else OWN) if plan[j][0] == q else CROSS
+                        p[j] = max(p.get(j, 0), d + plan[j][2])
+        if q == "P":
+            if writes[0][0] in bank:
+                p.setdefault(bank[writes[0][0]], 0)
+            bank[writes[0][0]] = i
+        if after is not None:
+            p[after] = plan[after][2]
+        pred.append(p)
+        for reg in writes:
+            acc[reg[0]] = [x for x in acc.get(reg[0], []) if not covers(reg, x[1])] + [(i, reg, True)]
+        for reg in reads:
+            acc.setdefault(reg[0], []).append((i, reg, False))
+    succ = [{} for _ in plan]
+    for i in range(n):
+        for j, d in pred[i].items():
+            succ[j][i] = d
+    banks = [{r[0] for r in x[3] + x[4] if r[0].startswith("pb")} for x in plan]
+
+    def lay(pred, succ, urge, head, tail):
+        left = [len(p) for p in pred]
+        ready = {i: head[i] for i in range(n) if not left[i]}
+        free, end, used, out = {}, [0] * n, {}, []
+        while ready:
+            st = {i: max([free.get(plan[i][0], 0), s] + [e + CROSS for b in banks[i] for r, e in used.get(b, {}).items() if r != plan[i][0]])
+                  for i, s in ready.items()}
+            first = min(st, key=lambda i: (st[i], -urge[i]))
+            q = plan[first][0]
+            i = max((j for j in st if plan[j][0] == q and st[j] <= st[first] + min(SLACK, plan[first][1])), key=lambda j: urge[j])
+            end[i] = free[q] = st[i] + plan[i][1]
+            for b in banks[i]:
+                used.setdefault(b, {})[q] = end[i]
+            del ready[i]
+            out.append(i)
+            for k in succ[i]:
+                left[k] -= 1
+                if not left[k]:
+                    ready[k] = max([head[k]] + [end[j] + d for j, d in pred[k].items()])
+        return max(end[i] + tail[i] for i in range(n)), out, end
+
+    none, lag = [0] * n, [x[2] for x in plan]
+    best = run = lay(pred, succ, [-i for i in range(n)], none, lag)
+    for _ in range(ROUNDS):
+        run = lay(pred, succ, lay(succ, pred, run[2], lag, none)[2], none, lag)
+        best = min(best, run)
+    return best[1]
 
 
 def rank_program(g, core, T, topo):
@@ -189,26 +290,53 @@ def rank_program(g, core, T, topo):
     if rank is None:
         return
     K = make(g, T)
-    B, I, tt, ts, cp, scat, scan, red, fill, act, mm, iota, asel, dma = (K[k] for k in (
-        "B", "I", "tt", "ts", "cp", "scat", "scan", "red", "fill", "act", "mm", "iota", "asel", "dma"))
+    B, I, tt, ts, cp, scat, scan, fill, act, mm, iota, asel, dma = (K[k] for k in (
+        "B", "I", "tt", "ts", "cp", "scat", "scan", "fill", "act", "mm", "iota", "asel", "dma"))
     nxt = T.cores[(rank + 3) % len(T.cores)]
     prv_eng = len(topo.engines(T.cores[(rank + 1) % len(T.cores)], core))
+    ET, FT, XS = B("ET", SP, SP + 2048), B("FT", 16, 2064), B("XS")
 
-    def dedupe(c, bank, a, flist, fpos):
-        s = str(c)
-        own = B("FL", 96 * c + 15, 96 * c + 96, 16)
-        return [lambda: tt(B("RMk" + s), B(bank, a, a + 96), B("NEG", 0, 96), A.add),
-                lambda: scan(B("FL", 96 * c, 96 * c + 96), B("HOLD", 0, 96), B("RMk" + s), 0.0, A.add, A.max),
-                lambda: tt(B("eq" + s, 0, 95), B(bank, a + 1, a + 96), B("FL", 96 * c, 96 * c + 95), A.is_equal),
-                lambda: cp(flist, own),
-                lambda: scan(B("dup" + s, 0, 95), B("SEG", 0, 95), B("eq" + s, 0, 95), 0.0, A.mult, A.max),
-                lambda: ts(B("pT" + s), B("dup" + s, 14, 95, 16), B("TC"), None, A.mult),
-                lambda: tt(B("pQ" + s), B("pT" + s), own, A.max),
-                lambda: cp(fpos, B("pQ" + s))]
+    def lin(name, o, a, scale, bias):
+        if name in ONS:
+            act(o, a, scale=scale, bias=bias)
+        elif scale == 1.0:
+            ts(o, a, bias, None, A.add)
+        else:
+            ts(o, a, scale, bias, A.mult, A.add)
 
-    def marks(tab, val, pos, p0, t, c):
-        return [lambda b=b: scat(B(tab), B(pos, p0 + 2 * b, p0 + 2 * b + 1), B(val, 192 * t + 16 * b, 192 * t + 16 * b + 16))
-                for b in range(6 * c + 5, 6 * c - 1, -1)]
+    def lst(buf, t, c, a=0, b=None):
+        o = 64 * t + 32 * c
+        return B(buf, o + a, o + (CHUNK[c][1] // 16 if b is None else b))
+
+    def msg(buf, t, c, j, j1=None):
+        p0, n = CHUNK[c]
+        o = 576 * t + 3 * p0
+        return B(buf, o + n * j, o + n * (j + 1 if j1 is None else j1))
+
+    def col(name, c, h=None):
+        p0, n = CHUNK[c]
+        if h is None:
+            return B(name, p0, p0 + n)
+        return B(name, 2 * p0, 2 * p0 + 2 * n) if h == 2 else B(name, 2 * p0 + h * n, 2 * p0 + h * n + n)
+
+    def spread(c, l, r):
+        mm(col("pb7", c, 2), B("ID"), col("CB", c, 2), True, False)
+        mm(col("pb7", c, 1), l, r, False, False)
+        mm(col("pb7", c, 0), l, r, False, True)
+
+    def dedupe(c, buf, t):
+        n, s = CHUNK[c][1], str(c)
+        fl, ne, dup = B("FL" + s, 0, n), B("ne" + s, 0, n), B("dup" + s, 0, n)
+        scan(fl, B("HOLD", 0, n), col("pb7", c, 1), 0.0, A.add, A.max)
+        tt(ne, col("pb7", c, 0), fl, A.not_equal)
+        ts(lst(buf, t, c), B("FL" + s, 15, n, 16), -16.0, None, A.add)
+        scan(dup, ne, col("pb7", c, 1), 0.0, A.mult, A.max)
+        ts(B(buf, 64 * t + 32 * c + 8, 64 * t + 32 * c + 8 + n // 8, 2), B("dup" + s, 15, n, 16), B("qi"), None, A.max)
+
+    def marks(q, val, v0, buf, t, c):
+        p0, n = CHUNK[c]
+        for b in range(n // 16 - 1, -1, -1):
+            scat(q, B("FT"), lst(buf, t, c, 8 + 2 * b, 9 + 2 * b), B(val, v0 + p0 + 16 * b, v0 + p0 + 16 * b + 16))
 
     dma("Y", "ld0", T.v0s[:], T.v0[:], [B("v0s")], [])
     QW = 512
@@ -218,355 +346,268 @@ def rank_program(g, core, T, topo):
     dma("S", "ld2", T.wts[:], T.wt[:], [B("wts")], [])
     dma("S", "ld7", T.XS[:], T.xs[:], [B("XS")], [])
 
-    fill(B("ones"), 1.0); fill(B("onef"), 1.0); fill(B("GFt"), 32.0); fill(B("GTt"), 1024.0); fill(B("o32"), 1.0 / 32)
+    for n, v in (("ones", 1.0), ("onef", 1.0), ("HOLD", 0.0), ("CB", 16.0), ("v0f", 0.0), ("OT", 0), ("WNa", -128 * U), ("RST", -1.0e20),
+                 ("RSP", 1.0e6), ("C32", 32.0), ("WF0", 0.0), ("WF1", 0.0), ("WS0", 0.0), ("WS1", 0.0)):
+        fill(B(n), v)
+    fill(B("HOLD", 0, 128, 16), -8192.0); fill(B("RST", 0, 128, 16), 1.0e20); fill(B("pb6", 256, 272), 0.0); fill(B("RT", 0, 64), 0)
     iota(B("qI"), [[0, 1]], 0, 1, True)
-    iota(B("CI"), [[0, 12], [1, 16]], 0, 0)
-    asel(B("BDt"), B("ones", 0, 128), [[-16, 8], [0, 16]], A.is_ge, 0.0, 0, 1)
+    iota(B("CI"), [[0, 16], [1, 16]], 0, 0)
+    iota(B("LI"), [[1, 12]], 0, 0)
+    iota(B("RSi"), [[-16, 16]], -16, 0)
+    for j in range(4):
+        iota(B("FT", 516 * j, 516 * j + 516), [[0, 516]], 9999, 0)
+    for t in range(HOPS):
+        iota(B("VV", 192 * t, 192 * t + 192), [[32, 12], [-2, 16]], 4096 - 512 * t + 29, 0)
+        iota(B("VAL", 192 * t, 192 * t + 192), [[32, 12], [-2, 16]], 4096 - 512 * t + 30, 0)
+    for c in (0, 1):
+        iota(col("CKt", c, 2), [[0, 2], [-64, CHUNK[c][1] // 16], [4, 16]], -2202 - 60 - 4 * CHUNK[c][0], 0)
+    asel(B("BDt"), B("ones"), [[-16, 8], [0, 16]], A.is_ge, 0.0, 0, 1)
     asel(B("BD"), B("BDt"), [[16, 8], [0, 16]], A.is_ge, 0.0, 15, -1)
-    asel(B("BAND"), B("ones", 0, 160), [[1, 160]], A.is_equal, 0.0, -16, -1)
+    asel(B("ID"), B("ones"), [[-1, 128]], A.is_equal, 0.0, 0, 1)
+    asel(B("SEL"), B("onef"), [[-1, 16], [-16, 8]], A.is_equal, 0.0, 0, 1)
     asel(B("GBt"), B("onef", 0, 8), [[-16, 8]], A.is_ge, 0.0, 0, 1)
     asel(B("GB"), B("GBt"), [[16, 8]], A.is_ge, 0.0, 15, -1)
-    asel(B("ID"), B("ones", 0, 128), [[-1, 128]], A.is_equal, 0.0, 0, 1)
-    iota(B("VAL", 0, 192), [[32, 12], [-2, 16]], 30, 0)
-    iota(B("VV", 0, 192), [[32, 12], [-2, 16]], 29, 0)
-    asel(B("EXPT"), B("ones", 0, 136), [[-16, 8], [0, 17]], A.is_equal, 0.0, 0, 1)
-    iota(B("FV"), [[0, 2064]], 9999, 0)
-    ts(B("qJ"), B("qI"), 15, None, A.bitwise_and)
-    cp(B("qi"), B("qJ"))
-    ts(B("RM16"), B("CI", 0, 16), B("qi"), None, A.is_equal)
-    ts(B("WC"), B("RM16"), -2097152.0 + 8192.0, -8192.0, A.mult, A.add)
-    act(B("GBs"), B("GB"), scale=2.0 ** -10)
-    for i in range(16):
-        act(B("selB", 8 * i, 8 * i + 8), B("GBs"), scale=B("RM16", i, i + 1))
-        act(B("WN", 8 * i, 8 * i + 8), B("GB"), scale=B("WC", i, i + 1))
-    act(B("INK"), B("ID"), scale=-2048.0)
-    ts(B("EQD"), B("CI"), B("qi"), None, A.is_equal)
-    ts(B("NEG"), B("EQD"), 4096.0, -4096.0, A.mult, A.add)
-    fill(B("HOLD"), 0.0); fill(B("SEG"), 1.0); fill(B("OT"), 0); fill(B("MM", 192, 384), 0.0)
-    fill(B("HOLD", 0, 192, 16), -8192.0); fill(B("SEG", 0, 192, 16), 0.0)
-    cp(B("v0f"), B("v0s"))
-    for i in range(16):
-        act(B("LM", i, 192, 16), B("v0f"), scale=B("RM16", 15 - i, 16 - i))
-    mm(B("pb7", 0, 192), B("BD"), B("LM"))
-    act(B("MM", 0, 192), B("pb7", 0, 192))
-    ts(B("TC"), B("qi"), 2048.0, None, A.add)
-    for i in range(16):
-        ts(B("ZI", 160 * i, 160 * i + 160), B("BAND"), B("RM16", i, i + 1), None, A.mult)
-    fill(B("NT", 2048, 2432), 0.0); fill(B("ST", 2048, 2432), 0.0)
-    for j in range(4):
-        a, b = j * QW, (j + 1) * QW
-        ts(B("tmpB", a, b), B("enS", a, b), 1.0 / 2048, 159.5 + 1.0 / 8192, A.mult, A.add)
-        act(B("ST", a, b), B("tmpB", a, b), bias=-160.0)
-        mm(B("pb%d" % j), B("INK"), B("ST", a, b))
-    for i in range(16):
-        act(B("Zz", i, 192, 16), B("z0s", 15 - i, 192, 16))
-    weave(*[dedupe(c, "pb7", 96 * c, B("RT", 6 * c, 6 * c + 6), B("RT", 12 + 12 * c, 24 + 12 * c, 2)) for c in CH])
-    ts(B("qs1"), B("qi"), 1.0, None, A.add)
-    cp(B("wtf"), B("wts"))
-    ts(B("q15"), B("qi"), 15.0, None, A.is_equal)
+    asel(B("WNb"), B("WNa"), [[0, 16], [-16, 8]], A.is_ge, 0.0, 0, 1)
+    asel(B("WNa"), B("WNb"), [[0, 16], [16, 8]], A.is_ge, 0.0, 15, -1)
+    asel(B("WN"), B("WNa"), [[-1, 16], [-16, 8]], A.not_equal, -65536 * U, 0, 1)
+    asel(B("GF", 0, 128, 1, 0, 16), B("ones", 0, 128, 1, 0, 16), [[-1, 8], [0, 16]], A.is_equal, 0.0, 0, 1)
+    asel(B("GT", 0, 128, 1, 0, 16), B("ones", 0, 128, 1, 0, 16), [[-1, 8], [0, 16]], A.is_equal, 0.0, -8, 1)
+    ts(B("qJ"), B("qI"), 15, None, A.bitwise_and); cp(B("qi"), B("qJ")); cp(B("qp"), B("qI")); cp(B("wtf"), B("wts"))
     ts(B("qK"), B("qJ"), 1, None, A.bitwise_and)
-    ts(B("qe"), B("qK"), -1.0, 1.0, A.mult, A.add)
-    tt(B("w1"), B("qe"), B("q15"), A.add)
-    ts(B("qo"), B("w1"), -1.0, 1.0, A.mult, A.add)
-    act(B("W16"), B("GB"), scale=1024.0)
-    act(B("WD"), B("GB"), scale=B("wtf"))
-    act(B("IDb"), B("ID")); act(B("I22"), B("ID"), scale=4194304.0)
+    ts(B("qr"), B("qi"), -1.0, 15.0, A.mult, A.add)
+    ts(B("qa"), B("qi"), -15.5 - T0, None, A.add); ts(B("qb"), B("qi"), 2.0 ** -18, None, A.mult)
+    ts(B("q15"), B("qi"), 15.0, None, A.is_equal); ts(B("qe"), B("qK"), -1.0, 1.0, A.mult, A.add)
+    tt(B("w1"), B("qe"), B("q15"), A.add); ts(B("qo"), B("w1"), -1.0, 1.0, A.mult, A.add)
+    ts(B("qh"), B("qp"), 8.0, None, A.is_ge)
+    ts(B("SCq"), B("qh"), 1.0 / 2048 - 1.0, 1.0, A.mult, A.add); ts(B("BIq"), B("qh"), -B0 / 2048, None, A.mult)
+    ts(B("EQD"), B("CI"), B("qi"), None, A.is_equal); ts(B("EQR"), B("CI", 0, 192), B("qr"), None, A.is_equal)
+    cp(B("LC"), B("LI")); ts(B("LP"), B("LI"), 16.0, B("qr"), A.mult, A.add)
+    ts(B("RSP", 0, 256, 16), B("RSi"), B("qi"), None, A.add)
+    act(B("CKu"), B("EQD"), scale=2.0)
+    for c in (0, 1):
+        act(col("CB", c, 1), B("EQD", 0, CHUNK[c][1]), scale=4096.0, bias=-4080.0)
+        tt(col("CK", c, 2), col("CKt", c, 2), B("CKu", 0, 2 * CHUNK[c][1]), A.add)
+    for n, v in (("I2K", 2048.0), ("I37", 2.0 ** 18 * U), ("IDb", 1.0), ("NID", -1.0), ("N64", -64.0), ("I4K", 4096.0),
+                 ("DE", B("qe")), ("DO", B("qo")), ("D15", B("q15"))):
+        act(B(n), B("ID"), scale=v)
+    for n, v in (("WX", 32 * U), ("WR", -16 * U), ("WA", 16 * U), ("WD", B("wtf"))):
+        act(B(n), B("GB"), scale=v)
+    for t in range(HOPS - 1):
+        act(B("BT", t, t + 1), B("q15"), scale=2048.0 * (9 + t))
+    act(B("qs1"), B("qi"), bias=1.0); act(B("qy15"), B("q15"), scale=16.0)
+    act(B("YW"), B("BD"), scale=B("qs1")); act(B("Y15"), B("BD"), scale=B("qy15"))
+    act(B("YE"), B("YW"), scale=B("qe")); act(B("YO"), B("YW"), scale=B("qo"))
+
     for j in range(4):
-        a, b = j * QW, (j + 1) * QW
-        tt(B("NT", a, b), B("enS", a, b), B("pb%d" % j), A.add)
-
-    def consts_late(part):
-        if part:
-            iota(B("FF"), [[0, 2064]], 9999, 0)
-            for t in range(1, HOPS):
-                iota(B("VAL", 192 * t, 192 * t + 192), [[32, 12], [-2, 16]], 30 - 512 * t, 0)
-                iota(B("VV", 192 * t, 192 * t + 192), [[32, 12], [-2, 16]], 29 - 512 * t, 0)
-            return
-        asel(B("SELT"), B("o32"), [[-16, 8], [-1, 17]], A.is_equal, 0.0, 1, 1)
-        iota(B("KTHR"), [[0, 8], [-1, 17]], 17, 0)
-        iota(B("BK"), [[0, 8], [64, 17]], -64, 0)
-        asel(B("GF", 0, 128, 1, 0, 16), B("GFt", 0, 128, 1, 0, 16), [[-1, 8], [0, 16]], A.is_equal, 0.0, 0, 1)
-        asel(B("GT", 0, 128, 1, 0, 16), B("GTt", 0, 128, 1, 0, 16), [[-1, 8], [0, 16]], A.is_equal, 0.0, -8, 1)
-        iota(B("TRb"), [[1, 24]], 2048, 0)
-
-    def consts_v1():
-        return [lambda: fill(B("SELT", 0, 136, 17), 0.0), lambda: fill(B("BK", 0, 136, 17), -524288.0),
-                lambda: fill(B("RST"), -1.0e7), lambda: fill(B("RST", 0, 136, 17), 1.0e7)]
-
-    def consts_v2():
-        return [lambda: ts(B("q24"), B("qi"), 24.0, None, A.mult), lambda: ts(B("TR"), B("TRb"), B("q24"), None, A.add),
-                lambda: ts(B("OFFD"), B("EQD"), 1.0e6, -1.0e6, A.mult, A.add),
-                lambda: tt(B("OWN", 0, 192), B("VAL", 0, 192), B("OFFD"), A.add)]
-
-    def consts_s():
-        act(B("NID"), B("ID"), scale=-1.0); act(B("P64"), B("ID"), scale=64.0); act(B("N64"), B("ID"), scale=-64.0)
-        act(B("DE"), B("ID"), scale=B("qe")); act(B("DO"), B("ID"), scale=B("qo")); act(B("D15"), B("ID"), scale=B("q15"))
-        act(B("DEb"), B("ID"), scale=B("qe")); act(B("DOb"), B("ID"), scale=B("qo"))
-        for t in range(HOPS):
-            act(B("BT", t, t + 1), B("q15"), scale=9.0 + t)
-        act(B("I2K"), B("ID"), scale=2048.0)
-        act(B("GBy"), B("GB"), scale=2048.0)
-        act(B("YWn"), B("GB"), scale=B("qs1")); act(B("YWs"), B("GBy"), scale=B("qs1"))
+        cp(B("ET", SP + j * QW, SP + j * QW + QW), B("enS", j * QW, j * QW + QW))
+    cp(B("v0f", 0, 12), B("v0s"))
+    tt(B("LM"), I(B("v0f"), B("LC")), B("EQR"), A.mult)
+    for c in (0, 1):
+        fill(msg("MM", 0, c, 1), T0)
+        spread(c, B("BD"), col("LM", c))
+        mm(col("pb4", c), B("BD"), col("LM", c))
+        act(msg("MM", 0, c, 0), col("pb4", c))
+        act(msg("MM", 0, c, 2), I(B("z0s"), B("LP", CHUNK[c][0] // 16, (CHUNK[c][0] + CHUNK[c][1]) // 16)))
+        dedupe(c, "RT", 0)
 
     sent = 0
-    held = []
     for t in range(HOPS):
         last = t == HOPS - 1
-        zc, mc, rc = 192 * t, 384 * t, 40 * t
+        base = 4096 - 512 * t
         if t > 0:
-            K["arrive"]("aL%d" % t, prv_eng, B("RT", rc, rc + 36))
-            K["arrive"]("aM%d" % t, prv_eng, B("MM", mc, mc + 384))
-            for c in CH:
-                K["arrive"]("aZ%d%d" % (c, t), prv_eng, B("Zz", zc + 96 * c, zc + 96 * c + 96))
-        vl, fl = B("RT", rc, rc + 12), B("OT", rc, rc + 12)
+            for c in (0, 1):
+                K["arrive"]("aL%d%d" % (c, t), prv_eng, lst("RT", t, c, 0, 24))
+                K["arrive"]("aM%d%d" % (c, t), prv_eng, msg("MM", t, c, 0, 3))
 
-        def W(n, a=0, b=16, st=1):
-            return B(n, a, b, st, 0, 96)
+        def W(c, n, a=0, b=128, st=1):
+            return B(n, a, b, st, 0, CHUNK[c][1])
 
         def bc(name, c, k):
-            return B(name, 1536 * c + k, 1536 * c + 1536, 16)
+            return B(name, 16 * CHUNK[c][0] + k, 16 * (CHUNK[c][0] + CHUNK[c][1]), 16)
 
-        def gat(c, what):
-            act(B(what, 1536 * c, 1536 * c + 1536), I(B("NT" if what == "X" else "ST"), B("RL", 96 * c, 96 * c + 96)))
+        def ring(c):
+            cp(col("RI", c), I(ET, lst("RT", t, c)))
+            ts(col("RJ", c), col("RI", c), 2047, None, A.bitwise_and)
+            cp(col("RL", c), col("RJ", c))
 
-        def selx(c):
+        def rings(q, a, b):
+            for p in range(a, b, PC):
+                o, i = B("X", 16 * p, 16 * min(b, p + PC)), I(ET, B("RL", p, min(b, p + PC)))
+                if q == "V":
+                    ts(o, i, B0, None, A.add)
+                else:
+                    act(o, i, bias=B0)
+
+        def records(q, a, b):
+            for p in range(a, b, PC):
+                (cp if q == "V" else act)(B("R", 16 * p, 16 * min(b, p + PC)), I(XS, B("AL", p, min(b, p + PC))))
+
+        def pick(c):
+            s, n = str(c), CHUNK[c][1]
             for k in range(16):
                 i = (k + t) % 16
-                off = 160 * i + 16 - (k - i)
-                mm(B("pb4", 96 * c, 96 * c + 96), B("ZI", off, off + 128), bc("X", c, k), k == 0, k == 15)
-
-        def lists(c):
-            cp(B("AL", 96 * c, 96 * c + 96), B("pb4", 96 * c, 96 * c + 96))
-            cp(B("CN", 96 * c, 96 * c + 96), B("AL", 96 * c, 96 * c + 96))
-
-        def rec(c):
-            tt(B("D", 1536 * c, 1536 * c + 1536), I(B("XS"), B("AL", 96 * c, 96 * c + 96)), B("ZE", 1536 * c, 1536 * c + 1536), A.subtract)
-
-        def size(c):
-            act(B("AB", 1536 * c, 1536 * c + 1536), B("D", 1536 * c, 1536 * c + 1536), F.Abs)
+                mm(W(c, "pb" + s, k, 128, 16), bc("X", c, k), B("SEL", 8 * i, 8 * i + 8))
+            lin("sb", W(c, "sb" + s), W(c, "pb" + s), 1.0, -1023.5)
+            tt(W(c, "nm" + s), W(c, "pb" + s), W(c, "sb" + s), A.subtract)
+            mm(col("pb6", c), W(c, "nm" + s), W(c, "ID", 0, n))
+            cp(col("AL", c), col("pb6", c))
 
         def newer(c):
-            return [lambda k=k: tt(bc("M", c, k), bc("S", c, k), B("pb5", 96 * c, 96 * c + 96), A.is_gt) for k in range(16)]
-
-        def pay(c):
-            mm(W("pb%d" % (2 + c), 0, 136), B("CN", 96 * c, 96 * c + 96), B("SELT"), True, False)
+            kk = "pb%d" % (2 + c)
+            mm(col("pb4", c), B("I2K"), msg("MM", t, c, 1))
+            ts(col("PEN", c), msg("MM", t, c, 1), B("qa"), B("qb"), A.add, A.max)
+            mm(W(c, kk), col("PEN", c), B("I37"), True, False)
             for k in range(16):
+                tt(bc("M", c, k), bc("X", c, k), col("pb4", c), A.is_ge)
                 i = (k + t) % 16
-                mm(W("pb%d" % (2 + c), 1 + k, 136, 17), bc("S", c, k), B("selB", 8 * i, 8 * i + 8), False, False)
+                mm(W(c, kk, k, 128, 16), bc("M", c, k), B("WN", 8 * i, 8 * i + 8), False, False)
 
-        def failcol(c):
-            mm(W("pb%d" % (2 + c), 0, 136, 17), W("ID", 0, 96), W("ff", 8 * c, 8 * c + 8), False, True)
-
-        def key0(c):
-            mm(W("pb%d" % c, 0, 136), W("IDb", 0, 96), W("BK", 0, 136), True, False)
-            mm(W("pb%d" % c, 0, 136), W("I22", 0, 96), W("TBc", 136 * c, 136 * c + 136), False, False)
-
-        def keyA(c):
+        def upper(c):
+            kk = "pb%d" % (2 + c)
+            mm(col("pb5", c), B("ID"), msg("MM", t, c, 2))
             for k in range(16):
-                mm(W("pb%d" % c, 1 + k, 136, 17), bc("AB", c, k), B("W16"), False, False)
-
-        def keyM(c):
+                mm(W(c, kk, k, 128, 16), bc("R", c, k), B("WR"), False, False)
             for k in range(16):
-                i = (k + t) % 16
-                mm(W("pb%d" % c, 1 + k, 136, 17), bc("M", c, k), B("WN", 8 * i, 8 * i + 8), False, k == 15)
+                tt(bc("MX", c, k), bc("R", c, k), col("pb5", c), A.max)
+                mm(W(c, kk, k, 128, 16), bc("MX", c, k), B("WX"), False, k == 15)
 
-        def zexp(c, q, k0, k1):
-            for k in range(k0, k1):
-                z = B("Zz", zc + 96 * c, zc + 96 * c + 96)
-                if q == "G":
-                    asel(bc("ZE", c, k), z, [[0, 96]], A.is_equal, 0.0, 0, 0)
-                elif q == "S":
-                    act(bc("ZE", c, k), z)
-                else:
-                    cp(bc("ZE", c, k), z)
+        def sizes(c):
+            p0, n = CHUNK[c]
+            m = 512 // n
+            for k0 in range(0, 16, m):
+                bk = DB[k0 // m % 2]
+                ks = range(k0, min(16, k0 + m))
+                for k in ks:
+                    o = B(bk, (k - k0) * n, (k - k0) * n + n)
+                    mm(o, B("NID"), msg("MM", t, c, 2), True, False)
+                    mm(o, B("IDb"), bc("R", c, k), False, True)
+                act(B("MX", 16 * p0 + k0 * n, 16 * p0 + (k0 + len(ks)) * n), B(bk, 0, len(ks) * n), F.Abs)
+                for k in ks:
+                    mm(W(c, "pb%d" % (2 + c), k, 128, 16), B("MX", 16 * p0 + k * n, 16 * p0 + k * n + n), B("WA"), False, k == 15)
 
-        def tail(c):
+        def hash_():
+            for c in (0, 1):
+                mm(W(c, "pb6", 256 + 8 * c, 264 + 8 * c), msg("MM", t, c, 2), B("WD"))
+            cp(B("ui"), B("pb6", 256, 272))
+            ts(B("ua"), B("ui"), 2047, None, A.bitwise_and)
+            ts(B("ub"), B("ua"), 1184.0, None, A.add)
+            tt(B("uc"), B("ua"), B("ub"), A.mult)
+            if t > 0:
+                act(B("Ax"), B("pb6", 272, 273), scale=-1.0, bias=4080 - 17 * 65536.0)
+                act(B("Ay"), B("pb6", 272, 273), F.Identity, bias=B("Ax"))
+                ts(B("ud"), B("uc"), B("Ay"), None, A.add)
+            else:
+                cp(B("ud"), B("uc"))
+            ts(B("ue"), B("ud"), 5, 2047, A.arith_shift_right, A.bitwise_and)
+            ts(B("ff"), B("ue"), B0 - 2048, None, A.add)
+
+        def least(c):
             s = str(c)
-            kk, pp = W("pb%d" % c, 0, 136), W("pb%d" % (2 + c), 0, 136)
-            mn, dd, ee, oo = (W(n + s, 0, 136) for n in ("Mn", "dd", "ee", "oo"))
-            o16 = W("oo" + s, 16, 136, 17)
-            return [lambda: scan(mn, W("RST", 0, 136), kk, 0.0, A.max, A.min), lambda: tt(dd, kk, mn, A.subtract),
-                    lambda: tt(ee, pp, dd, A.subtract), lambda: scan(oo, dd, ee, 0.0, A.min, A.max),
-                    lambda: ts(W("WT" + s, 0, 8), o16, 393216.0, 393216.0, A.add, A.subtract),
-                    lambda: tt(W("WT" + s, 8, 16), o16, W("WT" + s, 0, 8), A.subtract)]
+            kk, pp = W(c, "pb%d" % (2 + c)), W(c, "pb" + s)
+            mn, dd, ee, oo = (W(c, n + s) for n in ("Mn", "dd", "ee", "oo"))
+            t1, t2, fin = (W(c, n + s, 0, 8) for n in ("t1", "t2", "fin"))
+            scan(mn, W(c, "RST"), kk, 0.0, A.max, A.min)
+            tt(dd, kk, mn, A.subtract)
+            lin("t1", t1, W(c, "Mn" + s, 15, 128, 16), -1.0, -16384 * U)
+            tt(ee, pp, dd, A.subtract)
+            tt(t2, t1, W(c, "ff", 8 * c, 8 * c + 8), A.max)
+            scan(oo, dd, ee, 0.0, A.min, A.max)
+            tt(fin, W(c, "oo" + s, 15, 128, 16), t2, A.min)
+            lin("WS", W(c, "WS" + s, 8, 16), fin, 1.0, -1023.5)
+            tt(W(c, "WF" + s, 0, 8), fin, W(c, "WS" + s, 8, 16), A.subtract)
 
         def turn(c):
-            q = B("pb6", 320 + 96 * c, 416 + 96 * c, 1, 0, 16)
-            tp = B("TPs", 96 * c, 96 * c + 96, 1, 0, 16)
-            mm(q, W("WT%d" % c, 0, 16), W("ID", 0, 96))
-            act(tp, q)
-            mm(B(RB[c], 0, 96), B("GF", 0, 128, 1, 0, 16), tp)
-            mm(B(RB[c], 96, 192), B("GT", 0, 128, 1, 0, 16), tp)
-
-        def share(c):
-            for k in (0, 1):
-                act(B("MO", mc + 192 * k + 96 * c, mc + 192 * k + 96 * c + 96), B(RB[c], 96 * k, 96 * k + 96))
+            p0, n = CHUNK[c]
+            q = B("pb6", 288 + p0, 288 + p0 + n, 1, 0, 16)
+            tp = B("TPs", p0, p0 + n, 1, 0, 16)
+            mm(q, W(c, "WS%d" % c, 0, 16), W(c, "IDb", 0, n), True, False)
+            mm(q, W(c, "WF%d" % c, 0, 16), W(c, "ID", 0, n), False, True)
+            act(tp, q, F.Relu, scale=B("SCq", 0, 1, 1, 0, 16), bias=B("BIq", 0, 1, 1, 0, 16))
+            spread(c, B("GF", 0, 128, 1, 0, 16), tp)
+            mm(B("pb4", 0, n), B("GF", 0, 128, 1, 0, 16), tp)
+            mm(B("pb4", n, 2 * n), B("GT", 0, 128, 1, 0, 16), tp)
+            act(msg("MO", t, c, 0), B("pb4", 0, n))
+            act(msg("MO", t, c, 1), B("pb4", n, 2 * n), bias=T0)
 
         def zproc(c):
-            a, b = 96 * c, 96 * c + 96
-            zt = B("Zz", zc + a, zc + b)
-            act(B("FM", a, b), B(RB[c], 96, 192), F.Relu, scale=-1.0, bias=1.0)
-            act(B("XF", a, b), I(B("XS"), B("OT", rc + 6 * c, rc + 6 * c + 6)))
-            mm(B("pb1", a, b), B("ID"), zt, True, False)
-            mm(B("pb1", a, b), B("NID"), B("XF", a, b), False, True)
-            mm(B("pb3", a, b), B("ID"), zt, True, False)
-            mm(B("pb3", a, b), B("N64"), B("FM", a, b), False, True)
-            act(B("AZ", a, b), B("pb1", a, b), F.Abs)
-            act(B("R1", a, b), B("pb3", a, b), F.Relu)
-            mm(B("pb3", 192 + a, 192 + b), B("ID"), B("AZ", a, b), True, False)
-            mm(B("pb3", 192 + a, 192 + b), B("P64"), B("FM", a, b), False, True)
-            act(B("R2", a, b), B("pb3", 192 + a, 192 + b), F.Relu, bias=-64.0)
-            mm(B("pb1", 192 + a, 192 + b), B("ID"), B("R1", a, b), True, False)
-            mm(B("pb1", 192 + a, 192 + b), B("ID"), B("R2", a, b), False, True)
-            if not last:
-                act(B("ZO", zc + a, zc + b), B("pb1", 192 + a, 192 + b))
+            n = CHUNK[c][1]
+            p1, p2 = B("pb4", 256, 256 + n), B("pb4", 384, 384 + n)
+            act(col("XF", c), I(XS, lst("OT", t, c)))
+            mm(p1, B("N64"), msg("MO", t, c, 1), True, False)
+            mm(p1, B("ID"), col("XF", c), False, True)
+            act(col("R1", c), p1, F.Relu, bias=64 * T0)
+            mm(p2, B("ID"), msg("MM", t, c, 2), True, False)
+            mm(p2, B("NID"), col("R1", c), False, True)
+            act(col("ZL", c) if last else msg("MO", t, c, 2), p2, F.Abs)
 
-        def out(o, src, n, a, b, sem):
-            if last:
-                return 0
-            return K["send"](core, nxt, topo, B(o, n * (t + 1) + a, n * (t + 1) + b), B(src, n * t + a, n * t + b), sem + str(t + 1))
+        def meetings(c):
+            p0, n = CHUNK[c]
+            y, ys, pos = "pb%d" % (2 + c), "ys%d" % c, B("POS", p0 // 8, (p0 + n) // 8)
+            vl, fl = lst("RT", t, c), lst("OT", t, c)
+            wo, we, w15 = ("YO", "YE", "Y15") if last else ("DO", "DE", "D15")
+            act(col("Rf", c), I(ET, fl))
+            for h, (own, oth, new) in enumerate((("Rv", "Rf", "MO"), ("Rf", "Rv", "MM"))):
+                o = B("pb%d" % c, n * h, n * h + n)
+                mm(o, B(w15), msg(new, t, c, 0), True, False)
+                for w, r in sorted(((wo, own), (we, oth)), key=lambda x: x[1] == "Rf"):
+                    mm(o, B(w), col(r, c), False, r == "Rf")
+            act(col("NN", c, 2), B("pb%d" % c, 0, 2 * n), F.Identity, bias=16 * 2048.0 * (9 + t) if last else B("BT", t, t + 1))
+            tt(col("PRE", c), I(FT, fl), B("VAL", 192 * t + p0, 192 * t + p0 + n), A.min)
+            marks(MQ[c], "PRE", 0, "OT", t, c)
+            mm(B(y, 0, 2 * n), B("I4K"), col("CK", c, 2), True, False)
+            mm(B(y, 0, n), B("ID"), msg("MM", t, c, 0), False, False)
+            mm(B(y, n, 2 * n), B("ID"), msg("MO", t, c, 0), False, False)
+            lin("av", col("av", c), I(FT, vl), 1.0, 1101.0 - base)
+            lin("af", col("af", c), I(FT, fl), 1.0, 1100.0 - base)
+            for a in ("av", "af"):
+                for h in (0, 1):
+                    mm(B(y, h * n, h * n + n), B("I4K"), col(a, c), False, a == "af" and h == 1)
+            scan(B(ys, 0, 2 * n), B("RSP", 0, 2 * n), B(y, 0, 2 * n), 1.0e6, A.min, A.max)
+            ts(pos, B(ys, 15, 2 * n, 16), float(SP), None, A.add)
+            scat("V", B("YS" if last else "ET"), pos, col("NN", c, 2))
 
-        for c in CH:
-            cp(B("RL", 96 * c, 96 * c + 96), I(B("NT"), B("RT", rc + 6 * c, rc + 6 * c + 6)))
-        act(B("X", 1536, HX), I(B("NT"), B("RL", 96, HR)))
-        cp(B("X", HX, 3072), I(B("NT"), B("RL", HR, 192)))
-        for f_ in held:
-            f_()
-        zexp(1, "S", G1 + V1, 16)
-        gat(0, "X"); gat(1, "S")
-        zexp(0, "S", G0, 16)
-        mm(B("pb5", 0, 192), B("ID"), B("MM", mc + 192, mc + 384))
+        def ysum(j, bk):
+            mm(B(bk), B("YW"), B("ET", SP + 512 * j, SP + 512 * j + 512))
+            act(B("YS", SP + 512 * j, SP + 512 * j + 512), B(bk))
+
+        ring(0); ring(1)
+        rings("S", EV, NA); rings("V", 0, EV); rings("S", NA, 192)
         for c in (0, 1):
-            mm(W("pb6", 136 * c, 136 * c + 136), B("MM", mc + 192 + 96 * c, mc + 288 + 96 * c), B("EXPT"))
-        selx(1)
-        zexp(1, "G", 0, G1)
-        if t == 0:
-            consts_late(0)
-        zexp(0, "G", 0, G0)
-        if t == 0:
-            consts_late(1)
-        e1, e2 = [], []
-        for c in (0, 1):
-            e1.append(lambda c=c: tt(W("TBc", 136 * c, 136 * c + 136), W("pb6", 136 * c, 136 * c + 136), W("KTHR", 0, 136), A.is_ge))
-        e1.append(lambda: cp(B("vlf"), vl))
-        if t > 0:
-            e1.append(lambda: red(W("Af", 0, 1), W("pb3", 480, 496)))
-            e1.append(lambda: cp(W("Ai", 0, 1), W("Af", 0, 1)))
-            e1.append(lambda: ts(W("Aj", 0, 1), W("Ai", 0, 1), 255, None, A.bitwise_and))
-            e1.append(lambda: cp(W("Ac", 0, 1), W("Aj", 0, 1)))
-        else:
-            e1.append(lambda: fill(B("Ac"), 0.0))
-        e2.append(lambda: cp(W("ui"), W("pb6", 288, 304)))
-        e2.append(lambda: ts(W("ua"), W("ui"), 2047, None, A.bitwise_and))
-        e2.append(lambda: tt(W("ub"), W("ua"), W("ua"), A.mult))
-        e2.append(lambda: ts(W("ud"), W("ua"), 37.0, W("Ac", 0, 1), A.mult, A.add))
-        e2.append(lambda: ts(W("uc"), W("ub"), 5, None, A.arith_shift_right))
-        e2.append(lambda: tt(W("ue"), W("uc"), W("ud"), A.add))
-        e2.append(lambda: ts(W("uf"), W("ue"), 2047, None, A.bitwise_and))
-        e2.append(lambda: ts(W("ff"), W("uf"), 1.0 / 32, None, A.mult))
-        weave([lambda k=k: zexp(1, "V", k, k + 1) for k in range(G1, G1 + V1)], consts_v1() if t == 0 else [])
-        lists(1); rec(1)
-        size(1)
-        gat(0, "S")
-        pay(1)
-        n1 = newer(1)
-        weave(n1[:8], e1)
-        for c in (0, 1):
-            mm(W("pb6", 288 + 8 * c, 296 + 8 * c), B("Zz", zc + 96 * c, zc + 96 * c + 96), B("WD"))
-        weave(n1[8:], e2)
-        selx(0)
-        key0(1); keyA(1); keyM(1)
-        failcol(1)
-        lists(0); rec(0)
-        pay(0); key0(0); failcol(0)
-        weave(consts_v2() if t == 0 else [])
-        size(0)
-        n0 = newer(0)
-        weave(n0[:6], tail(1))
-        turn(1)
-        weave(n0[6:], marks("FV", "VV", "RT", rc + 12, t, 1) + marks("FV", "VV", "RT", rc + 12, t, 0))
-        keyA(0); keyM(0)
-        act(B("Rv"), I(B("NT"), vl))
-        act(B("Sv"), I(B("ST"), vl))
-        if t > 0:
-            act(B("OWN", zc, zc + 192), B("OWN", 0, 192), bias=-512.0 * t)
-        else:
-            consts_s()
-        share(1)
-        act(B("G0"), I(B("FV"), vl), bias=1.0)
-        weave(tail(0), dedupe(1, RB[1], 0, B("OT", rc + 6, rc + 12), B("OT", rc + 24, rc + 36, 2)))
-        turn(0)
-        share(0)
-        zproc(1)
-        sent += out("Zz", "ZO", 192, 96, 192, "aZ1")
-        m1 = marks("FF", "VAL", "OT", rc + 12, t, 1)
-        weave(m1[:3], [lambda c=c: ts(W("FC", 8 * c, 8 * c + 8), W("WT%d" % c, 8, 16), 0.0, None, A.is_equal) for c in (0, 1)])
-        weave(dedupe(0, RB[0], 0, B("OT", rc, rc + 6), B("OT", rc + 12, rc + 24, 2)), m1[3:])
-        sent += out("MM", "MO", 384, 0, 384, "aM")
-        sent += out("RT", "OT", 40, 0, 36, "aL")
-        act(B("Rf"), I(B("NT"), fl))
-        act(B("Sf"), I(B("ST"), fl))
-        weave(marks("FF", "VAL", "OT", rc + 12, t, 0), [lambda: tt(B("pre"), I(B("FV"), fl), B("G0"), A.min)])
-        vr, fr = B("MM", mc, mc + 192), B("MO", mc, mc + 192)
-        for h, (own, oth, new) in enumerate((("Rv", "Rf", fr), ("Rf", "Rv", vr))):
-            o = B("pb0", 192 * h, 192 * h + 192)
-            mm(o, B("DO"), B(own), True, False)
-            mm(o, B("D15"), new, False, False)
-            mm(o, B("DE"), B(oth), False, True)
-        act(B("NNs"), B("pb0", 0, 384))
-        for h, (own, oth) in enumerate((("Sv", "Sf"), ("Sf", "Sv"))):
-            o = B("pb2", 192 * h, 192 * h + 192)
-            mm(o, B("DOb"), B(own), True, False)
-            mm(o, B("DEb"), B(oth), False, True)
-        act(B("NSs"), B("pb2", 0, 384), F.Identity, bias=B("BT", t, t + 1))
-        tt(B("ma"), I(B("FF"), vl), B("pre"), A.min)
-        tt(B("mb"), I(B("FF"), fl), B("ma"), A.min)
-        tt(B("nd"), B("mb"), B("OWN", zc, zc + 192), A.is_lt)
-        scan(B("ns"), B("SEG"), B("nd"), 0.0, A.mult, A.max)
-        nl = B("ns", 15, 192, 16)
-        tt(B("nT", 0, 12), nl, B("TR", 0, 12), A.mult)
-        tt(B("nT", 12, 24), nl, B("TR", 12, 24), A.mult)
-        tt(B("nP", 0, 12), B("nT", 0, 12), B("vlf"), A.max)
-        tt(B("nP", 12, 24), B("nT", 12, 24), B("FL", 15, 192, 16), A.max)
-        cp(B("POS"), B("nP"))
-        held = [lambda: scat(B("ST"), B("POS"), B("NSs"))]
+            act(col("Rv", c), I(ET, lst("RT", t, c)))
+            pick(c); newer(c)
+        marks("S", "VV", 192 * t, "RT", t, 1); marks("S", "VV", 192 * t, "RT", t, 0)
+        records("S", RV, NA); records("V", 0, RV); records("S", NA, 192 - RW); records("V", 192 - RW, 192)
         if last:
-            held[0]()
-        scat(B("NT"), B("POS"), B("NNs"))
-        zproc(0)
+            ysum(0, "pb7"); ysum(1, "pb7")
+        hash_(); upper(0); sizes(1)
+        if last:
+            ysum(2, "pb5"); ysum(3, "pb5")
+        for c in (0, 1):
+            least(c); turn(c); dedupe(c, "OT", t)
+            if not last:
+                sent += K["send"](core, nxt, topo, lst("RT", t + 1, c, 0, 24), lst("OT", t, c, 0, 24), "aL%d%d" % (c, t + 1))
+            zproc(c)
+            if not last:
+                sent += K["send"](core, nxt, topo, msg("MM", t + 1, c, 0, 3), msg("MO", t, c, 0, 3), "aM%d%d" % (c, t + 1))
+            meetings(c)
         if not last:
-            sent += out("Zz", "ZO", 192, 0, 96, "aZ0")
-            mm(W("pb3", 480, 496), W("ones", 0, 96), W("FC"))
+            for c in (0, 1):
+                act(W(c, "FC", 8 * c, 8 * c + 8), W(c, "WS%d" % c, 8, 16), F.Relu, scale=-1.0, bias=B0 - 2047, total=W(c, "FA", c, c + 1))
+            for c in (0, 1):
+                mm(B("pb6", 272, 273), W(c, "C32"), W(c, "FA", c, c + 1), c == 0, c == 1)
 
-    mc = 384 * (HOPS - 1)
-    mm(B("pb7", 256, 448), B("ID"), B("MO", mc, mc + 192), True, False)
-    mm(B("pb7", 256, 448), B("I2K"), B("MO", mc + 192, mc + 384), False, True)
-    YB = ("pb2", "pb5", "pb4", "pb0")
-    for j in range(4):
-        mm(B(YB[j], 0, 512, 1, 0, 8), B("YWs"), B("ST", 512 * j, 512 * j + 512), True, False)
-    for i in range(16):
-        act(B("YP", 15 - i, 192, 16), B("pb7", 256 + i, 448, 16))
+    t = HOPS - 1
+    dma("Y", "st2", T.ys[:], T.YS[0:128:16, SP:SP + 2048], [], [B("YS")])
+    act(B("YZ"), I(B("ZL"), B("LP")))
+    dma("S", "st0", T.yz[:], T.YZ[:], [], [B("YZ")])
+    for c in (0, 1):
+        mm(col("pb5", c), B("ID"), msg("MO", t, c, 0), True, False)
+        mm(col("pb5", c), B("I2K"), msg("MO", t, c, 1), False, True)
+    act(B("YQ"), B("pb5", 0, 192), bias=-2048 * T0)
+    act(B("YP"), I(B("YQ"), B("LP")))
     dma("Y", "st1", T.yp[:], T.YP[0:128:16, :], [], [B("YP")])
-    for j in range(4):
-        a, b = 512 * j, 512 * j + 512
-        if j % 2:
-            act(B("NTh", a, b), B("NT", a, b))
-        else:
-            cp(B("NTh", a, b), B("NT", a, b))
-    for j in range(4):
-        mm(B(YB[j], 0, 512, 1, 0, 8), B("YWn"), B("NTh", 512 * j, 512 * j + 512), False, True)
-    for j in range(4):
-        a, b = 512 * j, 512 * j + 512
-        o = B(YB[j], 0, 512, 1, 0, 8)
-        if j % 2:
-            act(B("YS", a, b, 1, 0, 8), o)
-        else:
-            cp(B("YS", a, b, 1, 0, 8), o)
-    dma("Y", "st2", T.ys[:], T.YS[0:8, :], [], [B("YS")])
-    for i in range(16):
-        act(B("YZ", 15 - i, 192, 16), B("pb1", 192 + i, 384, 16))
-    dma("Y", "st0", T.yz[:], T.YZ[:], [], [B("YZ")])
 
+    K["issue"]()
     for q in ("V", "S", "P", "G"):
         g.wait_ge(T.sem["c" + q], K["cnt"][q])
     for j in range(8):

@@ -1,23 +1,27 @@
+import math
 from concourse.mybir import AluOpType as A, ActivationFunctionType as F
 
 HOPS = 5
 NA = 128
 CHUNK = ((0, NA), (NA, 192 - NA))
+WD = 4
 PC = 64
 EV, RV, RW = 64, 64, 0
-MQ = "SS"
-ONS = ("av", "sb", "Ax")
-DB = ("pb7", "pb7")
+MQ = "SV"
+ONS = ("av",)
+DB = ("pb7", "pb5")
+KS = (0, 4)
 SP = 384
 B0 = 2.0 ** 18 + 4096
 T0 = B0 / 2048 + 1
+B1 = B0 + 4096
 U = 2.0 ** 19
-PE, GATHER, SCATTER, FIX, OWN, CROSS, LAG, FAR = 0.6, 1.5, 3.5, 30, 60, 100, 1800, 2800
-SLACK, ROUNDS = 0, 4
+PE, GATHER, SCATTER, FIX, OWN, CROSS, LAG, FAR = 0.72, 1.5, 3.5, 48, 145, 300, 2200, 3500
+ROUNDS = 3
 f4, f2, b2, i4, u2 = "float32", "float16", "bfloat16", "int32", "uint16"
 SCRATCH = {}
-OWNBUF = ("enS", "ET", "YS", "XS", "FT", "YP", "YQ", "YZ", "ZL", "v0s", "v0f", "z0s", "wts", "X", "M", "R", "MX", "VAL", "VV", "MM", "MO",
-          "RT", "OT", "RL", "AL", "POS", "NN", "PRE", "LP", "LC")
+OWNBUF = ("enS", "ET", "YS", "XS", "FT", "FU", "YP", "YQ", "YZ", "ZL", "v0s", "v0f", "z0s", "wts", "X", "M", "R", "MX", "AB", "VAL", "VV", "MM", "MO",
+          "RT", "OT", "RL", "AL", "POS", "NN", "PRE", "LP", "LC", "fin0", "fin1")
 PLACE = {}
 
 
@@ -37,7 +41,7 @@ for n_, w_, t_ in (
         ("YP", 192, f4), ("YQ", 192, f4), ("YZ", 192, b2), ("ZL", 192, b2),
         ("v0s", 12, i4), ("v0f", 16, f4), ("z0s", 192, b2), ("wts", 1, i4), ("wtf", 1, f4), ("LP", 12, u2), ("LC", 12, u2),
         ("ones", 128, f2), ("onef", 128, f4), ("oneb", 192, b2), ("ID", 128, f2), ("NID", 128, f2), ("N64", 128, f2), ("I2K", 128, f2),
-        ("I4K", 128, f2), ("IDb", 128, b2), ("I37", 128, b2), ("ITH", 128, b2), ("BDt", 128, f2), ("BD", 128, f2), ("GBt", 8, f4), ("GB", 8, f4),
+        ("I4K", 128, f2), ("IDb", 128, b2), ("I37", 128, b2), ("I4b", 128, b2), ("CT", 1280, b2), ("GV", 128, f4), ("FU", 2064, f4), ("BDt", 128, f2), ("BD", 128, f2), ("GBt", 8, f4), ("GB", 8, f4),
         ("SEL", 128, f4), ("WNa", 128, b2), ("WNb", 128, b2), ("WN", 128, b2), ("WX", 8, b2), ("WR", 8, b2), ("WA", 8, b2), ("WD", 8, f2), ("C32", 128, f4),
         ("qI", 1, i4), ("qJ", 1, i4), ("qK", 1, i4), ("qi", 1, f4), ("qr", 1, f4), ("qe", 1, f4), ("q15", 1, f4), ("qo", 1, f4), ("qs1", 1, f4),
         ("w1", 1, f4), ("qa", 1, f4), ("qb", 1, f4), ("qy15", 1, f4), ("qp", 1, f4), ("qh", 1, f4), ("SCq", 1, f4), ("BIq", 1, f4),
@@ -45,7 +49,7 @@ for n_, w_, t_ in (
         ("RST", 128, f4), ("HOLD", 128, f4), ("RSP", 256, f4), ("RSi", 16, f4),
         ("DO", 128, f4), ("DE", 128, f4), ("D15", 128, f2), ("YO", 128, f4), ("YE", 128, f4), ("Y15", 128, f2), ("YW", 128, f4), ("BT", 5, f4),
         ("GF", 128, f2), ("GT", 128, f2), ("LM", 192, f2),
-        ("RI", 192, i4), ("RJ", 192, i4), ("RL", 192, u2), ("X", 3072, f4), ("M", 3072, b2), ("R", 3072, b2), ("MX", 3072, b2), ("AL", 192, u2),
+        ("RI", 192, i4), ("RJ", 192, i4), ("RL", 192, u2), ("X", 3072, f4), ("M", 3072, b2), ("R", 3072, b2), ("MX", 3072, b2), ("AB", 3072, b2), ("WZt", 128, b2), ("WZ0", 128, b2), ("WZ1", 128, b2), ("AL", 192, u2),
         ("PEN", 192, b2), ("ui", 16, i4), ("ua", 16, i4), ("ub", 16, f4), ("uc", 16, f4), ("ud", 16, i4), ("ue", 16, i4), ("ff", 16, f4),
         ("Ax", 1, b2), ("Ay", 1, f4), ("FC", 16, f4), ("FA", 2, f4), ("TPs", 192, f2), ("Rv", 192, f4), ("Rf", 192, f4), ("PRE", 192, f4),
         ("av", 192, f2), ("af", 192, f2), ("POS", 24, u2), ("NN", 384, f4), ("XF", 192, f2), ("R1", 192, f2),
@@ -53,7 +57,7 @@ for n_, w_, t_ in (
     declare(n_, w_, t_)
 for c_ in (0, 1):
     for n_, w_, t_ in (("sb", 128, b2), ("nm", 128, f2), ("Mn", 128, f4), ("dd", 128, f4), ("ee", 128, f4), ("oo", 128, f4), ("t1", 8, f4), ("t2", 8, f4),
-                       ("fin", 8, f4), ("WF", 16, f2), ("WS", 16, b2), ("FL", 128, f4), ("ne", 128, f4), ("dup", 128, f4), ("ys", 256, f4)):
+                       ("fin", 8, f4), ("WF", 128, f2), ("WS", 128, b2), ("FL", 128, f4), ("ne", 128, f4), ("dup", 128, f4), ("ys", 256, f4)):
         declare(n_ + str(c_), w_, t_)
 for b_ in range(8):
     SCRATCH["pb%d" % b_] = ("psum", [128, 512], f4)
@@ -64,7 +68,7 @@ ORDER = []
 
 
 def meet(x, y):
-    return x[1] < y[2] and y[1] < x[2] and not (x[3] == y[3] and (x[1] - y[1]) % x[3])
+    return x[1] < y[2] and y[1] < x[2] and not (x[1] - y[1]) % math.gcd(x[3], y[3])
 
 
 def covers(x, y):
@@ -254,21 +258,47 @@ def order(plan):
     for i in range(n):
         for j, d in pred[i].items():
             succ[j][i] = d
-    banks = [{r[0] for r in x[3] + x[4] if r[0].startswith("pb")} for x in plan]
+    banks = [sorted({r[0] for r in x[3] + x[4] if r[0].startswith("pb")}) for x in plan]
 
     def lay(pred, succ, urge, head, tail):
+        left = [len(p) for p in pred]
+        ready = {i for i in range(n) if not left[i]}
+        end, taken, out = [0] * n, {}, []
+        while ready:
+            i = max(ready, key=lambda j: urge[j])
+            q, cost = plan[i][:2]
+            s = max([head[i]] + [end[j] + d for j, d in pred[i].items()])
+            moved = True
+            while moved:
+                moved = False
+                for r in [q] + banks[i]:
+                    for (a, b, o) in taken.get(r, ()):
+                        gap = 0 if r == q else CROSS if o != q else None
+                        if gap is not None and a - gap < s + cost and s < b + gap:
+                            s, moved = b + gap, True
+            end[i] = s + cost
+            for r in [q] + banks[i]:
+                taken[r] = sorted(taken.get(r, []) + [(s, end[i], q)])
+            ready.remove(i)
+            out.append(i)
+            for k in succ[i]:
+                left[k] -= 1
+                if not left[k]:
+                    ready.add(k)
+        place = {i: x for x, i in enumerate(out)}
+        return max(end[i] + tail[i] for i in range(n)), sorted(out, key=lambda i: (end[i] - plan[i][1], place[i])), end
+
+    def run(pred, succ, urge, head, tail):
         left = [len(p) for p in pred]
         ready = {i: head[i] for i in range(n) if not left[i]}
         free, end, used, out = {}, [0] * n, {}, []
         while ready:
             st = {i: max([free.get(plan[i][0], 0), s] + [e + CROSS for b in banks[i] for r, e in used.get(b, {}).items() if r != plan[i][0]])
                   for i, s in ready.items()}
-            first = min(st, key=lambda i: (st[i], -urge[i]))
-            q = plan[first][0]
-            i = max((j for j in st if plan[j][0] == q and st[j] <= st[first] + min(SLACK, plan[first][1])), key=lambda j: urge[j])
-            end[i] = free[q] = st[i] + plan[i][1]
+            i = min(st, key=lambda i: (st[i], -urge[i]))
+            end[i] = free[plan[i][0]] = st[i] + plan[i][1]
             for b in banks[i]:
-                used.setdefault(b, {})[q] = end[i]
+                used.setdefault(b, {})[plan[i][0]] = end[i]
             del ready[i]
             out.append(i)
             for k in succ[i]:
@@ -278,10 +308,10 @@ def order(plan):
         return max(end[i] + tail[i] for i in range(n)), out, end
 
     none, lag = [0] * n, [x[2] for x in plan]
-    best = run = lay(pred, succ, [-i for i in range(n)], none, lag)
+    best = run(pred, succ, [-i for i in range(n)], none, lag)
     for _ in range(ROUNDS):
-        run = lay(pred, succ, lay(succ, pred, run[2], lag, none)[2], none, lag)
-        best = min(best, run)
+        for f in (run, lay):
+            best = min(best, f(pred, succ, f(succ, pred, best[2], lag, none)[2], none, lag))
     return best[1]
 
 
@@ -294,7 +324,7 @@ def rank_program(g, core, T, topo):
         "B", "I", "tt", "ts", "cp", "scat", "scan", "fill", "act", "mm", "iota", "asel", "dma"))
     nxt = T.cores[(rank + 3) % len(T.cores)]
     prv_eng = len(topo.engines(T.cores[(rank + 1) % len(T.cores)], core))
-    ET, FT, XS = B("ET", SP, SP + 2048), B("FT", 16, 2064), B("XS")
+    ET, FT, FU, XS = B("ET", SP, SP + 2048), B("FT", 16, 2064), B("FU", 16, 2064), B("XS")
 
     def lin(name, o, a, scale, bias):
         if name in ONS:
@@ -333,10 +363,10 @@ def rank_program(g, core, T, topo):
         scan(dup, ne, col("pb7", c, 1), 0.0, A.mult, A.max)
         ts(B(buf, 64 * t + 32 * c + 8, 64 * t + 32 * c + 8 + n // 8, 2), B("dup" + s, 15, n, 16), B("qi"), None, A.max)
 
-    def marks(q, val, v0, buf, t, c):
+    def marks(q, tab, val, v0, buf, t, c):
         p0, n = CHUNK[c]
         for b in range(n // 16 - 1, -1, -1):
-            scat(q, B("FT"), lst(buf, t, c, 8 + 2 * b, 9 + 2 * b), B(val, v0 + p0 + 16 * b, v0 + p0 + 16 * b + 16))
+            scat(q, B(tab), lst(buf, t, c, 8 + 2 * b, 9 + 2 * b), B(val, v0 + p0 + 16 * b, v0 + p0 + 16 * b + 16))
 
     dma("Y", "ld0", T.v0s[:], T.v0[:], [B("v0s")], [])
     QW = 512
@@ -344,23 +374,26 @@ def rank_program(g, core, T, topo):
         dma("Y", "ld%d" % (3 + j), T.enS[:, j * QW:(j + 1) * QW], T.en[:, j * QW:(j + 1) * QW], [B("enS", j * QW, (j + 1) * QW)], [])
     dma("S", "ld1", T.z0s[:], T.z0[:], [B("z0s")], [])
     dma("S", "ld2", T.wts[:], T.wt[:], [B("wts")], [])
-    dma("S", "ld7", T.XS[:], T.xs[:], [B("XS")], [])
+    dma("Y", "ld7", T.XS[:], T.xs[:], [B("XS")], [])
 
     for n, v in (("ones", 1.0), ("onef", 1.0), ("HOLD", 0.0), ("CB", 16.0), ("v0f", 0.0), ("OT", 0), ("WNa", -128 * U), ("RST", -1.0e20),
-                 ("RSP", 1.0e6), ("C32", 32.0), ("WF0", 0.0), ("WF1", 0.0), ("WS0", 0.0), ("WS1", 0.0)):
+                 ("RSP", 1.0e6), ("C32", 32.0), ("fin0", 0.0), ("fin1", 0.0)):
         fill(B(n), v)
-    fill(B("HOLD", 0, 128, 16), -8192.0); fill(B("RST", 0, 128, 16), 1.0e20); fill(B("pb6", 256, 272), 0.0); fill(B("RT", 0, 64), 0)
+    fill(B("HOLD", 0, 128, 16), -8192.0); fill(B("RST", 0, 128, 16), 1.0e20); fill(B("pb6", 192, 208), 0.0); fill(B("RT", 0, 64), 0)
     iota(B("qI"), [[0, 1]], 0, 1, True)
     iota(B("CI"), [[0, 16], [1, 16]], 0, 0)
     iota(B("LI"), [[1, 12]], 0, 0)
     iota(B("RSi"), [[-16, 16]], -16, 0)
     for j in range(4):
-        iota(B("FT", 516 * j, 516 * j + 516), [[0, 516]], 9999, 0)
+        iota(B("FT", 516 * j, 516 * j + 516), [[0, 516]], 2048, 0)
+        iota(B("FU", 516 * j, 516 * j + 516), [[0, 516]], 2048, 0)
     for t in range(HOPS):
-        iota(B("VV", 192 * t, 192 * t + 192), [[32, 12], [-2, 16]], 4096 - 512 * t + 29, 0)
-        iota(B("VAL", 192 * t, 192 * t + 192), [[32, 12], [-2, 16]], 4096 - 512 * t + 30, 0)
+        iota(B("VV", 192 * t, 192 * t + 192), [[32, 12], [-2, 16]], 1664 - 384 * t + 29, 0)
+        iota(B("VAL", 192 * t, 192 * t + 192), [[32, 12], [-2, 16]], 1664 - 384 * t + 30, 0)
+        if t > 0:
+            iota(B("CT", 256 * t, 256 * t + 256), [[0, 256]], 768 * t, 0)
     for c in (0, 1):
-        iota(col("CKt", c, 2), [[0, 2], [-64, CHUNK[c][1] // 16], [4, 16]], -2202 - 60 - 4 * CHUNK[c][0], 0)
+        iota(col("CKt", c, 2), [[0, 2], [-64, CHUNK[c][1] // 16], [4, 16]], -2 * 1664 - 62 - 4 * CHUNK[c][0], 0)
     asel(B("BDt"), B("ones"), [[-16, 8], [0, 16]], A.is_ge, 0.0, 0, 1)
     asel(B("BD"), B("BDt"), [[16, 8], [0, 16]], A.is_ge, 0.0, 15, -1)
     asel(B("ID"), B("ones"), [[-1, 128]], A.is_equal, 0.0, 0, 1)
@@ -370,16 +403,12 @@ def rank_program(g, core, T, topo):
     asel(B("WNb"), B("WNa"), [[0, 16], [-16, 8]], A.is_ge, 0.0, 0, 1)
     asel(B("WNa"), B("WNb"), [[0, 16], [16, 8]], A.is_ge, 0.0, 15, -1)
     asel(B("WN"), B("WNa"), [[-1, 16], [-16, 8]], A.not_equal, -65536 * U, 0, 1)
-    asel(B("GF", 0, 128, 1, 0, 16), B("ones", 0, 128, 1, 0, 16), [[-1, 8], [0, 16]], A.is_equal, 0.0, 0, 1)
-    asel(B("GT", 0, 128, 1, 0, 16), B("ones", 0, 128, 1, 0, 16), [[-1, 8], [0, 16]], A.is_equal, 0.0, -8, 1)
-    ts(B("qJ"), B("qI"), 15, None, A.bitwise_and); cp(B("qi"), B("qJ")); cp(B("qp"), B("qI")); cp(B("wtf"), B("wts"))
+    ts(B("qJ"), B("qI"), 15, None, A.bitwise_and); cp(B("qi"), B("qJ")); cp(B("wtf"), B("wts"))
     ts(B("qK"), B("qJ"), 1, None, A.bitwise_and)
     ts(B("qr"), B("qi"), -1.0, 15.0, A.mult, A.add)
     ts(B("qa"), B("qi"), -15.5 - T0, None, A.add); ts(B("qb"), B("qi"), 2.0 ** -18, None, A.mult)
     ts(B("q15"), B("qi"), 15.0, None, A.is_equal); ts(B("qe"), B("qK"), -1.0, 1.0, A.mult, A.add)
     tt(B("w1"), B("qe"), B("q15"), A.add); ts(B("qo"), B("w1"), -1.0, 1.0, A.mult, A.add)
-    ts(B("qh"), B("qp"), 8.0, None, A.is_ge)
-    ts(B("SCq"), B("qh"), 1.0 / 2048 - 1.0, 1.0, A.mult, A.add); ts(B("BIq"), B("qh"), -B0 / 2048, None, A.mult)
     ts(B("EQD"), B("CI"), B("qi"), None, A.is_equal); ts(B("EQR"), B("CI", 0, 192), B("qr"), None, A.is_equal)
     cp(B("LC"), B("LI")); ts(B("LP"), B("LI"), 16.0, B("qr"), A.mult, A.add)
     ts(B("RSP", 0, 256, 16), B("RSi"), B("qi"), None, A.add)
@@ -387,11 +416,15 @@ def rank_program(g, core, T, topo):
     for c in (0, 1):
         act(col("CB", c, 1), B("EQD", 0, CHUNK[c][1]), scale=4096.0, bias=-4080.0)
         tt(col("CK", c, 2), col("CKt", c, 2), B("CKu", 0, 2 * CHUNK[c][1]), A.add)
-    for n, v in (("I2K", 2048.0), ("I37", 2.0 ** 18 * U), ("IDb", 1.0), ("NID", -1.0), ("N64", -64.0), ("I4K", 4096.0),
+    for n, v in (("I2K", 2048.0), ("I37", 2.0 ** 18 * U), ("IDb", 1.0), ("NID", -1.0), ("N64", -64.0), ("I4K", 4096.0), ("I4b", 4096.0),
                  ("DE", B("qe")), ("DO", B("qo")), ("D15", B("q15"))):
         act(B(n), B("ID"), scale=v)
     for n, v in (("WX", 32 * U), ("WR", -16 * U), ("WA", 16 * U), ("WD", B("wtf"))):
         act(B(n), B("GB"), scale=v)
+    for c in (0, 1):
+        if 0 < KS[c] < 16 // WD:
+            act(B("WZt"), B("BD"), scale=16 * U)
+            asel(B("WZ%d" % c), B("WZt"), [[0, 8 * WD], [-1, 16 // WD]], A.is_ge, 0.0, KS[c] - 1, 0)
     for t in range(HOPS - 1):
         act(B("BT", t, t + 1), B("q15"), scale=2048.0 * (9 + t))
     act(B("qs1"), B("qi"), bias=1.0); act(B("qy15"), B("q15"), scale=16.0)
@@ -422,8 +455,8 @@ def rank_program(g, core, T, topo):
         def W(c, n, a=0, b=128, st=1):
             return B(n, a, b, st, 0, CHUNK[c][1])
 
-        def bc(name, c, k):
-            return B(name, 16 * CHUNK[c][0] + k, 16 * (CHUNK[c][0] + CHUNK[c][1]), 16)
+        def bc(name, c, k, st=16):
+            return B(name, 16 * CHUNK[c][0] + k, 16 * (CHUNK[c][0] + CHUNK[c][1]), st)
 
         def ring(c):
             cp(col("RI", c), I(ET, lst("RT", t, c)))
@@ -454,52 +487,65 @@ def rank_program(g, core, T, topo):
 
         def newer(c):
             kk = "pb%d" % (2 + c)
-            mm(col("pb4", c), B("I2K"), msg("MM", t, c, 1))
+            bk, a, b = ("pb4", 0, WD * NA) if c == 0 else ("pb6", 256, 256 + WD * (192 - NA))
+            if t > 0:
+                for m in range(WD):
+                    mm(B(bk, a + m, b, WD), B("I2K"), msg("MM", t, c, 1))
             ts(col("PEN", c), msg("MM", t, c, 1), B("qa"), B("qb"), A.add, A.max)
             mm(W(c, kk), col("PEN", c), B("I37"), True, False)
-            for k in range(16):
-                tt(bc("M", c, k), bc("X", c, k), col("pb4", c), A.is_ge)
-                i = (k + t) % 16
-                mm(W(c, kk, k, 128, 16), bc("M", c, k), B("WN", 8 * i, 8 * i + 8), False, False)
-
-        def upper(c):
-            kk = "pb%d" % (2 + c)
-            mm(col("pb5", c), B("ID"), msg("MM", t, c, 2))
-            for k in range(16):
-                mm(W(c, kk, k, 128, 16), bc("R", c, k), B("WR"), False, False)
-            for k in range(16):
-                tt(bc("MX", c, k), bc("R", c, k), col("pb5", c), A.max)
-                mm(W(c, kk, k, 128, 16), bc("MX", c, k), B("WX"), False, k == 15)
+            for j in range(16 // WD):
+                if t > 0:
+                    tt(bc("M", c, j, 16 // WD), bc("X", c, j, 16 // WD), B(bk, a, b), A.is_ge)
+                else:
+                    ts(bc("M", c, j, 16 // WD), bc("X", c, j, 16 // WD), 2048 * T0, None, A.is_ge)
+                for k in range(j, 16, 16 // WD):
+                    i = (k + t) % 16
+                    mm(W(c, kk, k, 128, 16), bc("M", c, k), B("WN", 8 * i, 8 * i + 8), False, False)
 
         def sizes(c):
             p0, n = CHUNK[c]
-            m = 512 // n
-            for k0 in range(0, 16, m):
-                bk = DB[k0 // m % 2]
-                ks = range(k0, min(16, k0 + m))
-                for k in ks:
-                    o = B(bk, (k - k0) * n, (k - k0) * n + n)
-                    mm(o, B("NID"), msg("MM", t, c, 2), True, False)
-                    mm(o, B("IDb"), bc("R", c, k), False, True)
-                act(B("MX", 16 * p0 + k0 * n, 16 * p0 + (k0 + len(ks)) * n), B(bk, 0, len(ks) * n), F.Abs)
-                for k in ks:
-                    mm(W(c, "pb%d" % (2 + c), k, 128, 16), B("MX", 16 * p0 + k * n, 16 * p0 + k * n + n), B("WA"), False, k == 15)
+            kk, J, z = "pb%d" % (2 + c), 16 // WD, msg("MM", t, c, 2)
+            bk, a = ("pb4", 0) if c == 0 else ("pb6", 256)
+            ks, m, sums = [k for k in range(16) if k % J < KS[c]], 512 // n, []
+            if 0 < KS[c] < J:
+                mm(W(c, kk), z, B("WZ%d" % c), False, False)
+            if KS[c] < J:
+                for j in range(WD):
+                    mm(B(bk, a + j, a + WD * n, WD), B("ID"), z)
+            for k in range(16):
+                if k not in ks:
+                    mm(W(c, kk, k, 128, 16), bc("R", c, k), B("WR"), False, False)
+            for x in range(max(J - KS[c], -(-len(ks) // m))):
+                part, db = ks[m * x:m * x + m], DB[(x + c * KS[0]) % 2]
+                for j, k in enumerate(part):
+                    mm(B(db, j * n, j * n + n), B("NID"), z, j == 0, False)
+                for j, k in enumerate(part):
+                    mm(B(db, j * n, j * n + n), B("IDb"), bc("R", c, k), False, k == part[-1])
+                o = 16 * p0 + m * x * n
+                if part:
+                    act(B("AB", o, o + len(part) * n), B(db, 0, len(part) * n), F.Abs)
+                if KS[c] + x < J:
+                    tt(bc("MX", c, KS[c] + x, J), bc("R", c, KS[c] + x, J), B(bk, a, a + WD * n), A.max)
+                    sums += [(k, bc("MX", c, k), "WX") for k in range(KS[c] + x, 16, J)]
+                sums += [(k, B("AB", o + j * n, o + j * n + n), "WA") for j, k in enumerate(part)]
+            for k, d, w in sums:
+                mm(W(c, kk, k, 128, 16), d, B(w), False, k == sums[-1][0])
 
         def hash_():
             for c in (0, 1):
-                mm(W(c, "pb6", 256 + 8 * c, 264 + 8 * c), msg("MM", t, c, 2), B("WD"))
-            cp(B("ui"), B("pb6", 256, 272))
+                mm(W(c, "pb6", 192 + 8 * c, 200 + 8 * c), msg("MM", t, c, 2), B("WD"))
+            cp(B("ui"), B("pb6", 192, 208))
             ts(B("ua"), B("ui"), 2047, None, A.bitwise_and)
             ts(B("ub"), B("ua"), 1184.0, None, A.add)
             tt(B("uc"), B("ua"), B("ub"), A.mult)
             if t > 0:
-                act(B("Ax"), B("pb6", 272, 273), scale=-1.0, bias=4080 - 17 * 65536.0)
-                act(B("Ay"), B("pb6", 272, 273), F.Identity, bias=B("Ax"))
+                act(B("Ax"), B("pb6", 208, 209), scale=-1.0, bias=4080 - 17 * 65536.0)
+                act(B("Ay"), B("pb6", 208, 209), F.Identity, bias=B("Ax"))
                 ts(B("ud"), B("uc"), B("Ay"), None, A.add)
             else:
                 cp(B("ud"), B("uc"))
             ts(B("ue"), B("ud"), 5, 2047, A.arith_shift_right, A.bitwise_and)
-            ts(B("ff"), B("ue"), B0 - 2048, None, A.add)
+            ts(B("ff"), B("ue"), -B1, None, A.add)
 
         def least(c):
             s = str(c)
@@ -513,21 +559,17 @@ def rank_program(g, core, T, topo):
             tt(t2, t1, W(c, "ff", 8 * c, 8 * c + 8), A.max)
             scan(oo, dd, ee, 0.0, A.min, A.max)
             tt(fin, W(c, "oo" + s, 15, 128, 16), t2, A.min)
-            lin("WS", W(c, "WS" + s, 8, 16), fin, 1.0, -1023.5)
-            tt(W(c, "WF" + s, 0, 8), fin, W(c, "WS" + s, 8, 16), A.subtract)
+            wide = I(B("fin" + s), B("LC", 0, 8))
+            lin("WS", B("WS" + s), wide, 1.0, -1023.5)
+            tt(B("WF" + s), wide, B("WS" + s), A.subtract)
 
         def turn(c):
-            p0, n = CHUNK[c]
-            q = B("pb6", 288 + p0, 288 + p0 + n, 1, 0, 16)
-            tp = B("TPs", p0, p0 + n, 1, 0, 16)
-            mm(q, W(c, "WS%d" % c, 0, 16), W(c, "IDb", 0, n), True, False)
-            mm(q, W(c, "WF%d" % c, 0, 16), W(c, "ID", 0, n), False, True)
-            act(tp, q, F.Relu, scale=B("SCq", 0, 1, 1, 0, 16), bias=B("BIq", 0, 1, 1, 0, 16))
-            spread(c, B("GF", 0, 128, 1, 0, 16), tp)
-            mm(B("pb4", 0, n), B("GF", 0, 128, 1, 0, 16), tp)
-            mm(B("pb4", n, 2 * n), B("GT", 0, 128, 1, 0, 16), tp)
+            n = CHUNK[c][1]
+            spread(c, W(c, "WF%d" % c), W(c, "ID", 0, n))
+            mm(B("pb4", 0, n), W(c, "WF%d" % c), W(c, "ID", 0, n))
+            mm(B("pb4", n, 2 * n), W(c, "WS%d" % c), W(c, "IDb", 0, n))
             act(msg("MO", t, c, 0), B("pb4", 0, n))
-            act(msg("MO", t, c, 1), B("pb4", n, 2 * n), bias=T0)
+            act(msg("MO", t, c, 1), B("pb4", n, 2 * n), F.Abs, scale=1.0 / 2048, bias=1.0)
 
         def zproc(c):
             n = CHUNK[c][1]
@@ -545,7 +587,6 @@ def rank_program(g, core, T, topo):
             y, ys, pos = "pb%d" % (2 + c), "ys%d" % c, B("POS", p0 // 8, (p0 + n) // 8)
             vl, fl = lst("RT", t, c), lst("OT", t, c)
             wo, we, w15 = ("YO", "YE", "Y15") if last else ("DO", "DE", "D15")
-            act(col("Rf", c), I(ET, fl))
             for h, (own, oth, new) in enumerate((("Rv", "Rf", "MO"), ("Rf", "Rv", "MM"))):
                 o = B("pb%d" % c, n * h, n * h + n)
                 mm(o, B(w15), msg(new, t, c, 0), True, False)
@@ -553,12 +594,20 @@ def rank_program(g, core, T, topo):
                     mm(o, B(w), col(r, c), False, r == "Rf")
             act(col("NN", c, 2), B("pb%d" % c, 0, 2 * n), F.Identity, bias=16 * 2048.0 * (9 + t) if last else B("BT", t, t + 1))
             tt(col("PRE", c), I(FT, fl), B("VAL", 192 * t + p0, 192 * t + p0 + n), A.min)
-            marks(MQ[c], "PRE", 0, "OT", t, c)
             mm(B(y, 0, 2 * n), B("I4K"), col("CK", c, 2), True, False)
+            if t > 0:
+                mm(B(y, 0, 2 * n), B("I4b"), B("CT", 256 * t, 256 * t + 2 * n), False, False)
             mm(B(y, 0, n), B("ID"), msg("MM", t, c, 0), False, False)
             mm(B(y, n, 2 * n), B("ID"), msg("MO", t, c, 0), False, False)
-            lin("av", col("av", c), I(FT, vl), 1.0, 1101.0 - base)
-            lin("af", col("af", c), I(FT, fl), 1.0, 1100.0 - base)
+            if c == 0:
+                marks(MQ[c], "FT", "PRE", 0, "OT", t, c)
+                lin("av", col("av", c), I(FT, vl), 1.0, 1.0)
+                lin("af", col("af", c), I(FT, fl), 1.0, 0.0)
+            else:
+                marks(MQ[c], "FU", "VAL", 192 * t, "OT", t, c)
+                act(B("GV", 0, n), I(FT, vl), bias=1.0)
+                tt(col("av", c), I(FU, vl), B("GV", 0, n), A.min)
+                tt(col("af", c), I(FU, fl), col("PRE", c), A.min)
             for a in ("av", "af"):
                 for h in (0, 1):
                     mm(B(y, h * n, h * n + n), B("I4K"), col(a, c), False, a == "af" and h == 1)
@@ -567,19 +616,21 @@ def rank_program(g, core, T, topo):
             scat("V", B("YS" if last else "ET"), pos, col("NN", c, 2))
 
         def ysum(j, bk):
-            mm(B(bk), B("YW"), B("ET", SP + 512 * j, SP + 512 * j + 512))
+            for a in range(0, 512, 128):
+                mm(B(bk, a, a + 128), B("YW"), B("ET", SP + 512 * j + a, SP + 512 * j + a + 128))
             act(B("YS", SP + 512 * j, SP + 512 * j + 512), B(bk))
 
         ring(0); ring(1)
         rings("S", EV, NA); rings("V", 0, EV); rings("S", NA, 192)
         for c in (0, 1):
             act(col("Rv", c), I(ET, lst("RT", t, c)))
-            pick(c); newer(c)
-        marks("S", "VV", 192 * t, "RT", t, 1); marks("S", "VV", 192 * t, "RT", t, 0)
+            newer(c)
+        pick(0); pick(1)
+        marks("S", "FT", "VV", 192 * t, "RT", t, 1); marks("S", "FT", "VV", 192 * t, "RT", t, 0)
         records("S", RV, NA); records("V", 0, RV); records("S", NA, 192 - RW); records("V", 192 - RW, 192)
         if last:
-            ysum(0, "pb7"); ysum(1, "pb7")
-        hash_(); upper(0); sizes(1)
+            ysum(0, "pb7"); ysum(1, "pb5")
+        hash_(); sizes(0); sizes(1)
         if last:
             ysum(2, "pb5"); ysum(3, "pb5")
         for c in (0, 1):
@@ -589,12 +640,13 @@ def rank_program(g, core, T, topo):
             zproc(c)
             if not last:
                 sent += K["send"](core, nxt, topo, msg("MM", t + 1, c, 0, 3), msg("MO", t, c, 0, 3), "aM%d%d" % (c, t + 1))
-            meetings(c)
+            act(col("Rf", c), I(ET, lst("OT", t, c)))
+        meetings(0); meetings(1)
         if not last:
             for c in (0, 1):
-                act(W(c, "FC", 8 * c, 8 * c + 8), W(c, "WS%d" % c, 8, 16), F.Relu, scale=-1.0, bias=B0 - 2047, total=W(c, "FA", c, c + 1))
+                act(W(c, "FC", 8 * c, 8 * c + 8), W(c, "WS%d" % c, 0, 128, 16), F.Relu, scale=-1.0, bias=1.0 - B1, total=W(c, "FA", c, c + 1))
             for c in (0, 1):
-                mm(B("pb6", 272, 273), W(c, "C32"), W(c, "FA", c, c + 1), c == 0, c == 1)
+                mm(B("pb6", 208, 209), W(c, "C32"), W(c, "FA", c, c + 1), c == 0, c == 1)
 
     t = HOPS - 1
     dma("Y", "st2", T.ys[:], T.YS[0:128:16, SP:SP + 2048], [], [B("YS")])

@@ -5,8 +5,12 @@ HOPS = 5
 NA = 128
 CHUNK = ((0, NA), (NA, 192 - NA))
 WD = 4
+FUSE = 0
+TB = "pb5"
 PC = 64
-EV, RV, RW = 64, 64, 0
+HALF = 2
+SPLIT = (1, 0)
+EV, RV = (32, 32, 0), (0, 32, 0)
 MQ = "SV"
 ONS = ("av",)
 DB = ("pb7", "pb5")
@@ -16,12 +20,16 @@ B0 = 2.0 ** 18 + 4096
 T0 = B0 / 2048 + 1
 B1 = B0 + 4096
 U = 2.0 ** 19
-PE, GATHER, SCATTER, FIX, OWN, CROSS, LAG, FAR = 0.72, 1.5, 3.5, 48, 145, 300, 2200, 3500
+PE, GATHER, SCATTER, FIX, OWN, CROSS, LAG, FAR = 0.72, 1.5, 3.5, 48, 145, 300, 2200, 4500
+SB = ("pb7", "pb5")
+FIRST = 3000
+YE = 1
+LW = 2
 ROUNDS = 3
 f4, f2, b2, i4, u2 = "float32", "float16", "bfloat16", "int32", "uint16"
 SCRATCH = {}
-OWNBUF = ("enS", "ET", "YS", "XS", "FT", "FU", "YP", "YQ", "YZ", "ZL", "v0s", "v0f", "z0s", "wts", "X", "M", "R", "MX", "AB", "VAL", "VV", "MM", "MO",
-          "RT", "OT", "RL", "AL", "POS", "NN", "PRE", "LP", "LC", "fin0", "fin1")
+OWNBUF = ("EF", "ZE", "D", "ET", "YS", "XS", "FT", "FU", "YP", "YQ", "YZ", "ZL", "v0s", "v0f", "z0s", "wts", "X", "M", "R", "MX", "AB", "VAL", "VV", "MM", "MO",
+          "RT", "OT", "RL", "AL", "POS", "NN", "PRE", "LP", "LC", "LD", "LE", "fin0", "fin1")
 PLACE = {}
 
 
@@ -37,16 +45,16 @@ def declare(name, w, t):
 
 
 for n_, w_, t_ in (
-        ("enS", 2048, i4), ("ET", SP + 2048, f4), ("YS", SP + 2048, f4), ("XS", 2048, b2), ("FT", 2064, f4),
+        ("EF", 2048, f4), ("ET", SP + 2048, i4), ("ZE", 3072, f2), ("D", 3072, b2), ("YS", SP + 2048, f4), ("XS", 2048, b2), ("FT", 2080, f4),
         ("YP", 192, f4), ("YQ", 192, f4), ("YZ", 192, b2), ("ZL", 192, b2),
-        ("v0s", 12, i4), ("v0f", 16, f4), ("z0s", 192, b2), ("wts", 1, i4), ("wtf", 1, f4), ("LP", 12, u2), ("LC", 12, u2),
-        ("ones", 128, f2), ("onef", 128, f4), ("oneb", 192, b2), ("ID", 128, f2), ("NID", 128, f2), ("N64", 128, f2), ("I2K", 128, f2),
-        ("I4K", 128, f2), ("IDb", 128, b2), ("I37", 128, b2), ("I4b", 128, b2), ("CT", 1280, b2), ("GV", 128, f4), ("FU", 2064, f4), ("BDt", 128, f2), ("BD", 128, f2), ("GBt", 8, f4), ("GB", 8, f4),
-        ("SEL", 128, f4), ("WNa", 128, b2), ("WNb", 128, b2), ("WN", 128, b2), ("WX", 8, b2), ("WR", 8, b2), ("WA", 8, b2), ("WD", 8, f2), ("C32", 128, f4),
+        ("v0s", 12, i4), ("v0f", 12, f4), ("z0s", 192, b2), ("wts", 1, i4), ("wtf", 1, f4), ("LP", 12, u2), ("LC", 12, u2),
+        ("onef", 128, f4), ("oneb", 192, b2), ("ID", 128, f2), ("NID", 128, f2), ("N64", 128, f2), ("I2K", 128, f2),
+        ("I4K", 128, f2), ("IDb", 128, b2), ("I37", 128, b2), ("I4b", 128, b2), ("CT", 1280, b2), ("GV", 128, f4), ("FU", 2080, f4), ("PERM", 256, f2), ("o256", 256, f2), ("CJ", 256, f4), ("EQ2", 256, f4), ("LM2", 384, f2), ("LK", 12, f4), ("LN", 24, f4), ("LD", 12, u2), ("LE", 24, u2), ("qi16", 1, f4), ("BDt", 128, f2), ("BD", 128, f2), ("GBt", 8, f4), ("GB", 8, f4),
+        ("SEL", 128, f4), ("SE2", 256, f4), ("E2t", 64, f2), ("E2", 64, f2), ("E2b", 64, b2), ("ODt", 128, f4), ("ODD", 128, b2), ("pm", 384, f4), ("sbh", 384, b2), ("nmh", 384, f2), ("WNa", 128, b2), ("WNb", 128, b2), ("WN", 128, b2), ("WX", 8, b2), ("WR", 8, b2), ("WA", 8, b2), ("WD", 8, f2), ("C32", 128, f4),
         ("qI", 1, i4), ("qJ", 1, i4), ("qK", 1, i4), ("qi", 1, f4), ("qr", 1, f4), ("qe", 1, f4), ("q15", 1, f4), ("qo", 1, f4), ("qs1", 1, f4),
         ("w1", 1, f4), ("qa", 1, f4), ("qb", 1, f4), ("qy15", 1, f4), ("qp", 1, f4), ("qh", 1, f4), ("SCq", 1, f4), ("BIq", 1, f4),
-        ("CI", 256, f4), ("EQD", 256, f4), ("EQR", 192, f4), ("LI", 12, f4), ("CKt", 384, f4), ("CKu", 256, f4), ("CK", 384, f2), ("CB", 384, f2),
-        ("RST", 128, f4), ("HOLD", 128, f4), ("RSP", 256, f4), ("RSi", 16, f4),
+        ("CI", 384, f4), ("EQD", 256, f4), ("EQR", 384, f4), ("LI", 12, f4), ("CKt", 384, f4), ("CKu", 256, f4), ("CK", 384, f2), ("CB", 768, f2),
+        ("RST", 128, f4), ("HOLD", 256, f4), ("RSP", 384, f4), ("RSi", 16, f4),
         ("DO", 128, f4), ("DE", 128, f4), ("D15", 128, f2), ("YO", 128, f4), ("YE", 128, f4), ("Y15", 128, f2), ("YW", 128, f4), ("BT", 5, f4),
         ("GF", 128, f2), ("GT", 128, f2), ("LM", 192, f2),
         ("RI", 192, i4), ("RJ", 192, i4), ("RL", 192, u2), ("X", 3072, f4), ("M", 3072, b2), ("R", 3072, b2), ("MX", 3072, b2), ("AB", 3072, b2), ("WZt", 128, b2), ("WZ0", 128, b2), ("WZ1", 128, b2), ("AL", 192, u2),
@@ -57,13 +65,13 @@ for n_, w_, t_ in (
     declare(n_, w_, t_)
 for c_ in (0, 1):
     for n_, w_, t_ in (("sb", 128, b2), ("nm", 128, f2), ("Mn", 128, f4), ("dd", 128, f4), ("ee", 128, f4), ("oo", 128, f4), ("t1", 8, f4), ("t2", 8, f4),
-                       ("fin", 8, f4), ("WF", 128, f2), ("WS", 128, b2), ("FL", 128, f4), ("ne", 128, f4), ("dup", 128, f4), ("ys", 256, f4)):
+                       ("fin", 8, f4), ("WF", 128, f2), ("WS", 128, b2), ("FL", 256, f4), ("ne", 256, f4), ("dup", 256, f4), ("ys", 256, f4)):
         declare(n_ + str(c_), w_, t_)
 for b_ in range(8):
     SCRATCH["pb%d" % b_] = ("psum", [128, 512], f4)
     PLACE["pb%d" % b_] = ("pb%d" % b_, 0, 512)
 SEMAPHORES = ["cV", "cS", "cP", "cG", "sent"] + ["ld%d" % k for k in range(8)] + ["st%d" % k for k in range(3)] + \
-    ["a%s%d" % (m, t) for m in ("L0", "L1", "M0", "M1") for t in range(1, HOPS)]
+    ["a%s%d" % (m, t) for m in ("L0", "L1", "M0", "M1", "Z0", "Z1") for t in range(1, HOPS)]
 ORDER = []
 
 
@@ -141,7 +149,7 @@ def make(g, T):
         if q == "G":
             return 150 + 2 * size(o)
         if kind == "scatter":
-            return 60 + SCATTER * size(ins[0])
+            return 60 + SCATTER * size(ins[0]) + (1600 if q == "S" and not any(x[0] == q and x[3][-1][0] == "RT" and x[4][0][0] == "FT" for x in plan if x[3]) else 0)
         if ins and len(ins[0][1]) > 1:
             return 60 + GATHER * size(o)
         if kind == "two":
@@ -205,7 +213,7 @@ def make(g, T):
             eng[q].dma_start(out, in_).then_inc(T.sem[sem], 16)
             snap[(sem, 16)] = dict(clk[q])
             note(sem, 16, reads, writes)
-        plan.append((q, 100, LAG + sum(size(x) for x in outs + ins), reads, writes, emit, None))
+        plan.append((q, 100, LAG + LW * sum(size(x) for x in outs), reads, writes, emit, None))
 
     def arrive(sem, n, b):
         def emit():
@@ -219,7 +227,7 @@ def make(g, T):
             rid, pid = topo.addr(dst, core)
             g.remote_dma(o[0], i[0], T.sem[rsem], T.sem.sent, pid, rid, topo.mask(core, dst))
         sends[rsem] = len(plan)
-        plan.append(("G", 600, FAR + 3 * size(i), i[1], [], emit, None))
+        plan.append(("G", 800 if len(sends) > 1 else FIRST, FAR + 3 * size(i), i[1], [], emit, None))
         return len(topo.engines(core, dst))
 
     def issue():
@@ -243,10 +251,11 @@ def order(plan):
                     if (w or rw) and meet(reg, old):
                         d = (0 if q == "P" else OWN) if plan[j][0] == q else CROSS
                         p[j] = max(p.get(j, 0), d + plan[j][2])
-        if q == "P":
-            if writes[0][0] in bank:
-                p.setdefault(bank[writes[0][0]], 0)
-            bank[writes[0][0]] = i
+        if q in ("P", "Y"):
+            b = writes[0][0] if q == "P" else q
+            if b in bank:
+                p.setdefault(bank[b], 0)
+            bank[b] = i
         if after is not None:
             p[after] = plan[after][2]
         pred.append(p)
@@ -308,10 +317,15 @@ def order(plan):
         return max(end[i] + tail[i] for i in range(n)), out, end
 
     none, lag = [0] * n, [x[2] for x in plan]
+    soon = {max(range(n), key=lambda i: plan[i][1] if plan[i][0] == "S" else 0)}
+    for i in range(n - 1, -1, -1):
+        if i in soon:
+            soon.update(pred[i])
     best = run(pred, succ, [-i for i in range(n)], none, lag)
     for _ in range(ROUNDS):
         for f in (run, lay):
-            best = min(best, f(pred, succ, f(succ, pred, best[2], lag, none)[2], none, lag))
+            back = f(succ, pred, best[2], lag, none)[2]
+            best = min(best, f(pred, succ, [back[i] + (max(back) if i in soon else 0) for i in range(n)], none, lag))
     return best[1]
 
 
@@ -324,7 +338,7 @@ def rank_program(g, core, T, topo):
         "B", "I", "tt", "ts", "cp", "scat", "scan", "fill", "act", "mm", "iota", "asel", "dma"))
     nxt = T.cores[(rank + 3) % len(T.cores)]
     prv_eng = len(topo.engines(T.cores[(rank + 1) % len(T.cores)], core))
-    ET, FT, FU, XS = B("ET", SP, SP + 2048), B("FT", 16, 2064), B("FU", 16, 2064), B("XS")
+    ET, FT, FU, XS = B("ET", SP, SP + 2048), B("FT", 32, 2080), B("FU", 32, 2080), B("XS")
 
     def lin(name, o, a, scale, bias):
         if name in ONS:
@@ -350,71 +364,93 @@ def rank_program(g, core, T, topo):
         return B(name, 2 * p0, 2 * p0 + 2 * n) if h == 2 else B(name, 2 * p0 + h * n, 2 * p0 + h * n + n)
 
     def spread(c, l, r):
-        mm(col("pb7", c, 2), B("ID"), col("CB", c, 2), True, False)
-        mm(col("pb7", c, 1), l, r, False, False)
-        mm(col("pb7", c, 0), l, r, False, True)
+        p0, n = CHUNK[c]
+        mm(B(SB[c], 0, 4 * n), B("ID"), B("CB", 4 * p0, 4 * p0 + 4 * n), True, False)
+        mm(B(SB[c], 2 * n, 4 * n), l, r, False, False)
+        mm(B(SB[c], 0, 2 * n), l, r, False, True)
 
     def dedupe(c, buf, t):
         n, s = CHUNK[c][1], str(c)
-        fl, ne, dup = B("FL" + s, 0, n), B("ne" + s, 0, n), B("dup" + s, 0, n)
-        scan(fl, B("HOLD", 0, n), col("pb7", c, 1), 0.0, A.add, A.max)
-        tt(ne, col("pb7", c, 0), fl, A.not_equal)
-        ts(lst(buf, t, c), B("FL" + s, 15, n, 16), -16.0, None, A.add)
-        scan(dup, ne, col("pb7", c, 1), 0.0, A.mult, A.max)
-        ts(B(buf, 64 * t + 32 * c + 8, 64 * t + 32 * c + 8 + n // 8, 2), B("dup" + s, 15, n, 16), B("qi"), None, A.max)
+        fl, ne, dup, o = B("FL" + s, 0, 2 * n), B("ne" + s, 0, 2 * n), B("dup" + s, 0, 2 * n), 64 * t + 32 * c + n // 16
+        scan(fl, B("HOLD", 0, 2 * n), B(SB[c], 2 * n, 4 * n), 0.0, A.add, A.max)
+        tt(ne, B(SB[c], 0, 2 * n), fl, A.not_equal)
+        ts(lst(buf, t, c), B("FL" + s, 31, 2 * n, 32), -32.0, None, A.add)
+        scan(dup, ne, B(SB[c], 2 * n, 4 * n), 0.0, A.mult, A.max)
+        for h in (0, 1):
+            ts(B(buf, o + h, o + n // 16, 2), B("dup" + s, 31 + 32 * h, 2 * n, 64), B(("qi", "qi16")[h]), None, A.max)
 
     def marks(q, tab, val, v0, buf, t, c):
         p0, n = CHUNK[c]
-        for b in range(n // 16 - 1, -1, -1):
-            scat(q, B(tab), lst(buf, t, c, 8 + 2 * b, 9 + 2 * b), B(val, v0 + p0 + 16 * b, v0 + p0 + 16 * b + 16))
+        for b in range(n // 32 - 1, -1, -1):
+            scat(q, B(tab), lst(buf, t, c, n // 16 + 2 * b, n // 16 + 2 * b + 2), B(val, v0 + p0 + 32 * b, v0 + p0 + 32 * b + 32))
 
     dma("Y", "ld0", T.v0s[:], T.v0[:], [B("v0s")], [])
-    QW = 512
-    for j in range(4):
-        dma("Y", "ld%d" % (3 + j), T.enS[:, j * QW:(j + 1) * QW], T.en[:, j * QW:(j + 1) * QW], [B("enS", j * QW, (j + 1) * QW)], [])
+    QW = 2048
+    for j in range(1):
+        dma("Y", "ld%d" % (3 + j), T.ET[:, SP + j * QW:SP + (j + 1) * QW], T.en[:, j * QW:(j + 1) * QW], [B("ET", SP + j * QW, SP + (j + 1) * QW)], [])
     dma("S", "ld1", T.z0s[:], T.z0[:], [B("z0s")], [])
     dma("S", "ld2", T.wts[:], T.wt[:], [B("wts")], [])
     dma("Y", "ld7", T.XS[:], T.xs[:], [B("XS")], [])
 
-    for n, v in (("ones", 1.0), ("onef", 1.0), ("HOLD", 0.0), ("CB", 16.0), ("v0f", 0.0), ("OT", 0), ("WNa", -128 * U), ("RST", -1.0e20),
-                 ("RSP", 1.0e6), ("C32", 32.0), ("fin0", 0.0), ("fin1", 0.0)):
-        fill(B(n), v)
-    fill(B("HOLD", 0, 128, 16), -8192.0); fill(B("RST", 0, 128, 16), 1.0e20); fill(B("pb6", 192, 208), 0.0); fill(B("RT", 0, 64), 0)
+    fill(B("o256"), 1.0); fill(B("onef"), 1.0); fill(B("pb6", 192, 208), 0.0)
+    for n, v in (("C32", 32.0), ("fin0", 0.0), ("fin1", 0.0), ("RST", -1.0e20), ("WNa", -128 * U), ("HOLD", 0.0)):
+        act(B(n), B("o256", 0, PLACE[n][2]), scale=v)
+    for a in (0, 192):
+        act(B("RSP", a, a + 192), B("o256", 0, 192), scale=1.0e6)
+    for c in (0, 1):
+        act(B("CB", 4 * CHUNK[c][0], 4 * CHUNK[c][0] + 2 * CHUNK[c][1]), B("o256", 0, 2 * CHUNK[c][1]), scale=32.0)
+    act(B("RST", 0, 128, 16), B("onef", 0, 8), scale=1.0e20)
+    act(B("HOLD", 0, 256, 32), B("onef", 0, 8), scale=-8192.0)
     iota(B("qI"), [[0, 1]], 0, 1, True)
-    iota(B("CI"), [[0, 16], [1, 16]], 0, 0)
+    iota(B("CI"), [[0, 24], [1, 16]], 0, 0)
     iota(B("LI"), [[1, 12]], 0, 0)
     iota(B("RSi"), [[-16, 16]], -16, 0)
     for j in range(4):
-        iota(B("FT", 516 * j, 516 * j + 516), [[0, 516]], 2048, 0)
-        iota(B("FU", 516 * j, 516 * j + 516), [[0, 516]], 2048, 0)
+        for a in (520 * j, 520 * j + 260):
+            act(B("FT", a, a + 260), B("CI", 0, 260), scale=0.0, bias=2048.0)
+        iota(B("FU", 520 * j, 520 * j + 520), [[0, 520]], 2048, 0)
+    iota(B("CJ", 0, 64), [[-100, 2], [100, 2], [1, 16]], 0, 0)
+    iota(B("LK"), [[2, 6], [-1, 2]], 1, 0)
+    iota(B("LN"), [[2, 6], [0, 2], [-1, 2]], 1, 0)
+    asel(B("PERM"), B("o256"), [[-32, 4], [0, 2], [-1, 32]], A.is_equal, 0.0, 0, 1)
     for t in range(HOPS):
-        iota(B("VV", 192 * t, 192 * t + 192), [[32, 12], [-2, 16]], 1664 - 384 * t + 29, 0)
-        iota(B("VAL", 192 * t, 192 * t + 192), [[32, 12], [-2, 16]], 1664 - 384 * t + 30, 0)
+        iota(B("VV", 192 * t, 192 * t + 192), [[64, 6], [-2, 32]], 1664 - 384 * t + 61, 0)
+        iota(B("VAL", 192 * t, 192 * t + 192), [[64, 6], [-2, 32]], 1664 - 384 * t + 62, 0)
         if t > 0:
             iota(B("CT", 256 * t, 256 * t + 256), [[0, 256]], 768 * t, 0)
     for c in (0, 1):
-        iota(col("CKt", c, 2), [[0, 2], [-64, CHUNK[c][1] // 16], [4, 16]], -2 * 1664 - 62 - 4 * CHUNK[c][0], 0)
-    asel(B("BDt"), B("ones"), [[-16, 8], [0, 16]], A.is_ge, 0.0, 0, 1)
+        iota(col("CKt", c, 2), [[0, 2], [-128, CHUNK[c][1] // 32], [4, 32]], -2 * 1664 - 126 - 4 * CHUNK[c][0], 0)
+    asel(B("BDt"), B("o256", 0, 128), [[-16, 8], [0, 16]], A.is_ge, 0.0, 0, 1)
     asel(B("BD"), B("BDt"), [[16, 8], [0, 16]], A.is_ge, 0.0, 15, -1)
-    asel(B("ID"), B("ones"), [[-1, 128]], A.is_equal, 0.0, 0, 1)
-    asel(B("SEL"), B("onef"), [[-1, 16], [-16, 8]], A.is_equal, 0.0, 0, 1)
+    asel(B("ID"), B("o256", 0, 128), [[-1, 128]], A.is_equal, 0.0, 0, 1)
+    if HALF < 2:
+        asel(B("SEL"), B("onef"), [[-1, 16], [-16, 8]], A.is_equal, 0.0, 0, 1)
+    for h in (0, 1):
+        asel(B("SE2", 128 * h, 128 * h + 128), B("onef"), [[-1, 8], [-16, 8], [8 - 16 * (1 - h), 2]], A.is_equal, 0.0, -8 * h, 1)
+    asel(B("E2t"), B("o256", 0, 64), [[-2, 64]], A.is_ge, 0.0, 0, 1)
+    asel(B("E2"), B("E2t"), [[2, 64]], A.is_ge, 0.0, 1, -1)
+    iota(B("ODt"), [[0, 8], [1, 2], [0, 8]], 0, 0)
     asel(B("GBt"), B("onef", 0, 8), [[-16, 8]], A.is_ge, 0.0, 0, 1)
     asel(B("GB"), B("GBt"), [[16, 8]], A.is_ge, 0.0, 15, -1)
     asel(B("WNb"), B("WNa"), [[0, 16], [-16, 8]], A.is_ge, 0.0, 0, 1)
     asel(B("WNa"), B("WNb"), [[0, 16], [16, 8]], A.is_ge, 0.0, 15, -1)
     asel(B("WN"), B("WNa"), [[-1, 16], [-16, 8]], A.not_equal, -65536 * U, 0, 1)
-    ts(B("qJ"), B("qI"), 15, None, A.bitwise_and); cp(B("qi"), B("qJ")); cp(B("wtf"), B("wts"))
+    ts(B("qJ"), B("qI"), 15, None, A.bitwise_and); cp(B("qi"), B("qJ")); act(B("wtf"), B("wts"))
     ts(B("qK"), B("qJ"), 1, None, A.bitwise_and)
     ts(B("qr"), B("qi"), -1.0, 15.0, A.mult, A.add)
-    ts(B("qa"), B("qi"), -15.5 - T0, None, A.add); ts(B("qb"), B("qi"), 2.0 ** -18, None, A.mult)
-    ts(B("q15"), B("qi"), 15.0, None, A.is_equal); ts(B("qe"), B("qK"), -1.0, 1.0, A.mult, A.add)
-    tt(B("w1"), B("qe"), B("q15"), A.add); ts(B("qo"), B("w1"), -1.0, 1.0, A.mult, A.add)
-    ts(B("EQD"), B("CI"), B("qi"), None, A.is_equal); ts(B("EQR"), B("CI", 0, 192), B("qr"), None, A.is_equal)
-    cp(B("LC"), B("LI")); ts(B("LP"), B("LI"), 16.0, B("qr"), A.mult, A.add)
-    ts(B("RSP", 0, 256, 16), B("RSi"), B("qi"), None, A.add)
+    act(B("qa"), B("qi"), bias=-15.5 - T0); act(B("qb"), B("qi"), scale=2.0 ** -18)
+    act(B("q15"), B("qi"), F.Relu, bias=-14.0); act(B("qe"), B("qK"), scale=-1.0, bias=1.0)
+    act(B("w1"), B("qe"), F.Identity, bias=B("q15")); act(B("qo"), B("w1"), scale=-1.0, bias=1.0)
+    ts(B("ODD"), B("ODt"), B("qe"), -2.0 ** 19, A.is_equal, A.mult); act(B("E2b"), B("E2"))
+    ts(B("EQD"), B("CI", 0, 256), B("qi"), None, A.is_equal); ts(B("EQR"), B("CI"), B("qr"), None, A.is_equal)
+    cp(B("LC"), B("LI")); cp(B("LD"), B("LK")); cp(B("LE"), B("LN")); ts(B("LP"), B("LK"), 16.0, B("qr"), A.mult, A.add)
+    ts(B("EQ2", 0, 64), B("CJ", 0, 64), B("qi"), None, A.is_equal); act(B("qi16"), B("qi"), bias=16.0)
+    act(B("RSP", 0, 256, 16), B("RSi"), F.Identity, bias=B("qi"))
+    act(B("RSP", 256, 384, 16), B("RSP", 0, 128, 16), bias=-4096.0)
     act(B("CKu"), B("EQD"), scale=2.0)
     for c in (0, 1):
-        act(col("CB", c, 1), B("EQD", 0, CHUNK[c][1]), scale=4096.0, bias=-4080.0)
+        for a in range(4 * CHUNK[c][0] + 2 * CHUNK[c][1], 4 * (CHUNK[c][0] + CHUNK[c][1]), 64):
+            act(B("CB", a, a + 64), B("EQ2", 0, 64), scale=4096.0, bias=-4064.0)
         tt(col("CK", c, 2), col("CKt", c, 2), B("CKu", 0, 2 * CHUNK[c][1]), A.add)
     for n, v in (("I2K", 2048.0), ("I37", 2.0 ** 18 * U), ("IDb", 1.0), ("NID", -1.0), ("N64", -64.0), ("I4K", 4096.0), ("I4b", 4096.0),
                  ("DE", B("qe")), ("DO", B("qo")), ("D15", B("q15"))):
@@ -431,13 +467,12 @@ def rank_program(g, core, T, topo):
     act(B("YW"), B("BD"), scale=B("qs1")); act(B("Y15"), B("BD"), scale=B("qy15"))
     act(B("YE"), B("YW"), scale=B("qe")); act(B("YO"), B("YW"), scale=B("qo"))
 
-    for j in range(4):
-        cp(B("ET", SP + j * QW, SP + j * QW + QW), B("enS", j * QW, j * QW + QW))
     cp(B("v0f", 0, 12), B("v0s"))
-    tt(B("LM"), I(B("v0f"), B("LC")), B("EQR"), A.mult)
+    tt(B("LM"), I(B("v0f"), B("LD")), B("EQR", 0, 192), A.mult)
+    tt(B("LM2"), I(B("v0f"), B("LE")), B("EQR"), A.mult)
     for c in (0, 1):
-        fill(msg("MM", 0, c, 1), T0)
-        spread(c, B("BD"), col("LM", c))
+        act(msg("MM", 0, c, 1), B("o256", 0, CHUNK[c][1]), scale=T0)
+        spread(c, B("BD"), col("LM2", c, 2))
         mm(col("pb4", c), B("BD"), col("LM", c))
         act(msg("MM", 0, c, 0), col("pb4", c))
         act(msg("MM", 0, c, 2), I(B("z0s"), B("LP", CHUNK[c][0] // 16, (CHUNK[c][0] + CHUNK[c][1]) // 16)))
@@ -449,8 +484,10 @@ def rank_program(g, core, T, topo):
         base = 4096 - 512 * t
         if t > 0:
             for c in (0, 1):
-                K["arrive"]("aL%d%d" % (c, t), prv_eng, lst("RT", t, c, 0, 24))
-                K["arrive"]("aM%d%d" % (c, t), prv_eng, msg("MM", t, c, 0, 3))
+                K["arrive"]("aL%d%d" % (c, t), prv_eng, lst("RT", t, c, 0, CHUNK[c][1] // 8))
+                K["arrive"]("aM%d%d" % (c, t), prv_eng, msg("MM", t, c, 0, 2 if SPLIT[c] else 3))
+                if SPLIT[c]:
+                    K["arrive"]("aZ%d%d" % (c, t), prv_eng, msg("MM", t, c, 2))
 
         def W(c, n, a=0, b=128, st=1):
             return B(n, a, b, st, 0, CHUNK[c][1])
@@ -459,8 +496,7 @@ def rank_program(g, core, T, topo):
             return B(name, 16 * CHUNK[c][0] + k, 16 * (CHUNK[c][0] + CHUNK[c][1]), st)
 
         def ring(c):
-            cp(col("RI", c), I(ET, lst("RT", t, c)))
-            ts(col("RJ", c), col("RI", c), 2047, None, A.bitwise_and)
+            ts(col("RJ", c), I(ET, lst("RT", t, c)), 2047, None, A.bitwise_and)
             cp(col("RL", c), col("RJ", c))
 
         def rings(q, a, b):
@@ -477,6 +513,28 @@ def rank_program(g, core, T, topo):
 
         def pick(c):
             s, n = str(c), CHUNK[c][1]
+            if HALF > 1 - c:
+                hs = range(CHUNK[c][0] // 64, (CHUNK[c][0] + n) // 64)
+                for h in hs:
+                    bk, a = (("pb1", 128), ("pb0", 128), ("pb1", 256))[h]
+                    pm, sb, nm = (B(x, 128 * h, 128 * h + 128) for x in ("pm", "sbh", "nmh"))
+                    mm(B(bk, a, a + 128), B("IDb"), B("ODD"), True, False)
+                    for k in range(8):
+                        i = (k + t) % 16
+                        mm(B(bk, a + k, a + 128, 8), B("X", 1024 * h + k, 1024 * h + 1024, 8), B("SE2", 16 * i, 16 * i + 16), False, k == 7)
+                    if "pm%d" % h in ONS:
+                        act(pm, B(bk, a, a + 128), F.Relu)
+                    else:
+                        ts(pm, B(bk, a, a + 128), 0.0, None, A.max)
+                    lin("sb%d" % h, sb, pm, 1.0, -1023.5)
+                    tt(nm, pm, sb, A.subtract)
+                    mm(B("pb6", 64 * h, 64 * h + 64), nm, B("E2"))
+                    ts(B("AL", 64 * h, 64 * h + 64), B("pb6", 64 * h, 64 * h + 64), -1024.0, None, A.add)
+                for h in hs:
+                    o = B("pb" + s, 0, 128, 1, 64 * (h % 2), 64 * (h % 2) + 64)
+                    mm(o, B("E2"), B("nmh", 128 * h, 128 * h + 128), True, False)
+                    mm(o, B("E2b"), B("sbh", 128 * h, 128 * h + 128), False, True)
+                return
             for k in range(16):
                 i = (k + t) % 16
                 mm(W(c, "pb" + s, k, 128, 16), bc("X", c, k), B("SEL", 8 * i, 8 * i + 8))
@@ -487,7 +545,7 @@ def rank_program(g, core, T, topo):
 
         def newer(c):
             kk = "pb%d" % (2 + c)
-            bk, a, b = ("pb4", 0, WD * NA) if c == 0 else ("pb6", 256, 256 + WD * (192 - NA))
+            bk, a, b = ("pb4", 0, WD * NA) if c == 0 else (TB, 256, 256 + WD * (192 - NA))
             if t > 0:
                 for m in range(WD):
                     mm(B(bk, a + m, b, WD), B("I2K"), msg("MM", t, c, 1))
@@ -531,21 +589,30 @@ def rank_program(g, core, T, topo):
             for k, d, w in sums:
                 mm(W(c, kk, k, 128, 16), d, B(w), False, k == sums[-1][0])
 
+        def fused(c):
+            p0, n = CHUNK[c]
+            for k in range(16):
+                asel(bc("ZE", c, k), msg("MM", t, c, 2), [[0, n]], A.is_equal, 0.0, 0, 0)
+            for p in range(p0, p0 + n, FUSE):
+                tt(B("D", 16 * p, 16 * (p + FUSE)), I(XS, B("AL", p, p + FUSE)), B("ZE", 16 * p, 16 * (p + FUSE)), A.subtract)
+                act(B("AB", 16 * p, 16 * (p + FUSE)), B("D", 16 * p, 16 * (p + FUSE)), F.Abs)
+            for k in range(16):
+                mm(W(c, "pb%d" % (2 + c), k, 128, 16), bc("AB", c, k), B("WA"), False, k == 15)
+
         def hash_():
             for c in (0, 1):
                 mm(W(c, "pb6", 192 + 8 * c, 200 + 8 * c), msg("MM", t, c, 2), B("WD"))
             cp(B("ui"), B("pb6", 192, 208))
             ts(B("ua"), B("ui"), 2047, None, A.bitwise_and)
-            ts(B("ub"), B("ua"), 1184.0, None, A.add)
-            tt(B("uc"), B("ua"), B("ub"), A.mult)
+            act(B("uc"), B("ua"), F.Square, bias=592.0)
             if t > 0:
                 act(B("Ax"), B("pb6", 208, 209), scale=-1.0, bias=4080 - 17 * 65536.0)
                 act(B("Ay"), B("pb6", 208, 209), F.Identity, bias=B("Ax"))
-                ts(B("ud"), B("uc"), B("Ay"), None, A.add)
+                ts(B("ud"), B("uc"), B("Ay"), -592.0 ** 2, A.add, A.add)
             else:
-                cp(B("ud"), B("uc"))
+                ts(B("ud"), B("uc"), -592.0 ** 2, None, A.add)
             ts(B("ue"), B("ud"), 5, 2047, A.arith_shift_right, A.bitwise_and)
-            ts(B("ff"), B("ue"), -B1, None, A.add)
+            act(B("ff"), B("ue"), bias=-B1)
 
         def least(c):
             s = str(c)
@@ -565,7 +632,7 @@ def rank_program(g, core, T, topo):
 
         def turn(c):
             n = CHUNK[c][1]
-            spread(c, W(c, "WF%d" % c), W(c, "ID", 0, n))
+            spread(c, W(c, "WF%d" % c), W(c, "PERM", 0, 2 * n))
             mm(B("pb4", 0, n), W(c, "WF%d" % c), W(c, "ID", 0, n))
             mm(B("pb4", n, 2 * n), W(c, "WS%d" % c), W(c, "IDb", 0, n))
             act(msg("MO", t, c, 0), B("pb4", 0, n))
@@ -593,7 +660,7 @@ def rank_program(g, core, T, topo):
                 for w, r in sorted(((wo, own), (we, oth)), key=lambda x: x[1] == "Rf"):
                     mm(o, B(w), col(r, c), False, r == "Rf")
             act(col("NN", c, 2), B("pb%d" % c, 0, 2 * n), F.Identity, bias=16 * 2048.0 * (9 + t) if last else B("BT", t, t + 1))
-            tt(col("PRE", c), I(FT, fl), B("VAL", 192 * t + p0, 192 * t + p0 + n), A.min)
+            tt(col("PRE", c), I(FU if c else FT, fl), B("VAL", 192 * t + p0, 192 * t + p0 + n), A.min)
             mm(B(y, 0, 2 * n), B("I4K"), col("CK", c, 2), True, False)
             if t > 0:
                 mm(B(y, 0, 2 * n), B("I4b"), B("CT", 256 * t, 256 * t + 2 * n), False, False)
@@ -604,42 +671,48 @@ def rank_program(g, core, T, topo):
                 lin("av", col("av", c), I(FT, vl), 1.0, 1.0)
                 lin("af", col("af", c), I(FT, fl), 1.0, 0.0)
             else:
-                marks(MQ[c], "FU", "VAL", 192 * t, "OT", t, c)
-                act(B("GV", 0, n), I(FT, vl), bias=1.0)
+                marks(MQ[c], "FU", "PRE", 0, "OT", t, c)
+                act(B("GV", 0, n), I(FT, vl)); act(B("GV", n, 2 * n), I(FT, fl))
                 tt(col("av", c), I(FU, vl), B("GV", 0, n), A.min)
-                tt(col("af", c), I(FU, fl), col("PRE", c), A.min)
+                tt(col("af", c), I(FU, fl), B("GV", n, 2 * n), A.min)
             for a in ("av", "af"):
                 for h in (0, 1):
                     mm(B(y, h * n, h * n + n), B("I4K"), col(a, c), False, a == "af" and h == 1)
-            scan(B(ys, 0, 2 * n), B("RSP", 0, 2 * n), B(y, 0, 2 * n), 1.0e6, A.min, A.max)
-            ts(pos, B(ys, 15, 2 * n, 16), float(SP), None, A.add)
+            scan(B(ys, 0, 2 * n), B("RSP", 256 * c, 256 * c + 2 * n), B(y, 0, 2 * n), 1.0e6, A.min, A.max)
+            ts(pos, B(ys, 15, 2 * n, 16), SP + 4096.0 * c, None, A.add)
             scat("V", B("YS" if last else "ET"), pos, col("NN", c, 2))
 
         def ysum(j, bk):
+            act(B("EF", 512 * j, 512 * j + 512), B("ET", SP + 512 * j, SP + 512 * j + 512))
             for a in range(0, 512, 128):
-                mm(B(bk, a, a + 128), B("YW"), B("ET", SP + 512 * j + a, SP + 512 * j + a + 128))
+                mm(B(bk, a, a + 128), B("YW"), B("EF", 512 * j + a, 512 * j + a + 128))
             act(B("YS", SP + 512 * j, SP + 512 * j + 512), B(bk))
 
         ring(0); ring(1)
-        rings("S", EV, NA); rings("V", 0, EV); rings("S", NA, 192)
+        for h in range(3):
+            rings("V", 64 * h, 64 * h + EV[h]); rings("S", 64 * h + EV[h], 64 * h + 64)
         for c in (0, 1):
             act(col("Rv", c), I(ET, lst("RT", t, c)))
             newer(c)
         pick(0); pick(1)
-        marks("S", "FT", "VV", 192 * t, "RT", t, 1); marks("S", "FT", "VV", 192 * t, "RT", t, 0)
-        records("S", RV, NA); records("V", 0, RV); records("S", NA, 192 - RW); records("V", 192 - RW, 192)
+        marks("S", "FT", "VV", 192 * t, "RT", t, 0); marks("S", "FU", "VV", 192 * t, "RT", t, 1)
+        for h in range(2 if FUSE else 3):
+            records("V", 64 * h, 64 * h + RV[h]); records("S", 64 * h + RV[h], 64 * h + 64)
         if last:
-            ysum(0, "pb7"); ysum(1, "pb5")
-        hash_(); sizes(0); sizes(1)
+            for j in range(YE):
+                ysum(j, ("pb7", "pb5")[j % 2])
+        hash_(); sizes(0); (fused if FUSE else sizes)(1)
         if last:
-            ysum(2, "pb5"); ysum(3, "pb5")
+            for j in range(YE, 4):
+                ysum(j, ("pb6", "pb5")[j % 2])
         for c in (0, 1):
             least(c); turn(c); dedupe(c, "OT", t)
             if not last:
-                sent += K["send"](core, nxt, topo, lst("RT", t + 1, c, 0, 24), lst("OT", t, c, 0, 24), "aL%d%d" % (c, t + 1))
+                sent += K["send"](core, nxt, topo, lst("RT", t + 1, c, 0, CHUNK[c][1] // 8), lst("OT", t, c, 0, CHUNK[c][1] // 8), "aL%d%d" % (c, t + 1))
             zproc(c)
             if not last:
-                sent += K["send"](core, nxt, topo, msg("MM", t + 1, c, 0, 3), msg("MO", t, c, 0, 3), "aM%d%d" % (c, t + 1))
+                for m, a, b in (("M", 0, 2), ("Z", 2, 3)) if SPLIT[c] else (("M", 0, 3),):
+                    sent += K["send"](core, nxt, topo, msg("MM", t + 1, c, a, b), msg("MO", t, c, a, b), "a%s%d%d" % (m, c, t + 1))
             act(col("Rf", c), I(ET, lst("OT", t, c)))
         meetings(0); meetings(1)
         if not last:
@@ -662,7 +735,7 @@ def rank_program(g, core, T, topo):
     K["issue"]()
     for q in ("V", "S", "P", "G"):
         g.wait_ge(T.sem["c" + q], K["cnt"][q])
-    for j in range(8):
+    for j in (0, 1, 2, 3, 7):
         g.wait_ge(T.sem["ld%d" % j], 16)
     for j in range(3):
         g.wait_ge(T.sem["st%d" % j], 16)

@@ -12,7 +12,7 @@ HALF = 2
 SPLIT = (1, 0)
 EV, RV = (32, 32, 0), (0, 32, 0)
 MQ = "SV"
-ONS = ("av",)
+ONS = ("av", "af", "t1", "WS")
 DB = ("pb7", "pb5")
 KS = (0, 4)
 SP = 384
@@ -20,9 +20,12 @@ B0 = 2.0 ** 18 + 4096
 T0 = B0 / 2048 + 1
 B1 = B0 + 4096
 U = 2.0 ** 19
-PE, GATHER, SCATTER, FIX, OWN, CROSS, LAG, FAR = 0.72, 1.5, 3.5, 48, 145, 300, 2200, 4500
+PE, GATHER, SCATTER, FIX, OWN, CROSS, LAG, FAR = 0.64, 1.6, 3.5, 24, 230, 230, 2200, 4500
 SB = ("pb7", "pb5")
-FIRST = 3000
+FIRST = 2200
+EG = ()
+RP = 64
+PB = "pb6"
 YE = 1
 LW = 2
 ROUNDS = 3
@@ -49,12 +52,12 @@ for n_, w_, t_ in (
         ("YP", 192, f4), ("YQ", 192, f4), ("YZ", 192, b2), ("ZL", 192, b2),
         ("v0s", 12, i4), ("v0f", 12, f4), ("z0s", 192, b2), ("wts", 1, i4), ("wtf", 1, f4), ("LP", 12, u2), ("LC", 12, u2),
         ("onef", 128, f4), ("oneb", 192, b2), ("ID", 128, f2), ("NID", 128, f2), ("N64", 128, f2), ("I2K", 128, f2),
-        ("I4K", 128, f2), ("IDb", 128, b2), ("I37", 128, b2), ("I4b", 128, b2), ("CT", 1280, b2), ("GV", 128, f4), ("FU", 2080, f4), ("PERM", 256, f2), ("o256", 256, f2), ("CJ", 256, f4), ("EQ2", 256, f4), ("LM2", 384, f2), ("LK", 12, f4), ("LN", 24, f4), ("LD", 12, u2), ("LE", 24, u2), ("qi16", 1, f4), ("BDt", 128, f2), ("BD", 128, f2), ("GBt", 8, f4), ("GB", 8, f4),
+        ("I4K", 128, f2), ("IDb", 128, b2), ("I37", 128, b2), ("I4b", 128, b2), ("CT", 1920, b2), ("ysa", 384, f4), ("GV", 128, f4), ("FU", 2080, f4), ("PERM", 256, f2), ("o256", 256, f2), ("CJ", 256, f4), ("EQ2", 256, f4), ("LM2", 384, f2), ("LK", 12, f4), ("LN", 24, f4), ("LD", 12, u2), ("LE", 24, u2), ("qi16", 1, f4), ("BDt", 128, f2), ("BD", 128, f2), ("GBt", 8, f4), ("GB", 8, f4),
         ("SEL", 128, f4), ("SE2", 256, f4), ("E2t", 64, f2), ("E2", 64, f2), ("E2b", 64, b2), ("ODt", 128, f4), ("ODD", 128, b2), ("pm", 384, f4), ("sbh", 384, b2), ("nmh", 384, f2), ("WNa", 128, b2), ("WNb", 128, b2), ("WN", 128, b2), ("WX", 8, b2), ("WR", 8, b2), ("WA", 8, b2), ("WD", 8, f2), ("C32", 128, f4),
         ("qI", 1, i4), ("qJ", 1, i4), ("qK", 1, i4), ("qi", 1, f4), ("qr", 1, f4), ("qe", 1, f4), ("q15", 1, f4), ("qo", 1, f4), ("qs1", 1, f4),
         ("w1", 1, f4), ("qa", 1, f4), ("qb", 1, f4), ("qy15", 1, f4), ("qp", 1, f4), ("qh", 1, f4), ("SCq", 1, f4), ("BIq", 1, f4),
         ("CI", 384, f4), ("EQD", 256, f4), ("EQR", 384, f4), ("LI", 12, f4), ("CKt", 384, f4), ("CKu", 256, f4), ("CK", 384, f2), ("CB", 768, f2),
-        ("RST", 128, f4), ("HOLD", 256, f4), ("RSP", 384, f4), ("RSi", 16, f4),
+        ("RST", 128, f4), ("HOLD", 256, f4), ("RSP", 384, f4), ("RSi", 24, f4),
         ("DO", 128, f4), ("DE", 128, f4), ("D15", 128, f2), ("YO", 128, f4), ("YE", 128, f4), ("Y15", 128, f2), ("YW", 128, f4), ("BT", 5, f4),
         ("GF", 128, f2), ("GT", 128, f2), ("LM", 192, f2),
         ("RI", 192, i4), ("RJ", 192, i4), ("RL", 192, u2), ("X", 3072, f4), ("M", 3072, b2), ("R", 3072, b2), ("MX", 3072, b2), ("AB", 3072, b2), ("WZt", 128, b2), ("WZ0", 128, b2), ("WZ1", 128, b2), ("AL", 192, u2),
@@ -404,10 +407,13 @@ def rank_program(g, core, T, topo):
     iota(B("qI"), [[0, 1]], 0, 1, True)
     iota(B("CI"), [[0, 24], [1, 16]], 0, 0)
     iota(B("LI"), [[1, 12]], 0, 0)
-    iota(B("RSi"), [[-16, 16]], -16, 0)
+    iota(B("RSi"), [[-16, 24]], -16 - 4096, 0)
     for j in range(4):
         for a in (520 * j, 520 * j + 260):
-            act(B("FT", a, a + 260), B("CI", 0, 260), scale=0.0, bias=2048.0)
+            if j < 2:
+                act(B("FT", a, a + 260), B("CI", 0, 260), scale=0.0, bias=2048.0)
+            else:
+                fill(B("FT", a, a + 260), 2048.0)
         iota(B("FU", 520 * j, 520 * j + 520), [[0, 520]], 2048, 0)
     iota(B("CJ", 0, 64), [[-100, 2], [100, 2], [1, 16]], 0, 0)
     iota(B("LK"), [[2, 6], [-1, 2]], 1, 0)
@@ -417,7 +423,7 @@ def rank_program(g, core, T, topo):
         iota(B("VV", 192 * t, 192 * t + 192), [[64, 6], [-2, 32]], 1664 - 384 * t + 61, 0)
         iota(B("VAL", 192 * t, 192 * t + 192), [[64, 6], [-2, 32]], 1664 - 384 * t + 62, 0)
         if t > 0:
-            iota(B("CT", 256 * t, 256 * t + 256), [[0, 256]], 768 * t, 0)
+            iota(B("CT", 384 * t, 384 * t + 384), [[0, 384]], 768 * t, 0)
     for c in (0, 1):
         iota(col("CKt", c, 2), [[0, 2], [-128, CHUNK[c][1] // 32], [4, 32]], -2 * 1664 - 126 - 4 * CHUNK[c][0], 0)
     asel(B("BDt"), B("o256", 0, 128), [[-16, 8], [0, 16]], A.is_ge, 0.0, 0, 1)
@@ -445,8 +451,7 @@ def rank_program(g, core, T, topo):
     ts(B("EQD"), B("CI", 0, 256), B("qi"), None, A.is_equal); ts(B("EQR"), B("CI"), B("qr"), None, A.is_equal)
     cp(B("LC"), B("LI")); cp(B("LD"), B("LK")); cp(B("LE"), B("LN")); ts(B("LP"), B("LK"), 16.0, B("qr"), A.mult, A.add)
     ts(B("EQ2", 0, 64), B("CJ", 0, 64), B("qi"), None, A.is_equal); act(B("qi16"), B("qi"), bias=16.0)
-    act(B("RSP", 0, 256, 16), B("RSi"), F.Identity, bias=B("qi"))
-    act(B("RSP", 256, 384, 16), B("RSP", 0, 128, 16), bias=-4096.0)
+    act(B("RSP", 0, 384, 16), B("RSi"), F.Identity, bias=B("qi"))
     act(B("CKu"), B("EQD"), scale=2.0)
     for c in (0, 1):
         for a in range(4 * CHUNK[c][0] + 2 * CHUNK[c][1], 4 * (CHUNK[c][0] + CHUNK[c][1]), 64):
@@ -496,8 +501,10 @@ def rank_program(g, core, T, topo):
             return B(name, 16 * CHUNK[c][0] + k, 16 * (CHUNK[c][0] + CHUNK[c][1]), st)
 
         def ring(c):
-            ts(col("RJ", c), I(ET, lst("RT", t, c)), 2047, None, A.bitwise_and)
-            cp(col("RL", c), col("RJ", c))
+            p0, n = CHUNK[c]
+            for p in range(0, n, RP):
+                ts(B("RJ", p0 + p, p0 + min(n, p + RP)), I(ET, lst("RT", t, c, p // 16, min(n, p + RP) // 16)), 2047, None, A.bitwise_and)
+                cp(B("RL", p0 + p, p0 + min(n, p + RP)), B("RJ", p0 + p, p0 + min(n, p + RP)))
 
         def rings(q, a, b):
             for p in range(a, b, PC):
@@ -517,16 +524,14 @@ def rank_program(g, core, T, topo):
                 hs = range(CHUNK[c][0] // 64, (CHUNK[c][0] + n) // 64)
                 for h in hs:
                     bk, a = (("pb1", 128), ("pb0", 128), ("pb1", 256))[h]
-                    pm, sb, nm = (B(x, 128 * h, 128 * h + 128) for x in ("pm", "sbh", "nmh"))
+                    sb, nm = (B(x, 128 * h, 128 * h + 128) for x in ("sbh", "nmh"))
                     mm(B(bk, a, a + 128), B("IDb"), B("ODD"), True, False)
                     for k in range(8):
                         i = (k + t) % 16
                         mm(B(bk, a + k, a + 128, 8), B("X", 1024 * h + k, 1024 * h + 1024, 8), B("SE2", 16 * i, 16 * i + 16), False, k == 7)
-                    if "pm%d" % h in ONS:
-                        act(pm, B(bk, a, a + 128), F.Relu)
-                    else:
-                        ts(pm, B(bk, a, a + 128), 0.0, None, A.max)
-                    lin("sb%d" % h, sb, pm, 1.0, -1023.5)
+                    pm = B(PB or bk, 384, 512)
+                    ts(sb, B(bk, a, a + 128), 0.0, -1023.5, A.max, A.add)
+                    ts(pm, B(bk, a, a + 128), 0.0, None, A.max)
                     tt(nm, pm, sb, A.subtract)
                     mm(B("pb6", 64 * h, 64 * h + 64), nm, B("E2"))
                     ts(B("AL", 64 * h, 64 * h + 64), B("pb6", 64 * h, 64 * h + 64), -1024.0, None, A.add)
@@ -651,7 +656,6 @@ def rank_program(g, core, T, topo):
 
         def meetings(c):
             p0, n = CHUNK[c]
-            y, ys, pos = "pb%d" % (2 + c), "ys%d" % c, B("POS", p0 // 8, (p0 + n) // 8)
             vl, fl = lst("RT", t, c), lst("OT", t, c)
             wo, we, w15 = ("YO", "YE", "Y15") if last else ("DO", "DE", "D15")
             for h, (own, oth, new) in enumerate((("Rv", "Rf", "MO"), ("Rf", "Rv", "MM"))):
@@ -661,29 +665,36 @@ def rank_program(g, core, T, topo):
                     mm(o, B(w), col(r, c), False, r == "Rf")
             act(col("NN", c, 2), B("pb%d" % c, 0, 2 * n), F.Identity, bias=16 * 2048.0 * (9 + t) if last else B("BT", t, t + 1))
             tt(col("PRE", c), I(FU if c else FT, fl), B("VAL", 192 * t + p0, 192 * t + p0 + n), A.min)
-            mm(B(y, 0, 2 * n), B("I4K"), col("CK", c, 2), True, False)
-            if t > 0:
-                mm(B(y, 0, 2 * n), B("I4b"), B("CT", 256 * t, 256 * t + 2 * n), False, False)
-            mm(B(y, 0, n), B("ID"), msg("MM", t, c, 0), False, False)
-            mm(B(y, n, 2 * n), B("ID"), msg("MO", t, c, 0), False, False)
             if c == 0:
                 marks(MQ[c], "FT", "PRE", 0, "OT", t, c)
-                lin("av", col("av", c), I(FT, vl), 1.0, 1.0)
+                lin("av", col("av", c), I(FT, vl), 1.0, 0.0)
                 lin("af", col("af", c), I(FT, fl), 1.0, 0.0)
             else:
                 marks(MQ[c], "FU", "PRE", 0, "OT", t, c)
-                act(B("GV", 0, n), I(FT, vl)); act(B("GV", n, 2 * n), I(FT, fl))
+                lin("g1", B("GV", 0, n), I(FT, vl), 1.0, 0.0); lin("g2", B("GV", n, 2 * n), I(FT, fl), 1.0, 0.0)
                 tt(col("av", c), I(FU, vl), B("GV", 0, n), A.min)
                 tt(col("af", c), I(FU, fl), B("GV", n, 2 * n), A.min)
-            for a in ("av", "af"):
-                for h in (0, 1):
-                    mm(B(y, h * n, h * n + n), B("I4K"), col(a, c), False, a == "af" and h == 1)
-            scan(B(ys, 0, 2 * n), B("RSP", 256 * c, 256 * c + 2 * n), B(y, 0, 2 * n), 1.0e6, A.min, A.max)
-            ts(pos, B(ys, 15, 2 * n, 16), SP + 4096.0 * c, None, A.add)
-            scat("V", B("YS" if last else "ET"), pos, col("NN", c, 2))
+
+        def stand():
+            mm(B("pb2", 0, 384), B("I4K"), B("CK"), True, False)
+            if t > 0:
+                mm(B("pb2", 0, 384), B("I4b"), B("CT", 384 * t, 384 * t + 384), False, False)
+            for h, m in enumerate(("MM", "MO")):
+                for c in (0, 1):
+                    mm(col("pb2", c, h), B("ID"), msg(m, t, c, 0), False, False)
+            for c in (0, 1):
+                for a in ("av", "af"):
+                    for h in (0, 1):
+                        mm(col("pb2", c, h), B("I4K"), col(a, c), False, (c, a, h) == (1, "af", 1))
+            scan(B("ysa"), B("RSP"), B("pb2", 0, 384), 1.0e6, A.min, A.max)
+            ts(B("POS"), B("ysa", 15, 384, 16), SP + 4096.0, None, A.add)
+            scat("V", B("YS" if last else "ET"), B("POS"), B("NN"))
 
         def ysum(j, bk):
-            act(B("EF", 512 * j, 512 * j + 512), B("ET", SP + 512 * j, SP + 512 * j + 512))
+            if j in EG:
+                asel(B("EF", 512 * j, 512 * j + 512), B("ET", SP + 512 * j, SP + 512 * j + 512), [[0, 512]], A.is_equal, 0.0, 0, 0)
+            else:
+                act(B("EF", 512 * j, 512 * j + 512), B("ET", SP + 512 * j, SP + 512 * j + 512))
             for a in range(0, 512, 128):
                 mm(B(bk, a, a + 128), B("YW"), B("EF", 512 * j + a, 512 * j + a + 128))
             act(B("YS", SP + 512 * j, SP + 512 * j + 512), B(bk))
@@ -714,7 +725,7 @@ def rank_program(g, core, T, topo):
                 for m, a, b in (("M", 0, 2), ("Z", 2, 3)) if SPLIT[c] else (("M", 0, 3),):
                     sent += K["send"](core, nxt, topo, msg("MM", t + 1, c, a, b), msg("MO", t, c, a, b), "a%s%d%d" % (m, c, t + 1))
             act(col("Rf", c), I(ET, lst("OT", t, c)))
-        meetings(0); meetings(1)
+        meetings(0); meetings(1); stand()
         if not last:
             for c in (0, 1):
                 act(W(c, "FC", 8 * c, 8 * c + 8), W(c, "WS%d" % c, 0, 128, 16), F.Relu, scale=-1.0, bias=1.0 - B1, total=W(c, "FA", c, c + 1))
@@ -722,7 +733,6 @@ def rank_program(g, core, T, topo):
                 mm(B("pb6", 208, 209), W(c, "C32"), W(c, "FA", c, c + 1), c == 0, c == 1)
 
     t = HOPS - 1
-    dma("Y", "st2", T.ys[:], T.YS[0:128:16, SP:SP + 2048], [], [B("YS")])
     act(B("YZ"), I(B("ZL"), B("LP")))
     dma("S", "st0", T.yz[:], T.YZ[:], [], [B("YZ")])
     for c in (0, 1):
@@ -730,7 +740,8 @@ def rank_program(g, core, T, topo):
         mm(col("pb5", c), B("I2K"), msg("MO", t, c, 1), False, True)
     act(B("YQ"), B("pb5", 0, 192), bias=-2048 * T0)
     act(B("YP"), I(B("YQ"), B("LP")))
-    dma("Y", "st1", T.yp[:], T.YP[0:128:16, :], [], [B("YP")])
+    dma("S", "st1", T.yp[:], T.YP[0:128:16, :], [], [B("YP")])
+    dma("Y", "st2", T.ys[:], T.YS[0:128:16, SP:SP + 2048], [], [B("YS")])
 
     K["issue"]()
     for q in ("V", "S", "P", "G"):

@@ -5,34 +5,34 @@ HOPS = 5
 NA = 128
 CHUNK = ((0, NA), (NA, 192 - NA))
 WD = 4
-FUSE = 0
-TB = "pb5"
 PC = 64
-HALF = 2
-SPLIT = (1, 0)
+SENDS = ("L0", "M0", "L1", "Z0", "M1", "D0", "D1")
 EV, RV = (32, 32, 0), (0, 32, 0)
 MQ = "SV"
-ONS = ("av", "af", "t1", "WS")
-DB = ("pb7", "pb5")
+MV = "SS"
+ONS = ("av0", "av1", "ns")
 KS = (0, 4)
+APART = 1
+EG = ()
+BANK = dict(pick=("pb0", "pb1", "pb7"), thr=("pb4", "pb5"), zz=("pb4", "pb6"), diff=("pb0", "pb1"), same=("pb7", "pb5"), lst=("pb0", "pb6"),
+            row=("pb1", "pb4"), zp=("pb4", "pb6"), new=("pb0", "pb1"), ys=("pb0", "pb1", "pb0", "pb1"))
 SP = 384
 B0 = 2.0 ** 18 + 4096
 T0 = B0 / 2048 + 1
-B1 = B0 + 4096
-U = 2.0 ** 19
+U = 1792.0
+BAR = 243.0 * 2 ** 16
+CC = (B0 - 1024) / 64
+HI = 1.5 * 2 ** 17
 PE, GATHER, SCATTER, FIX, OWN, CROSS, LAG, FAR = 0.64, 1.6, 3.5, 24, 230, 230, 2200, 4500
-SB = ("pb7", "pb5")
 FIRST = 2200
-EG = ()
 RP = 64
-PB = "pb6"
 YE = 1
 LW = 2
 ROUNDS = 3
 f4, f2, b2, i4, u2 = "float32", "float16", "bfloat16", "int32", "uint16"
 SCRATCH = {}
-OWNBUF = ("EF", "ZE", "D", "ET", "YS", "XS", "FT", "FU", "YP", "YQ", "YZ", "ZL", "v0s", "v0f", "z0s", "wts", "X", "M", "R", "MX", "AB", "VAL", "VV", "MM", "MO",
-          "RT", "OT", "RL", "AL", "POS", "NN", "PRE", "LP", "LC", "LD", "LE", "fin0", "fin1")
+OWNBUF = ("EF", "ET", "YS", "XS", "FT", "FU", "YP", "ZL", "v0s", "v0f", "z0s", "wts", "X", "M", "R", "MX", "AB", "VAL", "VV", "MM", "MO",
+          "LT", "RL", "AL", "POS", "NN", "PRE", "LD", "NF0", "NF1")
 PLACE = {}
 
 
@@ -47,34 +47,32 @@ def declare(name, w, t):
     PLACE[name] = (pool, a, w)
 
 
-for n_, w_, t_ in (
-        ("EF", 2048, f4), ("ET", SP + 2048, i4), ("ZE", 3072, f2), ("D", 3072, b2), ("YS", SP + 2048, f4), ("XS", 2048, b2), ("FT", 2080, f4),
-        ("YP", 192, f4), ("YQ", 192, f4), ("YZ", 192, b2), ("ZL", 192, b2),
-        ("v0s", 12, i4), ("v0f", 12, f4), ("z0s", 192, b2), ("wts", 1, i4), ("wtf", 1, f4), ("LP", 12, u2), ("LC", 12, u2),
-        ("onef", 128, f4), ("oneb", 192, b2), ("ID", 128, f2), ("NID", 128, f2), ("N64", 128, f2), ("I2K", 128, f2),
-        ("I4K", 128, f2), ("IDb", 128, b2), ("I37", 128, b2), ("I4b", 128, b2), ("CT", 1920, b2), ("ysa", 384, f4), ("GV", 128, f4), ("FU", 2080, f4), ("PERM", 256, f2), ("o256", 256, f2), ("CJ", 256, f4), ("EQ2", 256, f4), ("LM2", 384, f2), ("LK", 12, f4), ("LN", 24, f4), ("LD", 12, u2), ("LE", 24, u2), ("qi16", 1, f4), ("BDt", 128, f2), ("BD", 128, f2), ("GBt", 8, f4), ("GB", 8, f4),
-        ("SEL", 128, f4), ("SE2", 256, f4), ("E2t", 64, f2), ("E2", 64, f2), ("E2b", 64, b2), ("ODt", 128, f4), ("ODD", 128, b2), ("pm", 384, f4), ("sbh", 384, b2), ("nmh", 384, f2), ("WNa", 128, b2), ("WNb", 128, b2), ("WN", 128, b2), ("WX", 8, b2), ("WR", 8, b2), ("WA", 8, b2), ("WD", 8, f2), ("C32", 128, f4),
-        ("qI", 1, i4), ("qJ", 1, i4), ("qK", 1, i4), ("qi", 1, f4), ("qr", 1, f4), ("qe", 1, f4), ("q15", 1, f4), ("qo", 1, f4), ("qs1", 1, f4),
-        ("w1", 1, f4), ("qa", 1, f4), ("qb", 1, f4), ("qy15", 1, f4), ("qp", 1, f4), ("qh", 1, f4), ("SCq", 1, f4), ("BIq", 1, f4),
-        ("CI", 384, f4), ("EQD", 256, f4), ("EQR", 384, f4), ("LI", 12, f4), ("CKt", 384, f4), ("CKu", 256, f4), ("CK", 384, f2), ("CB", 768, f2),
-        ("RST", 128, f4), ("HOLD", 256, f4), ("RSP", 384, f4), ("RSi", 24, f4),
-        ("DO", 128, f4), ("DE", 128, f4), ("D15", 128, f2), ("YO", 128, f4), ("YE", 128, f4), ("Y15", 128, f2), ("YW", 128, f4), ("BT", 5, f4),
-        ("GF", 128, f2), ("GT", 128, f2), ("LM", 192, f2),
-        ("RI", 192, i4), ("RJ", 192, i4), ("RL", 192, u2), ("X", 3072, f4), ("M", 3072, b2), ("R", 3072, b2), ("MX", 3072, b2), ("AB", 3072, b2), ("WZt", 128, b2), ("WZ0", 128, b2), ("WZ1", 128, b2), ("AL", 192, u2),
-        ("PEN", 192, b2), ("ui", 16, i4), ("ua", 16, i4), ("ub", 16, f4), ("uc", 16, f4), ("ud", 16, i4), ("ue", 16, i4), ("ff", 16, f4),
-        ("Ax", 1, b2), ("Ay", 1, f4), ("FC", 16, f4), ("FA", 2, f4), ("TPs", 192, f2), ("Rv", 192, f4), ("Rf", 192, f4), ("PRE", 192, f4),
-        ("av", 192, f2), ("af", 192, f2), ("POS", 24, u2), ("NN", 384, f4), ("XF", 192, f2), ("R1", 192, f2),
-        ("VAL", 960, f4), ("VV", 960, f4), ("MM", 2880, f2), ("MO", 2880, f2), ("RT", 320, u2), ("OT", 320, u2)):
-    declare(n_, w_, t_)
+for t_, tiles in (
+        (f4, (("EF", 2048), ("YS", SP + 2048), ("FT", 2080), ("FU", 2080), ("YP", 192), ("v0f", 12), ("X", 3072), ("NN", 384), ("PRE", 192),
+              ("VAL", 960), ("VV", 960), ("Rv", 192), ("Rf", 192), ("ysa", 384), ("onef", 128), ("SE2", 256), ("C32", 128), ("LI", 12), ("CL", 256),
+              ("RSA", 256), ("RSB", 128), ("RSC", 128), ("THR", 16), ("RSP", 384), ("RSi", 24), ("QS", 6),
+              ("DO", 128), ("DE", 128), ("YO", 128), ("YE", 128), ("YW", 128), ("BT", 5), ("uc", 16), ("Ay", 1), ("FC", 16), ("FA", 2), ("wtf", 1))
+         + tuple((q, 1) for q in ("qi", "qe", "qo", "qs1", "qa", "qb", "qy", "qr", "qg", "qv", "qf", "q23", "qc", "qd", "qs", "qp"))),
+        (f2, (("o256", 256), ("m256", 256), ("ID", 128), ("NID", 128), ("I4K", 128), ("W4K", 128), ("BDt", 128), ("BD", 128), ("BDv", 128), ("BDf", 128),
+              ("WT", 128), ("W64", 128), ("WY", 128), ("D15t", 128), ("D15", 128), ("Y15", 128), ("PERM", 256), ("SEGt", 256), ("SEG", 256), ("GBt", 8),
+              ("GB", 8), ("GBs", 8), ("E2t", 64), ("E2", 64), ("WD", 8), ("WZ0", 384), ("WZ1", 384), ("LM", 192), ("nmh", 384), ("AV", 384), ("GV", 128),
+              ("XF", 192), ("R1", 192), ("MM", 1920), ("MO", 1920))),
+        (b2, (("XS", 2048), ("ZL", 192), ("z0s", 192), ("IDb", 128), ("NIb", 128), ("I8b", 128), ("E2b", 64), ("ODt", 128), ("ODD", 128), ("sbh", 384),
+              ("CI", 256), ("EQD", 256), ("CJ", 256), ("MK", 256), ("WNa", 384), ("WNb", 384), ("WN", 384), ("WX", 24), ("WR", 24), ("WA", 24),
+              ("WPa", 128), ("WPb", 128), ("WPd", 128), ("WP", 384), ("WH", 384), ("M", 3072), ("R", 3072), ("MX", 3072), ("AB", 3072), ("PEN", 192),
+              ("PE0", 128), ("hi", 192), ("Ax", 1))),
+        (i4, (("ET", SP + 2048), ("v0s", 12), ("wts", 1), ("qI", 1), ("qJ", 1), ("qK", 1), ("RJ", 192), ("ui", 16), ("ua", 16), ("ud", 16), ("ue", 16))),
+        (u2, (("LT", 64 * HOPS), ("RL", 192), ("AL", 192), ("POS", 24), ("LD", 12)))):
+    for n_, w_ in tiles:
+        declare(n_, w_, t_)
 for c_ in (0, 1):
-    for n_, w_, t_ in (("sb", 128, b2), ("nm", 128, f2), ("Mn", 128, f4), ("dd", 128, f4), ("ee", 128, f4), ("oo", 128, f4), ("t1", 8, f4), ("t2", 8, f4),
-                       ("fin", 8, f4), ("WF", 128, f2), ("WS", 128, b2), ("FL", 256, f4), ("ne", 256, f4), ("dup", 256, f4), ("ys", 256, f4)):
+    for n_, w_, t_ in (("Ma", 128, f4), ("Mb", 128, f4), ("Mc", 128, f4), ("NF", 8, f4), ("NS", 128, f2), ("WF", 256, f2), ("eq", 256, f4), ("dup", 256, f4)):
         declare(n_ + str(c_), w_, t_)
 for b_ in range(8):
     SCRATCH["pb%d" % b_] = ("psum", [128, 512], f4)
     PLACE["pb%d" % b_] = ("pb%d" % b_, 0, 512)
-SEMAPHORES = ["cV", "cS", "cP", "cG", "sent"] + ["ld%d" % k for k in range(8)] + ["st%d" % k for k in range(3)] + \
-    ["a%s%d" % (m, t) for m in ("L0", "L1", "M0", "M1", "Z0", "Z1") for t in range(1, HOPS)]
+SEMAPHORES = ["cV", "cS", "cP", "cG", "sent"] + ["ld%d" % k for k in range(5)] + ["st%d" % k for k in range(3)] + \
+    ["a%s%d" % (m, t) for m in ("L0", "L1", "D0", "D1", "D", "M0", "Z0", "M1", "Z") for t in range(1, HOPS)]
 ORDER = []
 
 
@@ -90,7 +88,7 @@ def make(g, T):
     eng = {"V": g.vector, "S": g.scalar, "P": g.tensor, "G": g, "Y": g.sync}
     cnt = {"V": 0, "S": 0, "P": 0, "G": 0}
     clk = {q: {} for q in eng}
-    snap, acc, plan, sends = {}, {}, [], {}
+    snap, acc, plan, sends, first = {}, {}, [], {}, []
 
     def semof(r):
         return T.sem["c" + r] if r in cnt else T.sem[r]
@@ -151,8 +149,10 @@ def make(g, T):
             return max(min(64, size(ins[0])), size(ins[1])) * (PE if narrow(ins[0]) else 4 * PE)
         if q == "G":
             return 150 + 2 * size(o)
+        if kind == "load":
+            return 2000
         if kind == "scatter":
-            return 60 + SCATTER * size(ins[0]) + (1600 if q == "S" and not any(x[0] == q and x[3][-1][0] == "RT" and x[4][0][0] == "FT" for x in plan if x[3]) else 0)
+            return 60 + SCATTER * size(ins[0])
         if ins and len(ins[0][1]) > 1:
             return 60 + GATHER * size(o)
         if kind == "two":
@@ -172,7 +172,7 @@ def make(g, T):
             snap[(q, n)] = dict(clk[q])
             snap[(q, n)][q] = n - 1
             note(q, n, reads, writes)
-        plan.append((q, cycles(q, outs[0], ins, kind), 0, reads, writes, emit, None))
+        plan.append((q, cycles(q, outs[0], ins, kind), 0, reads, writes, emit, kind if q == "P" else None))
 
     def sc(x):
         return x[0] if isinstance(x, tuple) else x
@@ -196,11 +196,11 @@ def make(g, T):
     def fill(o, c): op("V", lambda: eng["V"].memset(o[0], c), [o], [])
     def act(o, a, f=F.Copy, scale=1.0, bias=0.0, total=None):
         if total is None:
-            op("S", lambda: eng["S"].activation(o[0], a[0], f, bias=sc(bias), scale=sc(scale)), [o], [a] + tl(bias, scale))
+            op("S", lambda: eng["S"].activation(o[0], a[0], f, bias=sc(bias), scale=sc(scale)), [o], [a] + tl(bias, scale), "load" if f == F.Silu else None)
         else:
             op("S", lambda: eng["S"].activation(o[0], a[0], f, bias=sc(bias), scale=sc(scale), accum_out=total[0]), [o, total], [a] + tl(bias, scale))
     def mm(o, l, r, st=True, sp=True):
-        op("P", lambda: eng["P"].matmul(o[0], l[0], r[0], st, sp), [o if st and sp else B(o[1][0][0])], [l, r])
+        op("P", lambda: eng["P"].matmul(o[0], l[0], r[0], st, sp), [o if st and sp else B(o[1][0][0])], [l, r], None if st or sp else "free")
     def iota(o, pat, base, cm, whole=False):
         if whole:
             op("G", lambda: g.iota(o[0], pat, base, cm), [o], [])
@@ -243,12 +243,11 @@ def make(g, T):
                 arrive=arrive, send=send, issue=issue, cnt=cnt)
 
 
-def order(plan):
-    n = len(plan)
+def needs(plan):
     pred, acc, bank = [], {}, {}
     for i, (q, cost, lag, reads, writes, emit, after) in enumerate(plan):
-        p = {}
-        for regs, w in ((reads, False), (writes, True)):
+        p, free = {}, after == "free"
+        for regs, w in ((reads, False), ([] if free else writes, True)):
             for reg in regs:
                 for (j, old, rw) in acc.get(reg[0], ()):
                     if (w or rw) and meet(reg, old):
@@ -256,16 +255,22 @@ def order(plan):
                         p[j] = max(p.get(j, 0), d + plan[j][2])
         if q in ("P", "Y"):
             b = writes[0][0] if q == "P" else q
-            if b in bank:
-                p.setdefault(bank[b], 0)
-            bank[b] = i
-        if after is not None:
+            for j in bank.get(b, [])[:1 if free else None]:
+                p.setdefault(j, 0)
+            bank[b] = bank[b] + [i] if free else [i]
+        elif after is not None:
             p[after] = plan[after][2]
         pred.append(p)
-        for reg in writes:
+        for reg in [] if free else writes:
             acc[reg[0]] = [x for x in acc.get(reg[0], []) if not covers(reg, x[1])] + [(i, reg, True)]
         for reg in reads:
             acc.setdefault(reg[0], []).append((i, reg, False))
+    return pred
+
+
+def order(plan):
+    n = len(plan)
+    pred = needs(plan)
     succ = [{} for _ in plan]
     for i in range(n):
         for j, d in pred[i].items():
@@ -320,15 +325,12 @@ def order(plan):
         return max(end[i] + tail[i] for i in range(n)), out, end
 
     none, lag = [0] * n, [x[2] for x in plan]
-    soon = {max(range(n), key=lambda i: plan[i][1] if plan[i][0] == "S" else 0)}
-    for i in range(n - 1, -1, -1):
-        if i in soon:
-            soon.update(pred[i])
+    soon = max(range(n), key=lambda i: plan[i][1] if plan[i][0] == "S" else 0)
     best = run(pred, succ, [-i for i in range(n)], none, lag)
     for _ in range(ROUNDS):
         for f in (run, lay):
             back = f(succ, pred, best[2], lag, none)[2]
-            best = min(best, f(pred, succ, [back[i] + (max(back) if i in soon else 0) for i in range(n)], none, lag))
+            best = min(best, f(pred, succ, [back[i] + (max(back) if i == soon else 0) for i in range(n)], none, lag))
     return best[1]
 
 
@@ -341,24 +343,32 @@ def rank_program(g, core, T, topo):
         "B", "I", "tt", "ts", "cp", "scat", "scan", "fill", "act", "mm", "iota", "asel", "dma"))
     nxt = T.cores[(rank + 3) % len(T.cores)]
     prv_eng = len(topo.engines(T.cores[(rank + 1) % len(T.cores)], core))
-    ET, FT, FU, XS = B("ET", SP, SP + 2048), B("FT", 32, 2080), B("FU", 32, 2080), B("XS")
+    ET, FT, FU, XS = B("ET", SP, SP + 2048), B("FT"), B("FU"), B("XS")
 
-    def lin(name, o, a, scale, bias):
+    def lin(name, o, a, bias):
         if name in ONS:
-            act(o, a, scale=scale, bias=bias)
-        elif scale == 1.0:
-            ts(o, a, bias, None, A.add)
+            act(o, a, bias=bias)
         else:
-            ts(o, a, scale, bias, A.mult, A.add)
+            ts(o, a, bias, None, A.add)
 
-    def lst(buf, t, c, a=0, b=None):
-        o = 64 * t + 32 * c
-        return B(buf, o + a, o + (CHUNK[c][1] // 16 if b is None else b))
+    def lst(t, c, kind, a=0, b=None):
+        w = CHUNK[c][1] // 16
+        o = 64 * t + {"vm": 8 * c, "v": 24 + 16 * c - w, "vf": 24 + 16 * c - w, "f": 24 + 16 * c, "fm": 48 + 8 * c}[kind]
+        return B("LT", o + a, o + ((2 * w if kind == "vf" else w) if b is None else b))
 
     def msg(buf, t, c, j, j1=None):
         p0, n = CHUNK[c]
-        o = 576 * t + 3 * p0
+        o = 384 * t + 2 * p0
         return B(buf, o + n * j, o + n * (j + 1 if j1 is None else j1))
+
+    def parts(m, t):
+        if m[0] == "L":
+            return lst(t + 1, int(m[1]), "v"), lst(t, int(m[1]), "f")
+        if m[0] == "D":
+            c, b = (int(m[1]), None) if m[1:] else (0, 12)
+            return lst(t + 1, c, "vm", 0, b), lst(t, c, "fm", 0, b)
+        a, b = {"M0": (0, NA), "Z0": (NA, 2 * NA), "M1": (2 * NA, 384), "Z": (NA, 384)}[m]
+        return B("MM", 384 * (t + 1) + a, 384 * (t + 1) + b), B("MO", 384 * t + a, 384 * t + b)
 
     def col(name, c, h=None):
         p0, n = CHUNK[c]
@@ -366,144 +376,166 @@ def rank_program(g, core, T, topo):
             return B(name, p0, p0 + n)
         return B(name, 2 * p0, 2 * p0 + 2 * n) if h == 2 else B(name, 2 * p0 + h * n, 2 * p0 + h * n + n)
 
-    def spread(c, l, r):
-        p0, n = CHUNK[c]
-        mm(B(SB[c], 0, 4 * n), B("ID"), B("CB", 4 * p0, 4 * p0 + 4 * n), True, False)
-        mm(B(SB[c], 2 * n, 4 * n), l, r, False, False)
-        mm(B(SB[c], 0, 2 * n), l, r, False, True)
+    def W(c, n, a=0, b=128, st=1):
+        return B(n, a, b, st, 0, CHUNK[c][1])
 
-    def dedupe(c, buf, t):
-        n, s = CHUNK[c][1], str(c)
-        fl, ne, dup, o = B("FL" + s, 0, 2 * n), B("ne" + s, 0, 2 * n), B("dup" + s, 0, 2 * n), 64 * t + 32 * c + n // 16
-        scan(fl, B("HOLD", 0, 2 * n), B(SB[c], 2 * n, 4 * n), 0.0, A.add, A.max)
-        tt(ne, B(SB[c], 0, 2 * n), fl, A.not_equal)
-        ts(lst(buf, t, c), B("FL" + s, 31, 2 * n, 32), -32.0, None, A.add)
-        scan(dup, ne, B(SB[c], 2 * n, 4 * n), 0.0, A.mult, A.max)
-        for h in (0, 1):
-            ts(B(buf, o + h, o + n // 16, 2), B("dup" + s, 31 + 32 * h, 2 * n, 64), B(("qi", "qi16")[h]), None, A.max)
+    def dedupe(c, t, kind):
+        n, s, bk = CHUNK[c][1], str(c), BANK["same"][c]
+        wf, wm = W(c, "WF" + s), W(c, "WF" + s, 128, 256)
+        mm(B(bk, 0, 2 * n), wf, W(c, "PERM", 0, 2 * n), True, False)
+        mm(B(bk, 0, 2 * n), wm, W(c, "SEG", 0, 2 * n), False, False)
+        mm(B(bk, 2 * n, 4 * n, 32), wm, W(c, "GBs", 0, n // 16), False, True)
+        eq, dup = B("eq" + s, 0, 2 * n), B("dup" + s, 0, 2 * n)
+        tt(eq, B(bk, 0, 2 * n), B("MK", 0, 2 * n), A.is_equal)
+        scan(dup, eq, B(bk, 2 * n, 4 * n), 0.0, A.max, A.min)
+        ts(lst(t, c, kind), B("dup" + s, 31, 2 * n, 32), 4096.0, None, A.mult)
 
-    def marks(q, tab, val, v0, buf, t, c):
+    def marks(q, tab, val, v0, t, c, kind):
         p0, n = CHUNK[c]
         for b in range(n // 32 - 1, -1, -1):
-            scat(q, B(tab), lst(buf, t, c, n // 16 + 2 * b, n // 16 + 2 * b + 2), B(val, v0 + p0 + 32 * b, v0 + p0 + 32 * b + 32))
+            scat(q, B(tab), lst(t, c, kind, 2 * b, 2 * b + 2), B(val, v0 + p0 + 32 * b, v0 + p0 + 32 * b + 32))
+
+    def row(c, o, t):
+        n = CHUNK[c][1]
+        ps = B(BANK["row"][c], 0, n)
+        mm(ps, W(c, "NS%d" % c), W(c, "ID", 0, n))
+        act(o, ps, F.Identity, scale=B("qr"), bias=B("QS", t + 1, t + 2))
 
     dma("Y", "ld0", T.v0s[:], T.v0[:], [B("v0s")], [])
-    QW = 2048
-    for j in range(1):
-        dma("Y", "ld%d" % (3 + j), T.ET[:, SP + j * QW:SP + (j + 1) * QW], T.en[:, j * QW:(j + 1) * QW], [B("ET", SP + j * QW, SP + (j + 1) * QW)], [])
+    dma("Y", "ld3", T.ET[:, SP:SP + 2048], T.en[:], [ET], [])
     dma("S", "ld1", T.z0s[:], T.z0[:], [B("z0s")], [])
     dma("S", "ld2", T.wts[:], T.wt[:], [B("wts")], [])
-    dma("Y", "ld7", T.XS[:], T.xs[:], [B("XS")], [])
+    dma("Y", "ld4", T.XS[:], T.xs[:], [B("XS")], [])
 
-    fill(B("o256"), 1.0); fill(B("onef"), 1.0); fill(B("pb6", 192, 208), 0.0)
-    for n, v in (("C32", 32.0), ("fin0", 0.0), ("fin1", 0.0), ("RST", -1.0e20), ("WNa", -128 * U), ("HOLD", 0.0)):
+    def q(i):
+        return B("EQD", i, i + 1)
+
+    def mul(o, a, s1, s2=None):
+        if s2 is None:
+            ts(o, a, s1, None, A.mult)
+        else:
+            ts(o, a, s1, s2, A.mult, A.mult)
+
+    for n, v in (("o256", 1.0), ("m256", -1.0), ("WNa", 128 * U), ("NS0", 0.0), ("NS1", 0.0), ("NF1", 0.0)):
+        fill(B(n), v)
+    fill(B("pb6", 192, 208), 0.0); fill(B("FT", 1024, 2080), 2048.0)
+    for a in range(0, 1024, 256):
+        act(B("FT", a, a + 256), B("o256"), F.Copy if a else F.Silu, scale=2048.0)
+    for n, v in (("onef", 1.0), ("C32", 32.0), ("RSA", -1.0e20), ("RSB", -1.0e20), ("RSC", -1.0e20)):
         act(B(n), B("o256", 0, PLACE[n][2]), scale=v)
     for a in (0, 192):
         act(B("RSP", a, a + 192), B("o256", 0, 192), scale=1.0e6)
-    for c in (0, 1):
-        act(B("CB", 4 * CHUNK[c][0], 4 * CHUNK[c][0] + 2 * CHUNK[c][1]), B("o256", 0, 2 * CHUNK[c][1]), scale=32.0)
-    act(B("RST", 0, 128, 16), B("onef", 0, 8), scale=1.0e20)
-    act(B("HOLD", 0, 256, 32), B("onef", 0, 8), scale=-8192.0)
     iota(B("qI"), [[0, 1]], 0, 1, True)
-    iota(B("CI"), [[0, 24], [1, 16]], 0, 0)
+    iota(B("CI"), [[0, 16], [1, 16]], 0, 0)
     iota(B("LI"), [[1, 12]], 0, 0)
     iota(B("RSi"), [[-16, 24]], -16 - 4096, 0)
+    iota(B("THR"), [[0, 2], [2048, 8]], int(BAR), 0)
     for j in range(4):
-        for a in (520 * j, 520 * j + 260):
-            if j < 2:
-                act(B("FT", a, a + 260), B("CI", 0, 260), scale=0.0, bias=2048.0)
-            else:
-                fill(B("FT", a, a + 260), 2048.0)
         iota(B("FU", 520 * j, 520 * j + 520), [[0, 520]], 2048, 0)
-    iota(B("CJ", 0, 64), [[-100, 2], [100, 2], [1, 16]], 0, 0)
-    iota(B("LK"), [[2, 6], [-1, 2]], 1, 0)
-    iota(B("LN"), [[2, 6], [0, 2], [-1, 2]], 1, 0)
-    asel(B("PERM"), B("o256"), [[-32, 4], [0, 2], [-1, 32]], A.is_equal, 0.0, 0, 1)
+    iota(B("CJ"), [[0, 4], [-16, 2], [1, 32]], -1, 0)
+    iota(B("CL"), [[0, 4], [16, 2], [0, 32]], 2048, 0)
+    asel(B("PERM"), B("o256"), [[-32, 4], [0, 2], [-1, 32]], A.is_equal, 0.0, 1, 1)
+    asel(B("SEGt"), B("m256"), [[-16, 8], [0, 32]], A.is_ge, 0.0, 0, 1)
+    asel(B("SEG"), B("SEGt"), [[16, 8], [0, 32]], A.is_ge, 0.0, 15, -1)
     for t in range(HOPS):
-        iota(B("VV", 192 * t, 192 * t + 192), [[64, 6], [-2, 32]], 1664 - 384 * t + 61, 0)
-        iota(B("VAL", 192 * t, 192 * t + 192), [[64, 6], [-2, 32]], 1664 - 384 * t + 62, 0)
-        if t > 0:
-            iota(B("CT", 384 * t, 384 * t + 384), [[0, 384]], 768 * t, 0)
+        iota(B("VV", 192 * t, 192 * t + 192), [[2, 192]], 1664 - 384 * t - 1, 0)
+        iota(B("VAL", 192 * t, 192 * t + 192), [[2, 192]], 1664 - 384 * t, 0)
+    iota(B("qp"), [[0, 1]], -2, -4)
     for c in (0, 1):
-        iota(col("CKt", c, 2), [[0, 2], [-128, CHUNK[c][1] // 32], [4, 32]], -2 * 1664 - 126 - 4 * CHUNK[c][0], 0)
+        act(B("NS%d" % c, 1, 128, 16), B("o256", 0, 8), scale=CC)
+        for i in (2, 3):
+            act(B("NS%d" % c, i, 128, 16), B("o256", 0, 8), F.Identity, scale=-4.0 * CHUNK[c][0], bias=B("qp"))
     asel(B("BDt"), B("o256", 0, 128), [[-16, 8], [0, 16]], A.is_ge, 0.0, 0, 1)
     asel(B("BD"), B("BDt"), [[16, 8], [0, 16]], A.is_ge, 0.0, 15, -1)
     asel(B("ID"), B("o256", 0, 128), [[-1, 128]], A.is_equal, 0.0, 0, 1)
-    if HALF < 2:
-        asel(B("SEL"), B("onef"), [[-1, 16], [-16, 8]], A.is_equal, 0.0, 0, 1)
+    asel(B("D15t"), B("o256", 0, 128), [[-1, 128]], A.is_equal, 0.0, 15, 1)
     for h in (0, 1):
         asel(B("SE2", 128 * h, 128 * h + 128), B("onef"), [[-1, 8], [-16, 8], [8 - 16 * (1 - h), 2]], A.is_equal, 0.0, -8 * h, 1)
     asel(B("E2t"), B("o256", 0, 64), [[-2, 64]], A.is_ge, 0.0, 0, 1)
     asel(B("E2"), B("E2t"), [[2, 64]], A.is_ge, 0.0, 1, -1)
     iota(B("ODt"), [[0, 8], [1, 2], [0, 8]], 0, 0)
-    asel(B("GBt"), B("onef", 0, 8), [[-16, 8]], A.is_ge, 0.0, 0, 1)
+    asel(B("GBt"), B("o256", 0, 8), [[-16, 8]], A.is_ge, 0.0, 0, 1)
     asel(B("GB"), B("GBt"), [[16, 8]], A.is_ge, 0.0, 15, -1)
-    asel(B("WNb"), B("WNa"), [[0, 16], [-16, 8]], A.is_ge, 0.0, 0, 1)
-    asel(B("WNa"), B("WNb"), [[0, 16], [16, 8]], A.is_ge, 0.0, 15, -1)
-    asel(B("WN"), B("WNa"), [[-1, 16], [-16, 8]], A.not_equal, -65536 * U, 0, 1)
-    ts(B("qJ"), B("qI"), 15, None, A.bitwise_and); cp(B("qi"), B("qJ")); act(B("wtf"), B("wts"))
-    ts(B("qK"), B("qJ"), 1, None, A.bitwise_and)
-    ts(B("qr"), B("qi"), -1.0, 15.0, A.mult, A.add)
-    act(B("qa"), B("qi"), bias=-15.5 - T0); act(B("qb"), B("qi"), scale=2.0 ** -18)
-    act(B("q15"), B("qi"), F.Relu, bias=-14.0); act(B("qe"), B("qK"), scale=-1.0, bias=1.0)
-    act(B("w1"), B("qe"), F.Identity, bias=B("q15")); act(B("qo"), B("w1"), scale=-1.0, bias=1.0)
-    ts(B("ODD"), B("ODt"), B("qe"), -2.0 ** 19, A.is_equal, A.mult); act(B("E2b"), B("E2"))
-    ts(B("EQD"), B("CI", 0, 256), B("qi"), None, A.is_equal); ts(B("EQR"), B("CI"), B("qr"), None, A.is_equal)
-    cp(B("LC"), B("LI")); cp(B("LD"), B("LK")); cp(B("LE"), B("LN")); ts(B("LP"), B("LK"), 16.0, B("qr"), A.mult, A.add)
-    ts(B("EQ2", 0, 64), B("CJ", 0, 64), B("qi"), None, A.is_equal); act(B("qi16"), B("qi"), bias=16.0)
+    asel(B("WNb"), B("WNa"), [[0, 48], [-16, 8]], A.is_ge, 0.0, 0, 1)
+    asel(B("WNa"), B("WNb"), [[0, 48], [16, 8]], A.is_ge, 0.0, 15, -1)
+    asel(B("WN"), B("WNa"), [[-1, 16], [0, 3], [-16, 8]], A.not_equal, 2.0 ** 26, 0, 1)
+    ts(B("qJ"), B("qI"), 15, None, A.bitwise_and); cp(B("qi"), B("qJ")); ts(B("qK"), B("qJ"), 1, None, A.bitwise_and)
+    ts(B("EQD"), B("CI"), B("qi"), None, A.is_equal)
+    ts(B("qb"), B("qi"), 1.0, 1 / 32, A.max, A.mult)
+    for n, a, s, b in (("wtf", B("wts"), 1.0, 0.0), ("qa", B("qi"), 2048.0, -2048 * (15.5 + T0)), ("qe", B("qK"), -1.0, 1.0), ("qs1", B("qi"), 1.0, 1.0),
+                       ("qr", q(1), -31 / 32, 1.0), ("qg", q(0), -32 * U, 32 * U), ("qc", q(1), T0 - CC / 32, 0.0)):
+        act(B(n), a, scale=s, bias=b)
+    for n, a, s, b in (("qy", q(1), 2048.0, q(0)), ("qv", q(3), 4096.0, q(0)), ("qf", q(2), 4096.0, q(0)), ("q23", q(2), 1.0, q(3)),
+                       ("qd", q(2), -4096.0, B("qc")), ("qs", q(3), -3328.0, B("qd"))):
+        act(B(n), a, F.Identity, scale=s, bias=b)
+    ts(B("qo"), B("qK"), q(15), None, A.subtract); act(B("q23"), B("q23"), scale=768.0)
+    ts(B("QS"), B("LI", 0, 6), B("q23"), B("qs"), A.mult, A.add)
+    ts(B("ODD"), B("ODt"), B("qe"), 2.0 ** 45, A.is_equal, A.mult)
+    cp(B("LD"), B("LI"))
+    ts(B("MK"), B("CJ"), B("qi"), 4096.0, A.is_ge, A.mult)
+    for c in (0, 1):
+        n = CHUNK[c][1]
+        ts(B(BANK["same"][c], 2 * n, 4 * n), B("CL", 0, 2 * n), B("qi"), 1 / 4096, A.add, A.mult)
+    for n in ("PERM", "SEG"):
+        act(B(n, 0, 256, 32), B("o256", 0, 8), scale=0.0)
     act(B("RSP", 0, 384, 16), B("RSi"), F.Identity, bias=B("qi"))
-    act(B("CKu"), B("EQD"), scale=2.0)
+    act(B("RSB", 0, 128, 16), B("THR", 0, 8)); act(B("RSC", 0, 128, 16), B("THR", 0, 8), bias=CC)
+    for n, a, v in (("IDb", "ID", 1.0), ("NIb", "ID", -1.0), ("NID", "ID", -1.0), ("I4K", "ID", 4096.0), ("W4K", "ID", -4096.0), ("I8b", "ID", 8192.0),
+                    ("WPd", "ID", B("qg")), ("BDv", "BD", B("qv")), ("BDf", "BD", B("qf")), ("WY", "BD", B("qy")), ("D15", "D15t", q(0)), ("E2b", "E2", 1 / 64)):
+        mul(B(n), B(a), v)
+    for n, i, v in (("WT", 1, 2048.0), ("W64", 1, -64.0), ("Y15", 0, 16.0), ("WPa", 1, -32768.0), ("WPb", 0, -31 * 2.0 ** 24)):
+        mul(B(n), B("BD"), q(i), v)
+    mul(B("PE0"), B("o256", 0, 128), B("qb"))
+    tt(B("WP", 128, 256), B("WPb"), B("WPd"), A.add); tt(B("WP", 0, 128), B("WP", 128, 256), B("WPa"), A.add); cp(B("WP", 256, 384), B("WP", 128, 256))
+    for j in range(3):
+        mul(B("WH", 128 * j, 128 * j + 128), B("ID"), -1.0)
+    for n, v in (("WX", 1 / 4), ("WR", -1 / 8), ("WA", 1 / 8)):
+        act(B(n), B("WNa", 0, 24), scale=v)
+    act(B("WD"), B("GB"), scale=B("wtf")); act(B("GBs"), B("GB"), scale=1 / 4096)
     for c in (0, 1):
-        for a in range(4 * CHUNK[c][0] + 2 * CHUNK[c][1], 4 * (CHUNK[c][0] + CHUNK[c][1]), 64):
-            act(B("CB", a, a + 64), B("EQ2", 0, 64), scale=4096.0, bias=-4064.0)
-        tt(col("CK", c, 2), col("CKt", c, 2), B("CKu", 0, 2 * CHUNK[c][1]), A.add)
-    for n, v in (("I2K", 2048.0), ("I37", 2.0 ** 18 * U), ("IDb", 1.0), ("NID", -1.0), ("N64", -64.0), ("I4K", 4096.0), ("I4b", 4096.0),
-                 ("DE", B("qe")), ("DO", B("qo")), ("D15", B("q15"))):
-        act(B(n), B("ID"), scale=v)
-    for n, v in (("WX", 32 * U), ("WR", -16 * U), ("WA", 16 * U), ("WD", B("wtf"))):
-        act(B(n), B("GB"), scale=v)
-    for c in (0, 1):
-        if 0 < KS[c] < 16 // WD:
-            act(B("WZt"), B("BD"), scale=16 * U)
-            asel(B("WZ%d" % c), B("WZt"), [[0, 8 * WD], [-1, 16 // WD]], A.is_ge, 0.0, KS[c] - 1, 0)
+        if KS[c] < 16 // WD:
+            for j in range(3):
+                mul(B("WZ%d" % c, 128 * j, 128 * j + 128), B("BD"), -16 * U)
+            if KS[c]:
+                asel(B("WZ%d" % c), B("WZ%d" % c), [[0, 24 * WD], [1, 16 // WD]], A.is_ge, 0.0, -KS[c], 0)
     for t in range(HOPS - 1):
-        act(B("BT", t, t + 1), B("q15"), scale=2048.0 * (9 + t))
-    act(B("qs1"), B("qi"), bias=1.0); act(B("qy15"), B("q15"), scale=16.0)
-    act(B("YW"), B("BD"), scale=B("qs1")); act(B("Y15"), B("BD"), scale=B("qy15"))
-    act(B("YE"), B("YW"), scale=B("qe")); act(B("YO"), B("YW"), scale=B("qo"))
+        act(B("BT", t, t + 1), q(15), scale=2048.0 * (9 + t))
+    for n, a, v in (("DE", "ID", "qe"), ("DO", "ID", "qo"), ("YW", "BD", "qs1"), ("YE", "YW", "qe"), ("YO", "YW", "qo")):
+        act(B(n), B(a), scale=B(v))
 
-    cp(B("v0f", 0, 12), B("v0s"))
-    tt(B("LM"), I(B("v0f"), B("LD")), B("EQR", 0, 192), A.mult)
-    tt(B("LM2"), I(B("v0f"), B("LE")), B("EQR"), A.mult)
+    cp(B("v0f"), B("v0s"))
+    tt(B("LM"), I(B("v0f"), B("LD")), B("EQD", 0, 192), A.mult)
     for c in (0, 1):
-        act(msg("MM", 0, c, 1), B("o256", 0, CHUNK[c][1]), scale=T0)
-        spread(c, B("BD"), col("LM2", c, 2))
-        mm(col("pb4", c), B("BD"), col("LM", c))
-        act(msg("MM", 0, c, 0), col("pb4", c))
-        act(msg("MM", 0, c, 2), I(B("z0s"), B("LP", CHUNK[c][0] // 16, (CHUNK[c][0] + CHUNK[c][1]) // 16)))
-        dedupe(c, "RT", 0)
+        p0, n = CHUNK[c]
+        cp(lst(0, c, "v"), B("v0s", p0 // 16, (p0 + n) // 16))
+        bk = BANK["lst"][c]
+        mm(W(c, bk, 256, 384), col("LM", c), B("BD")); mm(W(c, bk, 384, 512), col("LM", c), B("ID"))
+        act(W(c, "WF%d" % c, 0, 256), W(c, bk, 256, 512))
+        act(W(c, "NS%d" % c, 0, 128, 16), W(c, "WF%d" % c, 0, 128, 16))
+        row(c, msg("MM", 0, c, 0), -1)
+        cp(msg("MM", 0, c, 1), col("z0s", c))
+        dedupe(c, 0, "vm")
 
     sent = 0
     for t in range(HOPS):
         last = t == HOPS - 1
-        base = 4096 - 512 * t
         if t > 0:
-            for c in (0, 1):
-                K["arrive"]("aL%d%d" % (c, t), prv_eng, lst("RT", t, c, 0, CHUNK[c][1] // 8))
-                K["arrive"]("aM%d%d" % (c, t), prv_eng, msg("MM", t, c, 0, 2 if SPLIT[c] else 3))
-                if SPLIT[c]:
-                    K["arrive"]("aZ%d%d" % (c, t), prv_eng, msg("MM", t, c, 2))
-
-        def W(c, n, a=0, b=128, st=1):
-            return B(n, a, b, st, 0, CHUNK[c][1])
+            for m in SENDS:
+                K["arrive"]("a%s%d" % (m, t), prv_eng, parts(m, t - 1)[0])
 
         def bc(name, c, k, st=16):
             return B(name, 16 * CHUNK[c][0] + k, 16 * (CHUNK[c][0] + CHUNK[c][1]), st)
 
+        def halves(c):
+            return range(CHUNK[c][0] // 64, (CHUNK[c][0] + CHUNK[c][1]) // 64)
+
+        def key(c, k):
+            return W(c, "pb%d" % (2 + c), k, 384, 16)
+
         def ring(c):
             p0, n = CHUNK[c]
             for p in range(0, n, RP):
-                ts(B("RJ", p0 + p, p0 + min(n, p + RP)), I(ET, lst("RT", t, c, p // 16, min(n, p + RP) // 16)), 2047, None, A.bitwise_and)
+                ts(B("RJ", p0 + p, p0 + min(n, p + RP)), I(ET, lst(t, c, "v", p // 16, min(n, p + RP) // 16)), 2047, None, A.bitwise_and)
                 cp(B("RL", p0 + p, p0 + min(n, p + RP)), B("RJ", p0 + p, p0 + min(n, p + RP)))
 
         def rings(q, a, b):
@@ -519,67 +551,59 @@ def rank_program(g, core, T, topo):
                 (cp if q == "V" else act)(B("R", 16 * p, 16 * min(b, p + PC)), I(XS, B("AL", p, min(b, p + PC))))
 
         def pick(c):
-            s, n = str(c), CHUNK[c][1]
-            if HALF > 1 - c:
-                hs = range(CHUNK[c][0] // 64, (CHUNK[c][0] + n) // 64)
-                for h in hs:
-                    bk, a = (("pb1", 128), ("pb0", 128), ("pb1", 256))[h]
-                    sb, nm = (B(x, 128 * h, 128 * h + 128) for x in ("sbh", "nmh"))
-                    mm(B(bk, a, a + 128), B("IDb"), B("ODD"), True, False)
-                    for k in range(8):
-                        i = (k + t) % 16
-                        mm(B(bk, a + k, a + 128, 8), B("X", 1024 * h + k, 1024 * h + 1024, 8), B("SE2", 16 * i, 16 * i + 16), False, k == 7)
-                    pm = B(PB or bk, 384, 512)
-                    ts(sb, B(bk, a, a + 128), 0.0, -1023.5, A.max, A.add)
-                    ts(pm, B(bk, a, a + 128), 0.0, None, A.max)
-                    tt(nm, pm, sb, A.subtract)
-                    mm(B("pb6", 64 * h, 64 * h + 64), nm, B("E2"))
-                    ts(B("AL", 64 * h, 64 * h + 64), B("pb6", 64 * h, 64 * h + 64), -1024.0, None, A.add)
-                for h in hs:
-                    o = B("pb" + s, 0, 128, 1, 64 * (h % 2), 64 * (h % 2) + 64)
-                    mm(o, B("E2"), B("nmh", 128 * h, 128 * h + 128), True, False)
-                    mm(o, B("E2b"), B("sbh", 128 * h, 128 * h + 128), False, True)
-                return
-            for k in range(16):
-                i = (k + t) % 16
-                mm(W(c, "pb" + s, k, 128, 16), bc("X", c, k), B("SEL", 8 * i, 8 * i + 8))
-            lin("sb", W(c, "sb" + s), W(c, "pb" + s), 1.0, -1023.5)
-            tt(W(c, "nm" + s), W(c, "pb" + s), W(c, "sb" + s), A.subtract)
-            mm(col("pb6", c), W(c, "nm" + s), W(c, "ID", 0, n))
-            cp(col("AL", c), col("pb6", c))
+            for h in halves(c):
+                bk = BANK["pick"][h]
+                sb, nm = (B(x, 128 * h, 128 * h + 128) for x in ("sbh", "nmh"))
+                mm(B(bk, 0, 128), B("IDb"), B("ODD"), True, False)
+                for k in range(8):
+                    i = (k + t) % 16
+                    mm(B(bk, k, 128, 8), B("X", 1024 * h + k, 1024 * h + 1024, 8), B("SE2", 16 * i, 16 * i + 16), False, False)
+                mm(B(bk, 0, 128), B("NIb"), B("ODD"), False, True)
+                lin("sb", sb, B(bk, 0, 128), -1023.5)
+                tt(nm, B(bk, 0, 128), sb, A.subtract)
+                mm(B("pb6", 64 * h, 64 * h + 64), nm, B("E2"))
+                ts(B("AL", 64 * h, 64 * h + 64), B("pb6", 64 * h, 64 * h + 64), -1024.0, None, A.add)
+            lin("hi", col("hi", c), col("pb6", c), HI - 1535.5)
 
-        def newer(c):
-            kk = "pb%d" % (2 + c)
-            bk, a, b = ("pb4", 0, WD * NA) if c == 0 else (TB, 256, 256 + WD * (192 - NA))
+        def older(c):
+            n, bk = CHUNK[c][1], BANK["thr"][c]
+            a = 512 - WD * n
             if t > 0:
                 for m in range(WD):
-                    mm(B(bk, a + m, b, WD), B("I2K"), msg("MM", t, c, 1))
-            ts(col("PEN", c), msg("MM", t, c, 1), B("qa"), B("qb"), A.add, A.max)
-            mm(W(c, kk), col("PEN", c), B("I37"), True, False)
+                    mm(B(bk, a + m, 512, WD), B("WT"), msg("MM", t, c, 0))
+                ts(col("PEN", c), B(bk, a, 512, WD), B("qa"), B("qb"), A.add, A.max)
+            mm(W(c, "pb%d" % (2 + c), 0, 384), col("PEN", c) if t else B("PE0", 0, n), B("WP"), True, False)
             for j in range(16 // WD):
                 if t > 0:
-                    tt(bc("M", c, j, 16 // WD), bc("X", c, j, 16 // WD), B(bk, a, b), A.is_ge)
+                    tt(bc("M", c, j, 16 // WD), bc("X", c, j, 16 // WD), B(bk, a, 512), A.is_lt)
                 else:
-                    ts(bc("M", c, j, 16 // WD), bc("X", c, j, 16 // WD), 2048 * T0, None, A.is_ge)
+                    ts(bc("M", c, j, 16 // WD), bc("X", c, j, 16 // WD), 2048 * T0, None, A.is_lt)
                 for k in range(j, 16, 16 // WD):
                     i = (k + t) % 16
-                    mm(W(c, kk, k, 128, 16), bc("M", c, k), B("WN", 8 * i, 8 * i + 8), False, False)
+                    mm(key(c, k), bc("M", c, k), B("WN", 24 * i, 24 * i + 24), False, False)
+
+        def entry(c, name, a, w, stop=False):
+            for h in halves(c):
+                mm(B("pb%d" % (2 + c), a, a + 128, 1, 64 * (h % 2), 64 * (h % 2) + 64), B(w), B(name, 128 * h, 128 * h + 128), False, stop)
 
         def sizes(c):
             p0, n = CHUNK[c]
-            kk, J, z = "pb%d" % (2 + c), 16 // WD, msg("MM", t, c, 2)
-            bk, a = ("pb4", 0) if c == 0 else ("pb6", 256)
+            kk, J, z = W(c, "pb%d" % (2 + c), 0, 384), 16 // WD, msg("MM", t, c, 1)
+            bk, a = BANK["zz"][c], 512 - WD * n
             ks, m, sums = [k for k in range(16) if k % J < KS[c]], 512 // n, []
-            if 0 < KS[c] < J:
-                mm(W(c, kk), z, B("WZ%d" % c), False, False)
-            if KS[c] < J:
+            mm(kk, col("hi", c), B("WH"), False, False)
+            entry(c, "sbh", 256, "E2b")
+            if KS[c] == J:
+                entry(c, "nmh", 0, "E2")
+            else:
+                mm(kk, z, B("WZ%d" % c), False, False)
                 for j in range(WD):
-                    mm(B(bk, a + j, a + WD * n, WD), B("ID"), z)
+                    mm(B(bk, a + j, 512, WD), B("ID"), z)
             for k in range(16):
                 if k not in ks:
-                    mm(W(c, kk, k, 128, 16), bc("R", c, k), B("WR"), False, False)
+                    mm(key(c, k), bc("R", c, k), B("WR"), False, False)
             for x in range(max(J - KS[c], -(-len(ks) // m))):
-                part, db = ks[m * x:m * x + m], DB[(x + c * KS[0]) % 2]
+                part, db = ks[m * x:m * x + m], BANK["diff"][(x + c * KS[0]) % 2]
                 for j, k in enumerate(part):
                     mm(B(db, j * n, j * n + n), B("NID"), z, j == 0, False)
                 for j, k in enumerate(part):
@@ -588,25 +612,17 @@ def rank_program(g, core, T, topo):
                 if part:
                     act(B("AB", o, o + len(part) * n), B(db, 0, len(part) * n), F.Abs)
                 if KS[c] + x < J:
-                    tt(bc("MX", c, KS[c] + x, J), bc("R", c, KS[c] + x, J), B(bk, a, a + WD * n), A.max)
+                    tt(bc("MX", c, KS[c] + x, J), bc("R", c, KS[c] + x, J), B(bk, a, 512), A.max)
                     sums += [(k, bc("MX", c, k), "WX") for k in range(KS[c] + x, 16, J)]
                 sums += [(k, B("AB", o + j * n, o + j * n + n), "WA") for j, k in enumerate(part)]
             for k, d, w in sums:
-                mm(W(c, kk, k, 128, 16), d, B(w), False, k == sums[-1][0])
-
-        def fused(c):
-            p0, n = CHUNK[c]
-            for k in range(16):
-                asel(bc("ZE", c, k), msg("MM", t, c, 2), [[0, n]], A.is_equal, 0.0, 0, 0)
-            for p in range(p0, p0 + n, FUSE):
-                tt(B("D", 16 * p, 16 * (p + FUSE)), I(XS, B("AL", p, p + FUSE)), B("ZE", 16 * p, 16 * (p + FUSE)), A.subtract)
-                act(B("AB", 16 * p, 16 * (p + FUSE)), B("D", 16 * p, 16 * (p + FUSE)), F.Abs)
-            for k in range(16):
-                mm(W(c, "pb%d" % (2 + c), k, 128, 16), bc("AB", c, k), B("WA"), False, k == 15)
+                mm(key(c, k), d, B(w), False, KS[c] == J and k == sums[-1][0])
+            if KS[c] < J:
+                entry(c, "nmh", 0, "E2", True)
 
         def hash_():
             for c in (0, 1):
-                mm(W(c, "pb6", 192 + 8 * c, 200 + 8 * c), msg("MM", t, c, 2), B("WD"))
+                mm(W(c, "pb6", 192 + 8 * c, 200 + 8 * c), msg("MM", t, c, 1), B("WD"))
             cp(B("ui"), B("pb6", 192, 208))
             ts(B("ua"), B("ui"), 2047, None, A.bitwise_and)
             act(B("uc"), B("ua"), F.Square, bias=592.0)
@@ -617,84 +633,82 @@ def rank_program(g, core, T, topo):
             else:
                 ts(B("ud"), B("uc"), -592.0 ** 2, None, A.add)
             ts(B("ue"), B("ud"), 5, 2047, A.arith_shift_right, A.bitwise_and)
-            act(B("ff"), B("ue"), bias=-B1)
+            tt(B("RSA", 0, 256, 16), B("THR"), B("ue"), A.add)
 
         def least(c):
-            s = str(c)
-            kk, pp = W(c, "pb%d" % (2 + c)), W(c, "pb" + s)
-            mn, dd, ee, oo = (W(c, n + s) for n in ("Mn", "dd", "ee", "oo"))
-            t1, t2, fin = (W(c, n + s, 0, 8) for n in ("t1", "t2", "fin"))
-            scan(mn, W(c, "RST"), kk, 0.0, A.max, A.min)
-            tt(dd, kk, mn, A.subtract)
-            lin("t1", t1, W(c, "Mn" + s, 15, 128, 16), -1.0, -16384 * U)
-            tt(ee, pp, dd, A.subtract)
-            tt(t2, t1, W(c, "ff", 8 * c, 8 * c + 8), A.max)
-            scan(oo, dd, ee, 0.0, A.min, A.max)
-            tt(fin, W(c, "oo" + s, 15, 128, 16), t2, A.min)
-            wide = I(B("fin" + s), B("LC", 0, 8))
-            lin("WS", B("WS" + s), wide, 1.0, -1023.5)
-            tt(B("WF" + s), wide, B("WS" + s), A.subtract)
-
-        def turn(c):
-            n = CHUNK[c][1]
-            spread(c, W(c, "WF%d" % c), W(c, "PERM", 0, 2 * n))
-            mm(B("pb4", 0, n), W(c, "WF%d" % c), W(c, "ID", 0, n))
-            mm(B("pb4", n, 2 * n), W(c, "WS%d" % c), W(c, "IDb", 0, n))
-            act(msg("MO", t, c, 0), B("pb4", 0, n))
-            act(msg("MO", t, c, 1), B("pb4", n, 2 * n), F.Abs, scale=1.0 / 2048, bias=1.0)
+            s, kk = str(c), "pb%d" % (2 + c)
+            ma, mb, mc = (W(c, x + s, 15, 128, 16) for x in ("Ma", "Mb", "Mc"))
+            wide = I(B("NF" + s), B("LD", 0, 8))
+            scan(W(c, "Ma" + s), W(c, "RSA", 128 * c, 128 * c + 128), W(c, kk), 0.0, A.max, A.min)
+            scan(W(c, "Mb" + s), W(c, "RSB"), W(c, kk, 128, 256), 0.0, A.max, A.min)
+            tt(W(c, "NF" + s, 0, 8), ma, mb, A.subtract)
+            act(B("WF" + s, 0, 128), wide)
+            tt(B("WF" + s, 128, 256), wide, B("EQD", 0, 128), A.mult)
+            scan(W(c, "Mc" + s), W(c, "RSC"), W(c, kk, 256, 384), 0.0, A.max, A.min)
+            if "ns" in ONS:
+                act(W(c, "NS" + s, 0, 128, 16), W(c, "NF" + s, 0, 8))
+            else:
+                tt(W(c, "NS" + s, 0, 128, 16), ma, mb, A.subtract)
+            tt(W(c, "NS" + s, 1, 128, 16), mc, mb, A.subtract)
+            o = B(BANK["lst"][c], 240, 240 + CHUNK[c][1] // 16)
+            mm(o, W(c, "WF" + s, 128, 256), W(c, "GB", 0, CHUNK[c][1] // 16))
+            cp(lst(t, c, "f"), o)
+            row(c, msg("MO", t, c, 0), t)
 
         def zproc(c):
-            n = CHUNK[c][1]
-            p1, p2 = B("pb4", 256, 256 + n), B("pb4", 384, 384 + n)
-            act(col("XF", c), I(XS, lst("OT", t, c)))
-            mm(p1, B("N64"), msg("MO", t, c, 1), True, False)
+            n, bk = CHUNK[c][1], BANK["zp"][c]
+            p1, p2 = B(bk, 256, 256 + n), B(bk, 384, 384 + n)
+            act(col("XF", c), I(XS, lst(t, c, "f")))
+            mm(p1, B("W64"), msg("MO", t, c, 0), True, False)
             mm(p1, B("ID"), col("XF", c), False, True)
             act(col("R1", c), p1, F.Relu, bias=64 * T0)
-            mm(p2, B("ID"), msg("MM", t, c, 2), True, False)
+            mm(p2, B("ID"), msg("MM", t, c, 1), True, False)
             mm(p2, B("NID"), col("R1", c), False, True)
-            act(col("ZL", c) if last else msg("MO", t, c, 2), p2, F.Abs)
+            act(col("ZL", c) if last else msg("MO", t, c, 1), p2, F.Abs)
 
         def meetings(c):
             p0, n = CHUNK[c]
-            vl, fl = lst("RT", t, c), lst("OT", t, c)
             wo, we, w15 = ("YO", "YE", "Y15") if last else ("DO", "DE", "D15")
+            bk = BANK["new"][c]
             for h, (own, oth, new) in enumerate((("Rv", "Rf", "MO"), ("Rf", "Rv", "MM"))):
-                o = B("pb%d" % c, n * h, n * h + n)
-                mm(o, B(w15), msg(new, t, c, 0), True, False)
-                for w, r in sorted(((wo, own), (we, oth)), key=lambda x: x[1] == "Rf"):
-                    mm(o, B(w), col(r, c), False, r == "Rf")
-            act(col("NN", c, 2), B("pb%d" % c, 0, 2 * n), F.Identity, bias=16 * 2048.0 * (9 + t) if last else B("BT", t, t + 1))
-            tt(col("PRE", c), I(FU if c else FT, fl), B("VAL", 192 * t + p0, 192 * t + p0 + n), A.min)
-            if c == 0:
-                marks(MQ[c], "FT", "PRE", 0, "OT", t, c)
-                lin("av", col("av", c), I(FT, vl), 1.0, 0.0)
-                lin("af", col("af", c), I(FT, fl), 1.0, 0.0)
+                o = B(bk, n * h, n * h + n)
+                mm(o, B(w15), msg(new, t, c, 0), h == 0, False)
+                mm(o, B(wo), col(own, c), False, False)
+                mm(o, B(we), col(oth, c), False, h == 1)
+            act(col("NN", c, 2), B(bk, 0, 2 * n), F.Identity, bias=16 * 2048.0 * (9 + t) if last else B("BT", t, t + 1))
+            tt(col("PRE", c), I(FU if c else FT, lst(t, c, "f")), B("VAL", 192 * t + p0, 192 * t + p0 + n), A.min)
+            marks(MQ[c], "FU" if c else "FT", "PRE", 0, t, c, "fm")
+            if "av%d" % c in ONS:
+                act(col("AV", c, 2), I(FU if c else FT, lst(t, c, "vf")))
             else:
-                marks(MQ[c], "FU", "PRE", 0, "OT", t, c)
-                lin("g1", B("GV", 0, n), I(FT, vl), 1.0, 0.0); lin("g2", B("GV", n, 2 * n), I(FT, fl), 1.0, 0.0)
-                tt(col("av", c), I(FU, vl), B("GV", 0, n), A.min)
-                tt(col("af", c), I(FU, fl), B("GV", n, 2 * n), A.min)
+                tt(col("AV", c, 2), I(FU if c else FT, lst(t, c, "vf")), B("EQD", 0, 2 * n), A.add)
+            if c:
+                top = 1664.0 - 384 * t + 2 * NA
+                if "gv" in ONS:
+                    act(B("GV"), I(FT, lst(t, c, "vf")), F.Relu, scale=-1.0, bias=top)
+                else:
+                    ts(B("GV"), I(FT, lst(t, c, "vf")), top, 4096.0, A.is_lt, A.mult)
 
-        def stand():
-            mm(B("pb2", 0, 384), B("I4K"), B("CK"), True, False)
-            if t > 0:
-                mm(B("pb2", 0, 384), B("I4b"), B("CT", 384 * t, 384 * t + 384), False, False)
-            for h, m in enumerate(("MM", "MO")):
-                for c in (0, 1):
-                    mm(col("pb2", c, h), B("ID"), msg(m, t, c, 0), False, False)
-            for c in (0, 1):
-                for a in ("av", "af"):
-                    for h in (0, 1):
-                        mm(col("pb2", c, h), B("I4K"), col(a, c), False, (c, a, h) == (1, "af", 1))
-            scan(B("ysa"), B("RSP"), B("pb2", 0, 384), 1.0e6, A.min, A.max)
-            ts(B("POS"), B("ysa", 15, 384, 16), SP + 4096.0, None, A.add)
-            scat("V", B("YS" if last else "ET"), B("POS"), B("NN"))
+        def stand(cs):
+            bk, a, b = "pb%d" % (2 + cs[0]), 2 * CHUNK[cs[0]][0], 2 * sum(CHUNK[cs[-1]])
+            terms = [(c, h, "I8b", B("EQD", 0, CHUNK[c][1])) for c in cs if "av%d" % c in ONS for h in (0, 1)]
+            terms += [(c, h, w, msg(m, t, c, 0)) for h, (w, m) in enumerate((("BDv", "MM"), ("BDf", "MO"))) for c in cs]
+            for c in cs:
+                if c:
+                    terms += [(c, h, "W4K" if "gv" in ONS else "NID", B("GV", 64 * x, 64 * x + 64)) for x in (0, 1) for h in (0, 1)]
+                terms += [(c, h, "I4K", col("AV", c, x)) for x in (0, 1) for h in (0, 1)]
+            for x, (c, h, w, r) in enumerate(terms):
+                mm(col(bk, c, h), B(w), r, x == 0, x == len(terms) - 1)
+            scan(B("ysa", a, b), B("RSP", a, b), B(bk, a, b), 1.0e6, A.min, A.max)
+            ts(B("POS", a // 16, b // 16), B("ysa", a + 15, b, 16), SP + 4096.0, None, A.add)
+            scat("V", B("YS" if last else "ET"), B("POS", a // 16, b // 16), B("NN", a, b))
 
-        def ysum(j, bk):
+        def ysum(j):
+            bk, ef, et = BANK["ys"][j], B("EF", 512 * j, 512 * j + 512), B("ET", SP + 512 * j, SP + 512 * j + 512)
             if j in EG:
-                asel(B("EF", 512 * j, 512 * j + 512), B("ET", SP + 512 * j, SP + 512 * j + 512), [[0, 512]], A.is_equal, 0.0, 0, 0)
+                asel(ef, et, [[0, 512]], A.is_equal, 0.0, 0, 0)
             else:
-                act(B("EF", 512 * j, 512 * j + 512), B("ET", SP + 512 * j, SP + 512 * j + 512))
+                act(ef, et)
             for a in range(0, 512, 128):
                 mm(B(bk, a, a + 128), B("YW"), B("EF", 512 * j + a, 512 * j + a + 128))
             act(B("YS", SP + 512 * j, SP + 512 * j + 512), B(bk))
@@ -703,50 +717,46 @@ def rank_program(g, core, T, topo):
         for h in range(3):
             rings("V", 64 * h, 64 * h + EV[h]); rings("S", 64 * h + EV[h], 64 * h + 64)
         for c in (0, 1):
-            act(col("Rv", c), I(ET, lst("RT", t, c)))
-            newer(c)
+            act(col("Rv", c), I(ET, lst(t, c, "v")))
+            older(c)
         pick(0); pick(1)
-        marks("S", "FT", "VV", 192 * t, "RT", t, 0); marks("S", "FU", "VV", 192 * t, "RT", t, 1)
-        for h in range(2 if FUSE else 3):
+        marks(MV[0], "FT", "VV", 192 * t, t, 0, "vm"); marks(MV[1], "FU", "VV", 192 * t, t, 1, "vm")
+        for h in range(3):
             records("V", 64 * h, 64 * h + RV[h]); records("S", 64 * h + RV[h], 64 * h + 64)
+        hash_(); sizes(0); sizes(1)
         if last:
             for j in range(YE):
-                ysum(j, ("pb7", "pb5")[j % 2])
-        hash_(); sizes(0); (fused if FUSE else sizes)(1)
+                ysum(j)
+        for c in (0, 1):
+            least(c); dedupe(c, t, "fm"); zproc(c)
+            act(col("Rf", c), I(ET, lst(t, c, "f")))
         if last:
             for j in range(YE, 4):
-                ysum(j, ("pb6", "pb5")[j % 2])
-        for c in (0, 1):
-            least(c); turn(c); dedupe(c, "OT", t)
-            if not last:
-                sent += K["send"](core, nxt, topo, lst("RT", t + 1, c, 0, CHUNK[c][1] // 8), lst("OT", t, c, 0, CHUNK[c][1] // 8), "aL%d%d" % (c, t + 1))
-            zproc(c)
-            if not last:
-                for m, a, b in (("M", 0, 2), ("Z", 2, 3)) if SPLIT[c] else (("M", 0, 3),):
-                    sent += K["send"](core, nxt, topo, msg("MM", t + 1, c, a, b), msg("MO", t, c, a, b), "a%s%d%d" % (m, c, t + 1))
-            act(col("Rf", c), I(ET, lst("OT", t, c)))
-        meetings(0); meetings(1); stand()
+                ysum(j)
+        else:
+            for m in SENDS:
+                sent += K["send"](core, nxt, topo, *parts(m, t), "a%s%d" % (m, t + 1))
+        meetings(0); meetings(1)
+        for cs in ((0,), (1,)) if APART else ((0, 1),):
+            stand(cs)
         if not last:
             for c in (0, 1):
-                act(W(c, "FC", 8 * c, 8 * c + 8), W(c, "WS%d" % c, 0, 128, 16), F.Relu, scale=-1.0, bias=1.0 - B1, total=W(c, "FA", c, c + 1))
+                act(W(c, "FC", 8 * c, 8 * c + 8), W(c, "NS%d" % c, 1, 128, 16), F.Relu, scale=-1 / 32, bias=1 + CC / 32, total=W(c, "FA", c, c + 1))
             for c in (0, 1):
                 mm(B("pb6", 208, 209), W(c, "C32"), W(c, "FA", c, c + 1), c == 0, c == 1)
 
     t = HOPS - 1
-    act(B("YZ"), I(B("ZL"), B("LP")))
-    dma("S", "st0", T.yz[:], T.YZ[:], [], [B("YZ")])
+    dma("S", "st0", T.yz[:], T.ZL[:], [], [B("ZL")])
     for c in (0, 1):
-        mm(col("pb5", c), B("ID"), msg("MO", t, c, 0), True, False)
-        mm(col("pb5", c), B("I2K"), msg("MO", t, c, 1), False, True)
-    act(B("YQ"), B("pb5", 0, 192), bias=-2048 * T0)
-    act(B("YP"), I(B("YQ"), B("LP")))
+        mm(col("pb4", c), B("WY"), msg("MO", t, c, 0))
+    act(B("YP"), B("pb4", 0, 192), bias=-2048 * T0)
     dma("S", "st1", T.yp[:], T.YP[0:128:16, :], [], [B("YP")])
     dma("Y", "st2", T.ys[:], T.YS[0:128:16, SP:SP + 2048], [], [B("YS")])
 
     K["issue"]()
-    for q in ("V", "S", "P", "G"):
-        g.wait_ge(T.sem["c" + q], K["cnt"][q])
-    for j in (0, 1, 2, 3, 7):
+    for q_ in ("V", "S", "P", "G"):
+        g.wait_ge(T.sem["c" + q_], K["cnt"][q_])
+    for j in range(5):
         g.wait_ge(T.sem["ld%d" % j], 16)
     for j in range(3):
         g.wait_ge(T.sem["st%d" % j], 16)

@@ -5,34 +5,41 @@ HOPS = 5
 NA = 128
 CHUNK = ((0, NA), (NA, 192 - NA))
 WD = 4
+MP, XP = 64, 64
 PC = 64
-SENDS = ("L0", "M0", "L1", "Z0", "M1", "D0", "D1")
-EV, RV = (32, 32, 0), (0, 32, 0)
+SENDS = ("L0", "M0", "L1", "Z0", "M1", "D")
+EV, RV = (32, 32, 0), (0, 16, 0)
 MQ = "SV"
 MV = "SS"
-ONS = ("av0", "av1", "ns")
+LQ = ("SV", "S")
+ONS = ("ns", "pen", "hi", "gv")
+ONG = ("C32", "RSB", "RSC")
+FV = 1568
 KS = (0, 4)
+FUSE = 0
 APART = 1
-EG = ()
-BANK = dict(pick=("pb0", "pb1", "pb7"), thr=("pb4", "pb5"), zz=("pb4", "pb6"), diff=("pb0", "pb1"), same=("pb7", "pb5"), lst=("pb0", "pb6"),
-            row=("pb1", "pb4"), zp=("pb4", "pb6"), new=("pb0", "pb1"), ys=("pb0", "pb1", "pb0", "pb1"))
+BANK = dict(ny="pb3", names=("pb0", "pb1", "pb7"), pick=("pb0", "pb1", "pb7"), thr=("pb4", "pb5"), zz=("pb4", "pb6"), diff=("pb0", "pb1"), same=(("pb5", 256, 0), ("pb7", 0, 192), ("pb7", 0, 352)), lst=("pb0", "pb1"),
+            row=("pb1", "pb4"), zp=(("pb4", 256, 384), ("pb5", 160, 416)), new=("pb0", "pb1"))
 SP = 384
-B0 = 2.0 ** 18 + 4096
+B0 = 2.0 ** 18 + 4096 - 512
 T0 = B0 / 2048 + 1
-U = 1792.0
-BAR = 243.0 * 2 ** 16
-CC = (B0 - 1024) / 64
+U = 1536.0
+BAR = 211.0 * 2 ** 16
+CC = B0 / 64
 HI = 1.5 * 2 ** 17
 PE, GATHER, SCATTER, FIX, OWN, CROSS, LAG, FAR = 0.64, 1.6, 3.5, 24, 230, 230, 2200, 4500
-FIRST = 2200
+FIRST, CALL = 2200, 800
 RP = 64
-YE = 1
+YT = ((3, 0), (3, 1), (3, 1), (3, 2), (3, 2), (4, 0), (4, 1), (4, 1))
+YN, YS = (4, 1), 128
 LW = 2
-ROUNDS = 3
+ALIKE = 0.4
+ROUNDS, STEPS, SLACK, LUMP = 8, 22000, 120, 350
+CASES = ((1, {"send": 1.1}), (0.75, {"gather": 1.2, "scatter": 1.4}))
 f4, f2, b2, i4, u2 = "float32", "float16", "bfloat16", "int32", "uint16"
 SCRATCH = {}
 OWNBUF = ("EF", "ET", "YS", "XS", "FT", "FU", "YP", "ZL", "v0s", "v0f", "z0s", "wts", "X", "M", "R", "MX", "AB", "VAL", "VV", "MM", "MO",
-          "LT", "RL", "AL", "POS", "NN", "PRE", "LD", "NF0", "NF1")
+          "LT", "RL", "AL", "POS", "PO3", "NY", "NN", "PRE", "LD", "LE", "dup0", "dup1", "dup2", "NF0", "NF1")
 PLACE = {}
 
 
@@ -48,31 +55,31 @@ def declare(name, w, t):
 
 
 for t_, tiles in (
-        (f4, (("EF", 2048), ("YS", SP + 2048), ("FT", 2080), ("FU", 2080), ("YP", 192), ("v0f", 12), ("X", 3072), ("NN", 384), ("PRE", 192),
-              ("VAL", 960), ("VV", 960), ("Rv", 192), ("Rf", 192), ("ysa", 384), ("onef", 128), ("SE2", 256), ("C32", 128), ("LI", 12), ("CL", 256),
+        (f4, (("EF", 2048), ("YS", SP + 2048), ("FT", 2112), ("FU", 2112), ("eq0", 160), ("eq1", 160), ("eq2", 160), ("dup0", 160), ("dup1", 160), ("dup2", 160), ("CD", 160), ("GB4", 4), ("YP", 192), ("v0f", 12), ("X", 3072), ("NN", 384), ("NY", 384), ("PRE", 192),
+              ("VAL", 960), ("VV", 960), ("Rv", 192), ("Rf", 192), ("ysa", 384), ("onef", 128), ("SE2", 256), ("C32", 128), ("LI", 12), ("GBf", 8),
               ("RSA", 256), ("RSB", 128), ("RSC", 128), ("THR", 16), ("RSP", 384), ("RSi", 24), ("QS", 6),
               ("DO", 128), ("DE", 128), ("YO", 128), ("YE", 128), ("YW", 128), ("BT", 5), ("uc", 16), ("Ay", 1), ("FC", 16), ("FA", 2), ("wtf", 1))
-         + tuple((q, 1) for q in ("qi", "qe", "qo", "qs1", "qa", "qb", "qy", "qr", "qg", "qv", "qf", "q23", "qc", "qd", "qs", "qp"))),
-        (f2, (("o256", 256), ("m256", 256), ("ID", 128), ("NID", 128), ("I4K", 128), ("W4K", 128), ("BDt", 128), ("BD", 128), ("BDv", 128), ("BDf", 128),
-              ("WT", 128), ("W64", 128), ("WY", 128), ("D15t", 128), ("D15", 128), ("Y15", 128), ("PERM", 256), ("SEGt", 256), ("SEG", 256), ("GBt", 8),
+         + tuple((q, 1) for q in ("qi", "qe", "qo", "qs1", "qa", "qb", "qy", "qr", "qg", "qv", "qf", "q23", "qc", "qd", "qs", "qp", "q64", "qx", "qw", "qu"))),
+        (f2, (("o256", 256), ("ID", 128), ("NID", 128), ("I4K", 128), ("W4K", 128), ("BDt", 128), ("BD", 128), ("BDv", 128), ("BDf", 128),
+              ("WT", 128), ("W64", 128), ("WY", 128), ("D15t", 128), ("D15", 128), ("Y15", 128), ("PERM", 160), ("SEG", 160), ("GBt", 8),
               ("GB", 8), ("GBs", 8), ("E2t", 64), ("E2", 64), ("WD", 8), ("WZ0", 384), ("WZ1", 384), ("LM", 192), ("nmh", 384), ("AV", 384), ("GV", 128),
               ("XF", 192), ("R1", 192), ("MM", 1920), ("MO", 1920))),
-        (b2, (("XS", 2048), ("ZL", 192), ("z0s", 192), ("IDb", 128), ("NIb", 128), ("I8b", 128), ("E2b", 64), ("ODt", 128), ("ODD", 128), ("sbh", 384),
-              ("CI", 256), ("EQD", 256), ("CJ", 256), ("MK", 256), ("WNa", 384), ("WNb", 384), ("WN", 384), ("WX", 24), ("WR", 24), ("WA", 24),
-              ("WPa", 128), ("WPb", 128), ("WPd", 128), ("WP", 384), ("WH", 384), ("M", 3072), ("R", 3072), ("MX", 3072), ("AB", 3072), ("PEN", 192),
-              ("PE0", 128), ("hi", 192), ("Ax", 1))),
-        (i4, (("ET", SP + 2048), ("v0s", 12), ("wts", 1), ("qI", 1), ("qJ", 1), ("qK", 1), ("RJ", 192), ("ui", 16), ("ua", 16), ("ud", 16), ("ue", 16))),
-        (u2, (("LT", 64 * HOPS), ("RL", 192), ("AL", 192), ("POS", 24), ("LD", 12)))):
+        (b2, (("XS", 2048), ("ZL", 192), ("z0s", 192), ("IDb", 128), ("NIb", 128), ("I8b", 128), ("I4b", 128), ("E2b", 64), ("ODt", 128), ("ODD", 128), ("sbh", 384),
+              ("CI", 256), ("EQD", 256), ("CJ", 64), ("CK", 64), ("MK", 160), ("WNa", 384), ("WNb", 384), ("WN", 384), ("WX", 24), ("WR", 24), ("WA", 24),
+              ("WPb", 128), ("WPd", 128), ("WP", 128), ("WH", 384), ("M", 3072), ("R", 3072), ("MX", 3072), ("AB", 3072), ("PEN", 192),
+              ("hi", 192), ("Ax", 1))),
+        (i4, (("ET", SP + 2048), ("v0s", 12), ("wts", 1), ("qI", 1), ("qJ", 1), ("qK", 1), ("qL", 1), ("RJ", 192), ("ui", 16), ("ua", 16), ("ud", 16), ("ue", 16))),
+        (u2, (("LT", 128 * HOPS), ("RL", 192), ("AL", 192), ("POS", 24), ("PO3", 24), ("LD", 12), ("LE", 2)))):
     for n_, w_ in tiles:
         declare(n_, w_, t_)
 for c_ in (0, 1):
-    for n_, w_, t_ in (("Ma", 128, f4), ("Mb", 128, f4), ("Mc", 128, f4), ("NF", 8, f4), ("NS", 128, f2), ("WF", 256, f2), ("eq", 256, f4), ("dup", 256, f4)):
+    for n_, w_, t_ in (("Ma", 128, f4), ("Mb", 128, f4), ("Mc", 128, f4), ("NF", 8, f4), ("NS", 128, f2), ("WF", 256, f2)):
         declare(n_ + str(c_), w_, t_)
 for b_ in range(8):
     SCRATCH["pb%d" % b_] = ("psum", [128, 512], f4)
     PLACE["pb%d" % b_] = ("pb%d" % b_, 0, 512)
 SEMAPHORES = ["cV", "cS", "cP", "cG", "sent"] + ["ld%d" % k for k in range(5)] + ["st%d" % k for k in range(3)] + \
-    ["a%s%d" % (m, t) for m in ("L0", "L1", "D0", "D1", "D", "M0", "Z0", "M1", "Z") for t in range(1, HOPS)]
+    ["a%s%d" % (m, t) for m in ("L0", "L1", "D0", "D1", "D", "M0", "Z0", "M1", "Z", "P1", "Z1", "ZP") for t in range(1, HOPS)]
 ORDER = []
 
 
@@ -88,7 +95,7 @@ def make(g, T):
     eng = {"V": g.vector, "S": g.scalar, "P": g.tensor, "G": g, "Y": g.sync}
     cnt = {"V": 0, "S": 0, "P": 0, "G": 0}
     clk = {q: {} for q in eng}
-    snap, acc, plan, sends, first = {}, {}, [], {}, []
+    snap, acc, plan, sends, parts = {}, {}, [], {}, [(0, 0, "start")]
 
     def semof(r):
         return T.sem["c" + r] if r in cnt else T.sem[r]
@@ -172,7 +179,8 @@ def make(g, T):
             snap[(q, n)] = dict(clk[q])
             snap[(q, n)][q] = n - 1
             note(q, n, reads, writes)
-        plan.append((q, cycles(q, outs[0], ins, kind), 0, reads, writes, emit, kind if q == "P" else None))
+        plan.append((q, cycles(q, outs[0], ins, kind), 0, reads, writes, emit, kind if q == "P" else None,
+                     "scatter" if kind == "scatter" else "gather" if ins and len(ins[0][1]) > 1 else None))
 
     def sc(x):
         return x[0] if isinstance(x, tuple) else x
@@ -199,8 +207,8 @@ def make(g, T):
             op("S", lambda: eng["S"].activation(o[0], a[0], f, bias=sc(bias), scale=sc(scale)), [o], [a] + tl(bias, scale), "load" if f == F.Silu else None)
         else:
             op("S", lambda: eng["S"].activation(o[0], a[0], f, bias=sc(bias), scale=sc(scale), accum_out=total[0]), [o, total], [a] + tl(bias, scale))
-    def mm(o, l, r, st=True, sp=True):
-        op("P", lambda: eng["P"].matmul(o[0], l[0], r[0], st, sp), [o if st and sp else B(o[1][0][0])], [l, r], None if st or sp else "free")
+    def mm(o, l, r, st=True, sp=True, late=False):
+        op("P", lambda: eng["P"].matmul(o[0], l[0], r[0], st, sp), [o if st and sp else B(o[1][0][0])], [l, r], None if st or sp or late else "free")
     def iota(o, pat, base, cm, whole=False):
         if whole:
             op("G", lambda: g.iota(o[0], pat, base, cm), [o], [])
@@ -216,13 +224,13 @@ def make(g, T):
             eng[q].dma_start(out, in_).then_inc(T.sem[sem], 16)
             snap[(sem, 16)] = dict(clk[q])
             note(sem, 16, reads, writes)
-        plan.append((q, 100, LAG + LW * sum(size(x) for x in outs), reads, writes, emit, None))
+        plan.append((q, 100, LAG + LW * sum(size(x) for x in outs), reads, writes, emit, None, None))
 
     def arrive(sem, n, b):
         def emit():
             snap[(sem, n)] = {}
             note(sem, n, [], b[1])
-        plan.append((sem, 0, 0, [], b[1], emit, sends[sem]))
+        plan.append((sem, 0, 0, [], b[1], emit, sends[sem], None))
 
     def send(core, dst, topo, o, i, rsem):
         def emit():
@@ -230,22 +238,26 @@ def make(g, T):
             rid, pid = topo.addr(dst, core)
             g.remote_dma(o[0], i[0], T.sem[rsem], T.sem.sent, pid, rid, topo.mask(core, dst))
         sends[rsem] = len(plan)
-        plan.append(("G", 800 if len(sends) > 1 else FIRST, FAR + 3 * size(i), i[1], [], emit, None))
+        plan.append(("G", CALL if len(sends) > 1 else FIRST, FAR + 3 * size(i), i[1], [], emit, None, "send"))
         return len(topo.engines(core, dst))
+
+    def part(t, what):
+        parts.append((len(plan), t, what))
 
     def issue():
         if not ORDER:
-            ORDER.extend(order(plan))
+            names = [(t, (what, i - a)) for (a, t, what), b in zip(parts, parts[1:] + [(len(plan),)]) for i in range(a, b[0])]
+            ORDER.extend(order([x + (y,) for x, y in zip(plan, names)]))
         for i in ORDER:
             plan[i][5]()
 
     return dict(B=B, I=I, tt=tt, ts=ts, cp=cp, scat=scat, scan=scan, fill=fill, act=act, mm=mm, iota=iota, asel=asel, dma=dma,
-                arrive=arrive, send=send, issue=issue, cnt=cnt)
+                arrive=arrive, send=send, part=part, issue=issue, cnt=cnt)
 
 
 def needs(plan):
     pred, acc, bank = [], {}, {}
-    for i, (q, cost, lag, reads, writes, emit, after) in enumerate(plan):
+    for i, (q, cost, lag, reads, writes, emit, after) in enumerate(x[:7] for x in plan):
         p, free = {}, after == "free"
         for regs, w in ((reads, False), ([] if free else writes, True)):
             for reg in regs:
@@ -269,69 +281,155 @@ def needs(plan):
 
 
 def order(plan):
-    n = len(plan)
-    pred = needs(plan)
-    succ = [{} for _ in plan]
-    for i in range(n):
-        for j, d in pred[i].items():
-            succ[j][i] = d
-    banks = [sorted({r[0] for r in x[3] + x[4] if r[0].startswith("pb")}) for x in plan]
+    need, lumps, of = needs(plan), [], []
+    for i, x in enumerate(plan):
+        l = lumps[-1] if lumps else [i]
+        y = plan[l[-1]]
+        if lumps and x[0] == y[0] == "P" and (x[4][0][0], x[3][0][0], x[3][1][0]) == (y[4][0][0], y[3][0][0], y[3][1][0]) \
+                and sum(plan[j][1] for j in l) + x[1] <= LUMP and {j for j in need[i] if plan[j][0] != "P"} <= {j for k in l for j in need[k]}:
+            l.append(i)
+        else:
+            lumps.append([i])
+        of.append(len(lumps) - 1)
+    n = len(lumps)
+    Q, C, lag = [plan[l[0]][0] for l in lumps], [sum(plan[j][1] for j in l) for l in lumps], [plan[l[0]][2] for l in lumps]
+    pred, succ = [{} for _ in lumps], [{} for _ in lumps]
+    for i, p in enumerate(need):
+        for j, d in p.items():
+            if of[j] != of[i]:
+                pred[of[i]][of[j]] = succ[of[j]][of[i]] = max(pred[of[i]].get(of[j], 0), d)
+    banks = [sorted({8 * int(r[0][2]) for j in l for r in plan[j][3] + plan[j][4] if r[0].startswith("pb")}) for l in lumps]
+    qi = ["GPSVY".index(q) if len(q) == 1 else -1 for q in Q]
 
-    def lay(pred, succ, urge, head, tail):
-        left = [len(p) for p in pred]
-        ready = {i for i in range(n) if not left[i]}
-        end, taken, out = [0] * n, {}, []
-        while ready:
-            i = max(ready, key=lambda j: urge[j])
-            q, cost = plan[i][:2]
-            s = max([head[i]] + [end[j] + d for j, d in pred[i].items()])
-            moved = True
-            while moved:
-                moved = False
-                for r in [q] + banks[i]:
-                    for (a, b, o) in taken.get(r, ()):
-                        gap = 0 if r == q else CROSS if o != q else None
-                        if gap is not None and a - gap < s + cost and s < b + gap:
-                            s, moved = b + gap, True
-            end[i] = s + cost
-            for r in [q] + banks[i]:
-                taken[r] = sorted(taken.get(r, []) + [(s, end[i], q)])
-            ready.remove(i)
-            out.append(i)
-            for k in succ[i]:
-                left[k] -= 1
-                if not left[k]:
-                    ready.add(k)
-        place = {i: x for x, i in enumerate(out)}
-        return max(end[i] + tail[i] for i in range(n)), sorted(out, key=lambda i: (end[i] - plan[i][1], place[i])), end
-
-    def run(pred, succ, urge, head, tail):
-        left = [len(p) for p in pred]
-        ready = {i: head[i] for i in range(n) if not left[i]}
-        free, end, used, out = {}, [0] * n, {}, []
-        while ready:
-            st = {i: max([free.get(plan[i][0], 0), s] + [e + CROSS for b in banks[i] for r, e in used.get(b, {}).items() if r != plan[i][0]])
-                  for i, s in ready.items()}
-            i = min(st, key=lambda i: (st[i], -urge[i]))
-            end[i] = free[plan[i][0]] = st[i] + plan[i][1]
+    def run(pred, succ, urge, head, tail, look):
+        left, ready = [len(p) for p in pred], {}
+        for i in range(n):
+            if not left[i]:
+                ready.setdefault(Q[i], {})[i] = head[i]
+        free, end, used, out = {}, [0] * n, [-CROSS] * 64, []
+        while len(out) < n:
+            st = [{i: max([s, free.get(q, 0)] + [used[r] + CROSS for b in banks[i] for r in range(b, b + 5) if r != b + qi[i]]) for i, s in r.items()}
+                  for q, r in ready.items() if r]
+            st = min(st, key=lambda x: min(x.values()))
+            s = min(st.values())
+            i = max((j for j in st if st[j] <= s), key=lambda j: urge[j])
+            i = max([j for j in st if st[j] < s + min(C[i], look) and urge[j] - urge[i] > st[j] - s] or [i], key=lambda j: urge[j] - st[j])
+            end[i] = free[Q[i]] = st[i] + C[i]
             for b in banks[i]:
-                used.setdefault(b, {})[plan[i][0]] = end[i]
-            del ready[i]
+                used[b + qi[i]] = end[i]
+            del ready[Q[i]][i]
             out.append(i)
             for k in succ[i]:
                 left[k] -= 1
                 if not left[k]:
-                    ready[k] = max([head[k]] + [end[j] + d for j, d in pred[k].items()])
+                    ready.setdefault(Q[k], {})[k] = max([head[k]] + [end[j] + d for j, d in pred[k].items()])
         return max(end[i] + tail[i] for i in range(n)), out, end
 
-    none, lag = [0] * n, [x[2] for x in plan]
-    soon = max(range(n), key=lambda i: plan[i][1] if plan[i][0] == "S" else 0)
-    best = run(pred, succ, [-i for i in range(n)], none, lag)
-    for _ in range(ROUNDS):
-        for f in (run, lay):
-            back = f(succ, pred, best[2], lag, none)[2]
-            best = min(best, f(pred, succ, [back[i] + (max(back) if i == soon else 0) for i in range(n)], none, lag))
-    return best[1]
+    none = [0] * n
+    soon = max(range(n), key=lambda i: C[i] if Q[i] == "S" else 0)
+    best = cur = run(pred, succ, [-i for i in range(n)], none, lag, 0)
+    for t in range(ROUNDS):
+        back = run(succ, pred, cur[2], lag, none, 150 * (t % 4))[2]
+        back[soon] += max(back)
+        new = run(pred, succ, back, none, lag, 150 * (t % 4))
+        cur, best = new if new[0] < 1.01 * cur[0] else cur, min(best, new)
+    cases = []
+    for wait, f in CASES:
+        k = [f.get(plan[l[0]][7], 1) for l in lumps]
+        late = [lag[i] * (k[i] if k[i] != 1 else wait) for i in range(n)]
+        cases.append(([60 + (C[i] - 60) * k[i] for i in range(n)], late, CROSS * wait,
+                      [[(j, (d - lag[j]) * wait + late[j]) for j, d in p.items()] for p in pred]))
+
+    def replay(case, o, a, end, why, kept, limit):
+        C, lag, CROSS, P = case
+        free, used, top, last = kept[a // 40]
+        free, used, end, why, kept = free[:], used[:], end[:], why[:], kept[:a // 40 + 1]
+        for x in range(a // 40 * 40, n):
+            if x == 40 * len(kept):
+                kept.append((free[:], used[:], top, last))
+            i = o[x]
+            q, s, w, swap = qi[i], 0, -1, True
+            if q >= 0:
+                w, free[q] = free[q], i
+                s = end[w] if w >= 0 else 0
+            for j, d in P[i]:
+                if end[j] + d >= s:
+                    s, w, swap = end[j] + d, j, False
+            for b in banks[i]:
+                for r in range(b, b + 5):
+                    j = used[r]
+                    if j >= 0 and r != b + q and end[j] + CROSS > s:
+                        s, w, swap = end[j] + CROSS, j, True
+                used[b + q] = i
+            end[i], why[i] = s + C[i], (w, swap)
+            if end[i] + lag[i] > top:
+                top, last = end[i] + lag[i], i
+                if top > limit:
+                    return None
+        return top, last, end, why, kept
+
+    def steps(why, i):
+        runs, out = [[]], []
+        while i >= 0:
+            runs[-1].insert(0, i)
+            if not why[i][1]:
+                runs.append([])
+            i = why[i][0]
+        for r in runs:
+            out += [(r[0], v, 0) for v in r[1:]] + [(u, r[-1], 1) for u in r[:-1]] + [(u, v, 0) for u, v in zip(r[1:], r[2:])]
+            out += [(u, v, x) for u, v in zip(r, r[2:]) for x in (0, 1)]
+        return out
+
+    def shift(o, a, b, back):
+        s = {o[a] if back else o[b]}
+        for x in range(a + 1, b + 1) if back else range(b - 1, a - 1, -1):
+            if not s.isdisjoint((pred if back else succ)[o[x]]):
+                s.add(o[x])
+        if o[a] in s and o[b] in s:
+            return None
+        return o[:a] + sorted(o[a:b + 1], key=lambda i: (i in s) == bool(back)) + o[b + 1:]
+
+    name = [plan[l[0]][8] for l in lumps]
+    twin = {x: i for i, x in enumerate(name)}
+    at = [best[2][i] - C[i] for i in range(n)]
+    head = [at[twin[(t, ("rings", 0))]] for t in range(HOPS)]
+    r = min(range(1, HOPS - 1), key=lambda t: head[t + 1] - head[t])
+    at = [at[twin[(r, x)]] + (t - r) * (head[r + 1] - head[r]) if (r, x) in twin else at[i] - head[t] + head[r] + (t - r) * (head[r + 1] - head[r])
+          for i, (t, x) in enumerate(name)]
+    o, left, ready = [], [len(p) for p in pred], {i for i in range(n) if not pred[i]}
+    while ready:
+        o.append(min(ready, key=lambda i: at[i]))
+        ready.remove(o[-1])
+        for k in succ[o[-1]]:
+            left[k] -= 1
+            if not left[k]:
+                ready.add(k)
+    now = [replay(c, o, 0, none, none, [([-1] * 5, [-1] * 64, 0, -1)], 1e18) for c in cases]
+    best, todo, seed = (sum(x[0] for x in now), o), [], 1
+    for step in range(STEPS):
+        if not todo:
+            todo, pos = [s for x in now for s in steps(x[3], x[1])], {i: x for x, i in enumerate(o)}
+            if step >= ALIKE * STEPS:
+                todo = [s for s in todo if name[s[1]][0] >= HOPS - 2 or (step % 8 == 0 and name[s[1]][0] == 0)] or todo
+        seed = (seed * 1103515245 + 12345) % 2 ** 31
+        u, v, back = todo.pop(seed // 8 % len(todo))
+        new, room, r, spans = shift(o, pos[u], pos[v], back), SLACK * (1 - step / STEPS) * (seed % 1024) / 1024, [], [(pos[u], pos[v])]
+        if new and step < ALIKE * STEPS:
+            for d in range(1 - HOPS, HOPS):
+                a, b = (pos.get(twin.get((name[x][0] + d, name[x][1])), -1) for x in (u, v))
+                if 0 <= a < b and all(b < y or z < a for y, z in spans):
+                    new = shift(new, a, b, back) or new
+                    spans.append((a, b))
+            room *= len(spans)
+        for c, x in zip(cases, now):
+            r.append(new and replay(c, new, min(spans)[0], x[2], x[3], x[4], x[0] + room + (SLACK if len(r) < len(now) - 1 else 0)))
+            if not r[-1]:
+                break
+            room += x[0] - r[-1][0]
+        else:
+            o, todo, now = new, [], r
+            best = min(best, (sum(x[0] for x in now), o))
+    return [j for i in best[1] for j in lumps[i]]
 
 
 def rank_program(g, core, T, topo):
@@ -339,8 +437,8 @@ def rank_program(g, core, T, topo):
     if rank is None:
         return
     K = make(g, T)
-    B, I, tt, ts, cp, scat, scan, fill, act, mm, iota, asel, dma = (K[k] for k in (
-        "B", "I", "tt", "ts", "cp", "scat", "scan", "fill", "act", "mm", "iota", "asel", "dma"))
+    B, I, tt, ts, cp, scat, scan, fill, act, mm, iota, asel, dma, part = (K[k] for k in (
+        "B", "I", "tt", "ts", "cp", "scat", "scan", "fill", "act", "mm", "iota", "asel", "dma", "part"))
     nxt = T.cores[(rank + 3) % len(T.cores)]
     prv_eng = len(topo.engines(T.cores[(rank + 1) % len(T.cores)], core))
     ET, FT, FU, XS = B("ET", SP, SP + 2048), B("FT"), B("FU"), B("XS")
@@ -353,7 +451,7 @@ def rank_program(g, core, T, topo):
 
     def lst(t, c, kind, a=0, b=None):
         w = CHUNK[c][1] // 16
-        o = 64 * t + {"vm": 8 * c, "v": 24 + 16 * c - w, "vf": 24 + 16 * c - w, "f": 24 + 16 * c, "fm": 48 + 8 * c}[kind]
+        o = 128 * t + {"vm": 32 * c, "v": 56 + 16 * c - w, "vf": 56 + 16 * c - w, "f": 56 + 16 * c, "fm": 80 + 32 * c}[kind]
         return B("LT", o + a, o + ((2 * w if kind == "vf" else w) if b is None else b))
 
     def msg(buf, t, c, j, j1=None):
@@ -365,9 +463,9 @@ def rank_program(g, core, T, topo):
         if m[0] == "L":
             return lst(t + 1, int(m[1]), "v"), lst(t, int(m[1]), "f")
         if m[0] == "D":
-            c, b = (int(m[1]), None) if m[1:] else (0, 12)
+            c, b = (int(m[1]), CHUNK[int(m[1])][1] // 4) if m[1:] else (0, 48)
             return lst(t + 1, c, "vm", 0, b), lst(t, c, "fm", 0, b)
-        a, b = {"M0": (0, NA), "Z0": (NA, 2 * NA), "M1": (2 * NA, 384), "Z": (NA, 384)}[m]
+        a, b = {"M0": (0, NA), "Z0": (NA, 2 * NA), "M1": (2 * NA, 384), "Z": (NA, 384), "P1": (2 * NA, 192 + NA), "Z1": (192 + NA, 384), "ZP": (NA, 192 + NA)}[m]
         return B("MM", 384 * (t + 1) + a, 384 * (t + 1) + b), B("MO", 384 * t + a, 384 * t + b)
 
     def col(name, c, h=None):
@@ -380,20 +478,24 @@ def rank_program(g, core, T, topo):
         return B(n, a, b, st, 0, CHUNK[c][1])
 
     def dedupe(c, t, kind):
-        n, s, bk = CHUNK[c][1], str(c), BANK["same"][c]
-        wf, wm = W(c, "WF" + s), W(c, "WF" + s, 128, 256)
-        mm(B(bk, 0, 2 * n), wf, W(c, "PERM", 0, 2 * n), True, False)
-        mm(B(bk, 0, 2 * n), wm, W(c, "SEG", 0, 2 * n), False, False)
-        mm(B(bk, 2 * n, 4 * n, 32), wm, W(c, "GBs", 0, n // 16), False, True)
-        eq, dup = B("eq" + s, 0, 2 * n), B("dup" + s, 0, 2 * n)
-        tt(eq, B(bk, 0, 2 * n), B("MK", 0, 2 * n), A.is_equal)
-        scan(dup, eq, B(bk, 2 * n, 4 * n), 0.0, A.max, A.min)
-        ts(lst(t, c, kind), B("dup" + s, 31, 2 * n, 32), 4096.0, None, A.mult)
+        for b in range(CHUNK[c][1] // 64 - 1, -1, -1):
+            s, (bk, d, e) = str(2 * c + b), BANK["same"][2 * c + b]
+
+            def R(n, a, z, st=1):
+                return B(n, a, z, st, 64 * b, 64 * b + 64)
+            wf, wm = R("WF%d" % c, 0, 128), R("WF%d" % c, 128, 256)
+            mm(B(bk, d, d + 160), wf, R("PERM", 0, 160), True, False)
+            mm(B(bk, d, d + 160), wm, R("SEG", 0, 160), False, False)
+            mm(B(bk, e, e + 49, 48), wm, R("GBs", 4 * b, 4 * b + 4, 2), False, False)
+            mm(B(bk, e + 16, e + 97, 80), wm, R("GBs", 4 * b + 1, 4 * b + 4, 2), False, True)
+            tt(B("eq" + s), B(bk, d, d + 160), B("MK"), A.is_equal)
+            scan(B("dup" + s), B("eq" + s), B(bk, e, e + 160), 0.0, A.max, A.min)
+            ts(lst(t, c, kind, 16 * b, 16 * b + 16), I(B("dup" + s), B("LE", 0, 1)), 4096.0, None, A.mult)
 
     def marks(q, tab, val, v0, t, c, kind):
         p0, n = CHUNK[c]
-        for b in range(n // 32 - 1, -1, -1):
-            scat(q, B(tab), lst(t, c, kind, 2 * b, 2 * b + 2), B(val, v0 + p0 + 32 * b, v0 + p0 + 32 * b + 32))
+        for b in range(n // 64 - 1, -1, -1):
+            scat(q, B(tab), lst(t, c, kind, 16 * b, 16 * b + 4), B(val, v0 + p0 + 64 * b, v0 + p0 + 64 * b + 64))
 
     def row(c, o, t):
         n = CHUNK[c][1]
@@ -416,13 +518,18 @@ def rank_program(g, core, T, topo):
         else:
             ts(o, a, s1, s2, A.mult, A.mult)
 
-    for n, v in (("o256", 1.0), ("m256", -1.0), ("WNa", 128 * U), ("NS0", 0.0), ("NS1", 0.0), ("NF1", 0.0)):
+    for n, v in (("o256", 1.0), ("WNa", 128 * U), ("NS0", 0.0), ("NS1", 0.0), ("NF1", 0.0)):
         fill(B(n), v)
-    fill(B("pb6", 192, 208), 0.0); fill(B("FT", 1024, 2080), 2048.0)
+    fill(B("pb6", 256, 272), 0.0); fill(B("FT", 1024, FV), 2048.0)
+    for a in range(FV, 2112, 544):
+        iota(B("FT", a, min(2112, a + 544)), [[0, min(2112, a + 544) - a]], 2048, 0)
     for a in range(0, 1024, 256):
         act(B("FT", a, a + 256), B("o256"), F.Copy if a else F.Silu, scale=2048.0)
-    for n, v in (("onef", 1.0), ("C32", 32.0), ("RSA", -1.0e20), ("RSB", -1.0e20), ("RSC", -1.0e20)):
-        act(B(n), B("o256", 0, PLACE[n][2]), scale=v)
+    for n, v in (("onef", 1), ("C32", 32), ("RSA", -15 * 2 ** 20), ("RSB", -15 * 2 ** 20), ("RSC", -15 * 2 ** 20)):
+        if n in ONG:
+            iota(B(n), [[0, PLACE[n][2]]], v, 0)
+        else:
+            act(B(n), B("o256", 0, PLACE[n][2]), scale=float(v))
     for a in (0, 192):
         act(B("RSP", a, a + 192), B("o256", 0, 192), scale=1.0e6)
     iota(B("qI"), [[0, 1]], 0, 1, True)
@@ -431,12 +538,8 @@ def rank_program(g, core, T, topo):
     iota(B("RSi"), [[-16, 24]], -16 - 4096, 0)
     iota(B("THR"), [[0, 2], [2048, 8]], int(BAR), 0)
     for j in range(4):
-        iota(B("FU", 520 * j, 520 * j + 520), [[0, 520]], 2048, 0)
-    iota(B("CJ"), [[0, 4], [-16, 2], [1, 32]], -1, 0)
-    iota(B("CL"), [[0, 4], [16, 2], [0, 32]], 2048, 0)
-    asel(B("PERM"), B("o256"), [[-32, 4], [0, 2], [-1, 32]], A.is_equal, 0.0, 1, 1)
-    asel(B("SEGt"), B("m256"), [[-16, 8], [0, 32]], A.is_ge, 0.0, 0, 1)
-    asel(B("SEG"), B("SEGt"), [[16, 8], [0, 32]], A.is_ge, 0.0, 15, -1)
+        iota(B("FU", 528 * j, 528 * j + 528), [[0, 528]], 2048, 0)
+    iota(B("CJ"), [[1, 64]], 0, 0)
     for t in range(HOPS):
         iota(B("VV", 192 * t, 192 * t + 192), [[2, 192]], 1664 - 384 * t - 1, 0)
         iota(B("VAL", 192 * t, 192 * t + 192), [[2, 192]], 1664 - 384 * t, 0)
@@ -455,43 +558,45 @@ def rank_program(g, core, T, topo):
     asel(B("E2"), B("E2t"), [[2, 64]], A.is_ge, 0.0, 1, -1)
     iota(B("ODt"), [[0, 8], [1, 2], [0, 8]], 0, 0)
     asel(B("GBt"), B("o256", 0, 8), [[-16, 8]], A.is_ge, 0.0, 0, 1)
-    asel(B("GB"), B("GBt"), [[16, 8]], A.is_ge, 0.0, 15, -1)
+    asel(B("GBf"), B("GBt"), [[16, 8]], A.is_ge, 0.0, 15, -1)
+    act(B("GB"), B("GBf")); tt(B("GB4"), B("GBf", 0, 4), B("GBf", 4, 8), A.add)
     asel(B("WNb"), B("WNa"), [[0, 48], [-16, 8]], A.is_ge, 0.0, 0, 1)
     asel(B("WNa"), B("WNb"), [[0, 48], [16, 8]], A.is_ge, 0.0, 15, -1)
     asel(B("WN"), B("WNa"), [[-1, 16], [0, 3], [-16, 8]], A.not_equal, 2.0 ** 26, 0, 1)
     ts(B("qJ"), B("qI"), 15, None, A.bitwise_and); cp(B("qi"), B("qJ")); ts(B("qK"), B("qJ"), 1, None, A.bitwise_and)
+    ts(B("qL"), B("qI"), 63, None, A.bitwise_and)
     ts(B("EQD"), B("CI"), B("qi"), None, A.is_equal)
-    ts(B("qb"), B("qi"), 1.0, 1 / 32, A.max, A.mult)
-    for n, a, s, b in (("wtf", B("wts"), 1.0, 0.0), ("qa", B("qi"), 2048.0, -2048 * (15.5 + T0)), ("qe", B("qK"), -1.0, 1.0), ("qs1", B("qi"), 1.0, 1.0),
-                       ("qr", q(1), -31 / 32, 1.0), ("qg", q(0), -32 * U, 32 * U), ("qc", q(1), T0 - CC / 32, 0.0)):
+    for n, a, s, b in (("wtf", B("wts"), 1.0, 0.0), ("qa", B("qi"), 2048.0, -2048 * (15.5 + T0)), ("qe", B("qK"), -1.0, 1.0), ("qs1", B("qi"), 1.0, 1.0), ("qb", B("qi"), 1 / 4096, 0.5),
+                       ("q64", B("qL"), 1.0, 1.0), ("qx", q(1), 32.0, 15.0), ("GB4", B("GB4"), -1.0, 0.0),
+                       ("qr", q(1), -31 / 32, 1.0), ("qg", B("qi"), U / HI, -1.0), ("qc", q(1), T0 - CC / 32, 0.0)):
         act(B(n), a, scale=s, bias=b)
     for n, a, s, b in (("qy", q(1), 2048.0, q(0)), ("qv", q(3), 4096.0, q(0)), ("qf", q(2), 4096.0, q(0)), ("q23", q(2), 1.0, q(3)),
-                       ("qd", q(2), -4096.0, B("qc")), ("qs", q(3), -3328.0, B("qd"))):
+                       ("qd", q(2), -4096.0, B("qc")), ("qs", q(3), -3328.0, B("qd")), ("qw", q(2), 80.0, B("qx")), ("qu", q(3), 144.0, B("qw"))):
         act(B(n), a, F.Identity, scale=s, bias=b)
     ts(B("qo"), B("qK"), q(15), None, A.subtract); act(B("q23"), B("q23"), scale=768.0)
     ts(B("QS"), B("LI", 0, 6), B("q23"), B("qs"), A.mult, A.add)
     ts(B("ODD"), B("ODt"), B("qe"), 2.0 ** 45, A.is_equal, A.mult)
     cp(B("LD"), B("LI"))
-    ts(B("MK"), B("CJ"), B("qi"), 4096.0, A.is_ge, A.mult)
-    for c in (0, 1):
-        n = CHUNK[c][1]
-        ts(B(BANK["same"][c], 2 * n, 4 * n), B("CL", 0, 2 * n), B("qi"), 1 / 4096, A.add, A.mult)
-    for n in ("PERM", "SEG"):
-        act(B(n, 0, 256, 32), B("o256", 0, 8), scale=0.0)
+    cp(B("LE", 0, 1), B("qu")); ts(B("CK"), B("CJ"), B("qi"), None, A.subtract)
+    for a in range(4):
+        o, n = 8 * a * (a + 1), 16 * a + 16
+        ts(B("MK", o, o + n), B("CK", 0, n), 16.0 * a + 1, 4096.0, A.is_ge, A.mult)
+        ts(B("PERM", o, o + n), B("CJ", 0, n), B("q64"), None, A.is_equal)
+        ts(B("SEG", o, o + n), B("CJ", 0, n), 0.5, B("GB4", a, a + 1), A.is_ge, A.mult)
+        act(B("CD", o, o + n), B("o256", 0, n), F.Identity, scale=a / 256, bias=B("qb"))
+    for bk, d, e in BANK["same"]:
+        act(B(bk, e, e + 160), B("CD"))
     act(B("RSP", 0, 384, 16), B("RSi"), F.Identity, bias=B("qi"))
     act(B("RSB", 0, 128, 16), B("THR", 0, 8)); act(B("RSC", 0, 128, 16), B("THR", 0, 8), bias=CC)
-    for n, a, v in (("IDb", "ID", 1.0), ("NIb", "ID", -1.0), ("NID", "ID", -1.0), ("I4K", "ID", 4096.0), ("W4K", "ID", -4096.0), ("I8b", "ID", 8192.0),
+    for n, a, v in (("IDb", "ID", 1.0), ("NIb", "ID", -1.0), ("NID", "ID", -1.0), ("I4K", "ID", 4096.0), ("W4K", "ID", -4096.0), ("I8b", "ID", 8192.0), ("I4b", "ID", 4096.0), ("WP", "ID", -65536.0),
                     ("WPd", "ID", B("qg")), ("BDv", "BD", B("qv")), ("BDf", "BD", B("qf")), ("WY", "BD", B("qy")), ("D15", "D15t", q(0)), ("E2b", "E2", 1 / 64)):
         mul(B(n), B(a), v)
-    for n, i, v in (("WT", 1, 2048.0), ("W64", 1, -64.0), ("Y15", 0, 16.0), ("WPa", 1, -32768.0), ("WPb", 0, -31 * 2.0 ** 24)):
+    for n, i, v in (("WT", 1, 2048.0), ("W64", 1, -64.0), ("Y15", 0, 16.0), ("WPb", 0, -70.0)):
         mul(B(n), B("BD"), q(i), v)
-    mul(B("PE0"), B("o256", 0, 128), B("qb"))
-    tt(B("WP", 128, 256), B("WPb"), B("WPd"), A.add); tt(B("WP", 0, 128), B("WP", 128, 256), B("WPa"), A.add); cp(B("WP", 256, 384), B("WP", 128, 256))
-    for j in range(3):
-        mul(B("WH", 128 * j, 128 * j + 128), B("ID"), -1.0)
+    tt(B("WH", 0, 128), B("WPb"), B("WPd"), A.add); cp(B("WH", 128, 256), B("WH", 0, 128)); cp(B("WH", 256, 384), B("WH", 0, 128))
     for n, v in (("WX", 1 / 4), ("WR", -1 / 8), ("WA", 1 / 8)):
         act(B(n), B("WNa", 0, 24), scale=v)
-    act(B("WD"), B("GB"), scale=B("wtf")); act(B("GBs"), B("GB"), scale=1 / 4096)
+    act(B("WD"), B("GB"), scale=B("wtf")); act(B("GBs"), B("GBf"), scale=1 / 4096)
     for c in (0, 1):
         if KS[c] < 16 // WD:
             for j in range(3):
@@ -519,12 +624,17 @@ def rank_program(g, core, T, topo):
     sent = 0
     for t in range(HOPS):
         last = t == HOPS - 1
+        part(t, "arrivals")
         if t > 0:
             for m in SENDS:
                 K["arrive"]("a%s%d" % (m, t), prv_eng, parts(m, t - 1)[0])
 
         def bc(name, c, k, st=16):
             return B(name, 16 * CHUNK[c][0] + k, 16 * (CHUNK[c][0] + CHUNK[c][1]), st)
+
+        def bp(name, c, p, j, m=MP):
+            p0, n = CHUNK[c]
+            return B(name, 16 * (p0 + p) + j, 16 * (p0 + min(n, p + m)), 16 // WD)
 
         def halves(c):
             return range(CHUNK[c][0] // 64, (CHUNK[c][0] + CHUNK[c][1]) // 64)
@@ -559,11 +669,14 @@ def rank_program(g, core, T, topo):
                     i = (k + t) % 16
                     mm(B(bk, k, 128, 8), B("X", 1024 * h + k, 1024 * h + 1024, 8), B("SE2", 16 * i, 16 * i + 16), False, False)
                 mm(B(bk, 0, 128), B("NIb"), B("ODD"), False, True)
-                lin("sb", sb, B(bk, 0, 128), -1023.5)
+                lin("sb", sb, B(bk, 0, 128), -511.5)
                 tt(nm, B(bk, 0, 128), sb, A.subtract)
-                mm(B("pb6", 64 * h, 64 * h + 64), nm, B("E2"))
-                ts(B("AL", 64 * h, 64 * h + 64), B("pb6", 64 * h, 64 * h + 64), -1024.0, None, A.add)
-            lin("hi", col("hi", c), col("pb6", c), HI - 1535.5)
+                o = B(BANK["names"][h], 128, 192)
+                if t > 0:
+                    mm(o, B("WP"), B("PEN", 64 * h, 64 * h + 64), True, False)
+                mm(o, nm, B("E2"), t == 0, True)
+                cp(B("AL", 64 * h, 64 * h + 64), o)
+                lin("hi", B("hi", 64 * h, 64 * h + 64), o, HI - 511.5)
 
         def older(c):
             n, bk = CHUNK[c][1], BANK["thr"][c]
@@ -571,16 +684,22 @@ def rank_program(g, core, T, topo):
             if t > 0:
                 for m in range(WD):
                     mm(B(bk, a + m, 512, WD), B("WT"), msg("MM", t, c, 0))
-                ts(col("PEN", c), B(bk, a, 512, WD), B("qa"), B("qb"), A.add, A.max)
-            mm(W(c, "pb%d" % (2 + c), 0, 384), col("PEN", c) if t else B("PE0", 0, n), B("WP"), True, False)
-            for j in range(16 // WD):
-                if t > 0:
-                    tt(bc("M", c, j, 16 // WD), bc("X", c, j, 16 // WD), B(bk, a, 512), A.is_lt)
+                if "pen" in ONS:
+                    act(col("PEN", c), B(bk, a, 512, WD), F.Relu, bias=B("qa"))
                 else:
-                    ts(bc("M", c, j, 16 // WD), bc("X", c, j, 16 // WD), 2048 * T0, None, A.is_lt)
+                    ts(col("PEN", c), B(bk, a, 512, WD), B("qa"), 0.0, A.add, A.max)
+            zsum = KS[c] < 16 // WD
+            if zsum:
+                mm(W(c, "pb%d" % (2 + c), 0, 384), msg("MM", t, c, 1), B("WZ%d" % c), True, False)
+            for j in range(16 // WD):
+                for p in range(0, n, MP):
+                    if t > 0:
+                        tt(bp("M", c, p, j), bp("X", c, p, j), B(bk, a + WD * p, a + WD * min(n, p + MP)), A.is_lt)
+                    else:
+                        ts(bp("M", c, p, j), bp("X", c, p, j), 2048 * T0, None, A.is_lt)
                 for k in range(j, 16, 16 // WD):
                     i = (k + t) % 16
-                    mm(key(c, k), bc("M", c, k), B("WN", 24 * i, 24 * i + 24), False, False)
+                    mm(key(c, k), bc("M", c, k), B("WN", 24 * i, 24 * i + 24), k == 0 and not zsum, False)
 
         def entry(c, name, a, w, stop=False):
             for h in halves(c):
@@ -591,12 +710,11 @@ def rank_program(g, core, T, topo):
             kk, J, z = W(c, "pb%d" % (2 + c), 0, 384), 16 // WD, msg("MM", t, c, 1)
             bk, a = BANK["zz"][c], 512 - WD * n
             ks, m, sums = [k for k in range(16) if k % J < KS[c]], 512 // n, []
-            mm(kk, col("hi", c), B("WH"), False, False)
+            mm(kk, col("hi", c), B("WH"), False, False, KS[c] == J)
             entry(c, "sbh", 256, "E2b")
             if KS[c] == J:
                 entry(c, "nmh", 0, "E2")
             else:
-                mm(kk, z, B("WZ%d" % c), False, False)
                 for j in range(WD):
                     mm(B(bk, a + j, 512, WD), B("ID"), z)
             for k in range(16):
@@ -612,7 +730,8 @@ def rank_program(g, core, T, topo):
                 if part:
                     act(B("AB", o, o + len(part) * n), B(db, 0, len(part) * n), F.Abs)
                 if KS[c] + x < J:
-                    tt(bc("MX", c, KS[c] + x, J), bc("R", c, KS[c] + x, J), B(bk, a, 512), A.max)
+                    for p in range(0, n, XP):
+                        tt(bp("MX", c, p, KS[c] + x, XP), bp("R", c, p, KS[c] + x, XP), B(bk, a + WD * p, a + WD * min(n, p + XP)), A.max)
                     sums += [(k, bc("MX", c, k), "WX") for k in range(KS[c] + x, 16, J)]
                 sums += [(k, B("AB", o + j * n, o + j * n + n), "WA") for j, k in enumerate(part)]
             for k, d, w in sums:
@@ -620,15 +739,27 @@ def rank_program(g, core, T, topo):
             if KS[c] < J:
                 entry(c, "nmh", 0, "E2", True)
 
+        def fused(c):
+            p0, n = CHUNK[c]
+            mm(W(c, "pb%d" % (2 + c), 0, 384), col("hi", c), B("WH"), False, False, True)
+            entry(c, "sbh", 256, "E2b"); entry(c, "nmh", 0, "E2")
+            for k in range(16):
+                asel(bc("MX", c, k), msg("MM", t, c, 1), [[0, n]], A.is_equal, 0.0, 0, 0)
+            for p in range(p0, p0 + n, FUSE):
+                tt(B("R", 16 * p, 16 * (p + FUSE)), I(XS, B("AL", p, p + FUSE)), B("MX", 16 * p, 16 * (p + FUSE)), A.subtract)
+                act(B("AB", 16 * p, 16 * (p + FUSE)), B("R", 16 * p, 16 * (p + FUSE)), F.Abs)
+            for k in range(16):
+                mm(key(c, k), bc("AB", c, k), B("WA"), False, k == 15)
+
         def hash_():
             for c in (0, 1):
-                mm(W(c, "pb6", 192 + 8 * c, 200 + 8 * c), msg("MM", t, c, 1), B("WD"))
-            cp(B("ui"), B("pb6", 192, 208))
+                mm(W(c, "pb6", 256 + 8 * c, 264 + 8 * c), msg("MM", t, c, 1), B("WD"))
+            cp(B("ui"), B("pb6", 256, 272))
             ts(B("ua"), B("ui"), 2047, None, A.bitwise_and)
             act(B("uc"), B("ua"), F.Square, bias=592.0)
             if t > 0:
-                act(B("Ax"), B("pb6", 208, 209), scale=-1.0, bias=4080 - 17 * 65536.0)
-                act(B("Ay"), B("pb6", 208, 209), F.Identity, bias=B("Ax"))
+                act(B("Ax"), B("pb6", 272, 273), scale=-1.0, bias=4080 - 17 * 65536.0)
+                act(B("Ay"), B("pb6", 272, 273), F.Identity, bias=B("Ax"))
                 ts(B("ud"), B("uc"), B("Ay"), -592.0 ** 2, A.add, A.add)
             else:
                 ts(B("ud"), B("uc"), -592.0 ** 2, None, A.add)
@@ -656,8 +787,8 @@ def rank_program(g, core, T, topo):
             row(c, msg("MO", t, c, 0), t)
 
         def zproc(c):
-            n, bk = CHUNK[c][1], BANK["zp"][c]
-            p1, p2 = B(bk, 256, 256 + n), B(bk, 384, 384 + n)
+            n, (bk, a, b) = CHUNK[c][1], BANK["zp"][c]
+            p1, p2 = B(bk, a, a + n), B(bk, b, b + n)
             act(col("XF", c), I(XS, lst(t, c, "f")))
             mm(p1, B("W64"), msg("MO", t, c, 0), True, False)
             mm(p1, B("ID"), col("XF", c), False, True)
@@ -678,10 +809,11 @@ def rank_program(g, core, T, topo):
             act(col("NN", c, 2), B(bk, 0, 2 * n), F.Identity, bias=16 * 2048.0 * (9 + t) if last else B("BT", t, t + 1))
             tt(col("PRE", c), I(FU if c else FT, lst(t, c, "f")), B("VAL", 192 * t + p0, 192 * t + p0 + n), A.min)
             marks(MQ[c], "FU" if c else "FT", "PRE", 0, t, c, "fm")
-            if "av%d" % c in ONS:
-                act(col("AV", c, 2), I(FU if c else FT, lst(t, c, "vf")))
-            else:
-                tt(col("AV", c, 2), I(FU if c else FT, lst(t, c, "vf")), B("EQD", 0, 2 * n), A.add)
+            for q, h, kind in {"S": [("S", 2, "vf")], "V": [("V", 2, "vf")], "SV": [("S", 0, "v"), ("V", 1, "f")]}[LQ[c]]:
+                if q == "S":
+                    act(col("AV", c, h), I(FU if c else FT, lst(t, c, kind)))
+                else:
+                    tt(col("AV", c, h), I(FU if c else FT, lst(t, c, kind)), B("EQD", 0, len(kind) * n), A.add)
             if c:
                 top = 1664.0 - 384 * t + 2 * NA
                 if "gv" in ONS:
@@ -691,7 +823,7 @@ def rank_program(g, core, T, topo):
 
         def stand(cs):
             bk, a, b = "pb%d" % (2 + cs[0]), 2 * CHUNK[cs[0]][0], 2 * sum(CHUNK[cs[-1]])
-            terms = [(c, h, "I8b", B("EQD", 0, CHUNK[c][1])) for c in cs if "av%d" % c in ONS for h in (0, 1)]
+            terms = [(c, h, "I8b" if LQ[c] == "S" else "I4b", B("EQD", 0, CHUNK[c][1])) for c in cs if LQ[c] != "V" for h in (0, 1)]
             terms += [(c, h, w, msg(m, t, c, 0)) for h, (w, m) in enumerate((("BDv", "MM"), ("BDf", "MO"))) for c in cs]
             for c in cs:
                 if c:
@@ -700,52 +832,71 @@ def rank_program(g, core, T, topo):
             for x, (c, h, w, r) in enumerate(terms):
                 mm(col(bk, c, h), B(w), r, x == 0, x == len(terms) - 1)
             scan(B("ysa", a, b), B("RSP", a, b), B(bk, a, b), 1.0e6, A.min, A.max)
-            ts(B("POS", a // 16, b // 16), B("ysa", a + 15, b, 16), SP + 4096.0, None, A.add)
-            scat("V", B("YS" if last else "ET"), B("POS", a // 16, b // 16), B("NN", a, b))
+            pos = "PO3" if t == HOPS - 2 else "POS"
+            ts(B(pos, a // 16, b // 16), B("ysa", a + 15, b, 16), SP + 4096.0, None, A.add)
+            if APART == 2:
+                a = 0 if b == 384 else b
+            if a < b:
+                scat("V", B("YS" if last else "ET"), B(pos, a // 16, b // 16), B("NN", a, b))
 
-        def ysum(j):
-            bk, ef, et = BANK["ys"][j], B("EF", 512 * j, 512 * j + 512), B("ET", SP + 512 * j, SP + 512 * j + 512)
-            if j in EG:
-                asel(ef, et, [[0, 512]], A.is_equal, 0.0, 0, 0)
-            else:
-                act(ef, et)
-            for a in range(0, 512, 128):
-                mm(B(bk, a, a + 128), B("YW"), B("EF", 512 * j + a, 512 * j + a + 128))
-            act(B("YS", SP + 512 * j, SP + 512 * j + 512), B(bk))
+        def ysum(when):
+            part(t, "sums %d" % when)
+            for a in range(0, 2048, 512):
+                if (t, when) == (HOPS - 1 if YT[a // 256] >= YN else HOPS - 2, 0):
+                    asel(B("EF", a, a + 512), B("ET", SP + a, SP + a + 512), [[0, 512]], A.is_equal, 0.0, 0, 0)
+            if (t, when) == YN:
+                for a in range(0, 384, YS):
+                    scat("V", B("YS"), B("PO3", a // 16, (a + YS) // 16), B("NY", a, a + YS))
+            for j in range(8):
+                if YT[j] == (t, when):
+                    for y in (0, 128):
+                        mm(B("pb6", y, y + 128), B("YW"), B("EF", 256 * j + y, 256 * j + y + 128))
+                    act(B("YS", SP + 256 * j, SP + 256 * j + 256), B("pb6", 0, 256))
 
+        part(t, "rings")
         ring(0); ring(1)
         for h in range(3):
             rings("V", 64 * h, 64 * h + EV[h]); rings("S", 64 * h + EV[h], 64 * h + 64)
+        ysum(0)
+        part(t, "candidates" if t else "first candidates")
         for c in (0, 1):
             act(col("Rv", c), I(ET, lst(t, c, "v")))
             older(c)
         pick(0); pick(1)
+        hash_()
+        part(t, "records")
         marks(MV[0], "FT", "VV", 192 * t, t, 0, "vm"); marks(MV[1], "FU", "VV", 192 * t, t, 1, "vm")
-        for h in range(3):
+        for h in range(2 if FUSE else 3):
             records("V", 64 * h, 64 * h + RV[h]); records("S", 64 * h + RV[h], 64 * h + 64)
-        hash_(); sizes(0); sizes(1)
-        if last:
-            for j in range(YE):
-                ysum(j)
+        sizes(0); (fused if FUSE else sizes)(1)
+        ysum(1)
+        part(t, "least")
         for c in (0, 1):
             least(c); dedupe(c, t, "fm"); zproc(c)
             act(col("Rf", c), I(ET, lst(t, c, "f")))
-        if last:
-            for j in range(YE, 4):
-                ysum(j)
-        else:
+        part(t, "sends")
+        if not last:
             for m in SENDS:
                 sent += K["send"](core, nxt, topo, *parts(m, t), "a%s%d" % (m, t + 1))
+        part(t, "meetings")
         meetings(0); meetings(1)
         for cs in ((0,), (1,)) if APART else ((0, 1),):
             stand(cs)
+        part(t, "new sums")
+        if t == HOPS - 2:
+            for a in range(0, 384, 128):
+                mm(B(BANK["ny"], a, a + 128), B("YW"), B("NN", a, a + 128))
+            act(B("NY"), B(BANK["ny"], 0, 384))
+        part(t, "failures")
         if not last:
             for c in (0, 1):
                 act(W(c, "FC", 8 * c, 8 * c + 8), W(c, "NS%d" % c, 1, 128, 16), F.Relu, scale=-1 / 32, bias=1 + CC / 32, total=W(c, "FA", c, c + 1))
             for c in (0, 1):
-                mm(B("pb6", 208, 209), W(c, "C32"), W(c, "FA", c, c + 1), c == 0, c == 1)
+                mm(B("pb6", 272, 273), W(c, "C32"), W(c, "FA", c, c + 1), c == 0, c == 1)
+            ysum(2)
 
     t = HOPS - 1
+    part(t, "end")
     dma("S", "st0", T.yz[:], T.ZL[:], [], [B("ZL")])
     for c in (0, 1):
         mm(col("pb4", c), B("WY"), msg("MO", t, c, 0))

import math
from concourse.mybir import AluOpType as A, ActivationFunctionType as F

HOPS = 5
NA = 128
CHUNK = ((0, NA), (NA, 192 - NA))
WD = 4
MP, XP = 64, 64
PC = 64
SENDS = ("L0", "M0", "L1", "Z0", "M1", "D")
EV, RV = (32, 32, 0), (0, 16, 0)
MQ = "SV"
MV = "SS"
LQ = ("SV", "S")
ONS = ("ns", "pen", "hi", "gv")
ONG = ("C32", "RSB", "RSC")
FV = 1568
KS = (0, 4)
FUSE = 0
APART = 1
BANK = dict(ny="pb3", names=("pb0", "pb1", "pb7"), pick=("pb0", "pb1", "pb7"), thr=("pb4", "pb5"), zz=("pb4", "pb6"), diff=("pb0", "pb1"), same=(("pb5", 256, 0), ("pb7", 0, 192), ("pb7", 0, 352)), lst=("pb0", "pb1"),
            row=("pb1", "pb4"), zp=(("pb4", 256, 384), ("pb5", 160, 416)), new=("pb0", "pb1"))
SP = 384
B0 = 2.0 ** 18 + 4096 - 512
T0 = B0 / 2048 + 1
U = 1536.0
BAR = 211.0 * 2 ** 16
CC = B0 / 64
HI = 1.5 * 2 ** 17
PE, GATHER, SCATTER, FIX, OWN, CROSS, LAG, FAR = 0.64, 1.6, 3.5, 24, 230, 230, 2200, 4500
FIRST, CALL = 2200, 800
RP = 64
YT = ((3, 0), (3, 1), (3, 1), (3, 2), (3, 2), (4, 0), (4, 1), (4, 1))
YN, YS = (4, 1), 128
LW = 2
ALIKE = 0.4
ROUNDS, STEPS, SLACK, LUMP = 8, 22000, 120, 350
CASES = ((1, {"send": 1.1}), (0.75, {"gather": 1.2, "scatter": 1.4}))
f4, f2, b2, i4, u2 = "float32", "float16", "bfloat16", "int32", "uint16"
SCRATCH = {}
OWNBUF = ("EF", "ET", "YS", "XS", "FT", "FU", "YP", "ZL", "v0s", "v0f", "z0s", "wts", "X", "M", "R", "MX", "AB", "VAL", "VV", "MM", "MO",
          "LT", "RL", "AL", "POS", "PO3", "NY", "NN", "PRE", "LD", "LE", "dup0", "dup1", "dup2", "NF0", "NF1")
PLACE = {}


def declare(name, w, t):
    if name in OWNBUF:
        SCRATCH[name] = ("sbuf", [128, w], t)
        PLACE[name] = (name, 0, w)
        return
    pool = "pool" + t
    a = SCRATCH[pool][1][1] if pool in SCRATCH else 0
    SCRATCH[pool] = ("sbuf", [128, a + w + w % 2], t)
    PLACE[name] = (pool, a, w)


for t_, tiles in (
        (f4, (("EF", 2048), ("YS", SP + 2048), ("FT", 2112), ("FU", 2112), ("eq0", 160), ("eq1", 160), ("eq2", 160), ("dup0", 160), ("dup1", 160), ("dup2", 160), ("CD", 160), ("GB4", 4), ("YP", 192), ("v0f", 12), ("X", 3072), ("NN", 384), ("NY", 384), ("PRE", 192),
              ("VAL", 960), ("VV", 960), ("Rv", 192), ("Rf", 192), ("ysa", 384), ("onef", 128), ("SE2", 256), ("C32", 128), ("LI", 12), ("GBf", 8),
              ("RSA", 256), ("RSB", 128), ("RSC", 128), ("THR", 16), ("RSP", 384), ("RSi", 24), ("QS", 6),
              ("DO", 128), ("DE", 128), ("YO", 128), ("YE", 128), ("YW", 128), ("BT", 5), ("uc", 16), ("Ay", 1), ("FC", 16), ("FA", 2), ("wtf", 1))
         + tuple((q, 1) for q in ("qi", "qe", "qo", "qs1", "qa", "qb", "qy", "qr", "qg", "qv", "qf", "q23", "qc", "qd", "qs", "qp", "q64", "qx", "qw", "qu"))),
        (f2, (("o256", 256), ("ID", 128), ("NID", 128), ("I4K", 128), ("W4K", 128), ("BDt", 128), ("BD", 128), ("BDv", 128), ("BDf", 128),
              ("WT", 128), ("W64", 128), ("WY", 128), ("D15t", 128), ("D15", 128), ("Y15", 128), ("PERM", 160), ("SEG", 160), ("GBt", 8),
              ("GB", 8), ("GBs", 8), ("E2t", 64), ("E2", 64), ("WD", 8), ("WZ0", 384), ("WZ1", 384), ("LM", 192), ("nmh", 384), ("AV", 384), ("GV", 128),
              ("XF", 192), ("R1", 192), ("MM", 1920), ("MO", 1920))),
        (b2, (("XS", 2048), ("ZL", 192), ("z0s", 192), ("IDb", 128), ("NIb", 128), ("I8b", 128), ("I4b", 128), ("E2b", 64), ("ODt", 128), ("ODD", 128), ("sbh", 384),
              ("CI", 256), ("EQD", 256), ("CJ", 64), ("CK", 64), ("MK", 160), ("WNa", 384), ("WNb", 384), ("WN", 384), ("WX", 24), ("WR", 24), ("WA", 24),
              ("WPb", 128), ("WPd", 128), ("WP", 128), ("WH", 384), ("M", 3072), ("R", 3072), ("MX", 3072), ("AB", 3072), ("PEN", 192),
              ("hi", 192), ("Ax", 1))),
        (i4, (("ET", SP + 2048), ("v0s", 12), ("wts", 1), ("qI", 1), ("qJ", 1), ("qK", 1), ("qL", 1), ("RJ", 192), ("ui", 16), ("ua", 16), ("ud", 16), ("ue", 16))),
        (u2, (("LT", 128 * HOPS), ("RL", 192), ("AL", 192), ("POS", 24), ("PO3", 24), ("LD", 12), ("LE", 2)))):
    for n_, w_ in tiles:
        declare(n_, w_, t_)
for c_ in (0, 1):
    for n_, w_, t_ in (("Ma", 128, f4), ("Mb", 128, f4), ("Mc", 128, f4), ("NF", 8, f4), ("NS", 128, f2), ("WF", 256, f2)):
        declare(n_ + str(c_), w_, t_)
for b_ in range(8):
    SCRATCH["pb%d" % b_] = ("psum", [128, 512], f4)
    PLACE["pb%d" % b_] = ("pb%d" % b_, 0, 512)
SEMAPHORES = ["cV", "cS", "cP", "cG", "sent"] + ["ld%d" % k for k in range(5)] + ["st%d" % k for k in range(3)] + \
    ["a%s%d" % (m, t) for m in ("L0", "L1", "D0", "D1", "D", "M0", "Z0", "M1", "Z", "P1", "Z1", "ZP") for t in range(1, HOPS)]
ORDER = []


def meet(x, y):
    return x[1] < y[2] and y[1] < x[2] and not (x[1] - y[1]) % math.gcd(x[3], y[3])


def covers(x, y):
    return y[1] >= x[1] and y[2] <= x[2] and (x[3] == 1 or (y[3] == x[3] and y[1] == x[1]))


def make(g, T):
    eng = {"V": g.vector, "S": g.scalar, "P": g.tensor, "G": g, "Y": g.sync}
    cnt = {"V": 0, "S": 0, "P": 0, "G": 0}
    clk = {q: {} for q in eng}
    snap, acc, plan, sends, parts = {}, {}, [], {}, [(0, 0, "start")]

    def semof(r):
        return T.sem["c" + r] if r in cnt else T.sem[r]

    def B(name, a=None, b=None, step=1, r0=0, r1=128):
        name, o, w = PLACE[name]
        a, b = (o, o + w) if a is None else (o + a, o + b)
        return (T[name][r0:r1, a:b:step] if step != 1 else T[name][r0:r1, a:b], [(name, a, b, step)])

    def I(win, off):
        return (win[0].indirect(off[0]), win[1] + off[1])

    def learn(q, r, n):
        c = clk[q]
        c[r] = max(c.get(r, 0), n)
        for k, v in snap.get((r, n), {}).items():
            if c.get(k, 0) < v:
                c[k] = v

    def sync(q, reads, writes):
        need = {}
        for regs, w in ((reads, False), (writes, True)):
            for reg in regs:
                ps = reg[0].startswith("pb")
                for (rq, rn, old, rw) in acc.get(reg[0], ()):
                    hit = meet(reg, old)
                    if rq == q:
                        if q == "P" or not hit or not (w or rw):
                            continue
                    elif not (ps or (hit and (w or rw))):
                        continue
                    if need.get(rq, 0) < rn:
                        need[rq] = rn
        turn = sorted(need, key=lambda r: (r not in cnt, -need[r]))
        for final in (False, True):
            for r in turn:
                if clk[q].get(r, 0) >= need[r]:
                    continue
                if not final and any(o != r and clk[q].get(o, 0) < need[o] and snap[(o, need[o])].get(r, 0) >= need[r] for o in turn):
                    continue
                eng[q].wait_ge(semof(r), need[r])
                learn(q, r, need[r])

    def note(ev, n, reads, writes):
        for reg in writes:
            acc[reg[0]] = [x for x in acc.get(reg[0], []) if not covers(reg, x[2])] + [(ev, n, reg, True)]
        for reg in reads:
            acc[reg[0]] = [x for x in acc.get(reg[0], []) if not (x[0] == ev and not x[3] and x[2] == reg)] + [(ev, n, reg, False)]

    def size(x):
        return len(range(*x[1][0][1:]))

    def narrow(*xs):
        return all(SCRATCH[x[1][0][0]][2] in (f2, b2, u2) for x in xs)

    def cycles(q, o, ins, kind):
        if q == "P":
            return max(min(64, size(ins[0])), size(ins[1])) * (PE if narrow(ins[0]) else 4 * PE)
        if q == "G":
            return 150 + 2 * size(o)
        if kind == "load":
            return 2000
        if kind == "scatter":
            return 60 + SCATTER * size(ins[0])
        if ins and len(ins[0][1]) > 1:
            return 60 + GATHER * size(o)
        if kind == "two":
            return FIX + max(64, size(o) * (1 if any(x[1][0][0].startswith("pb") for x in ins) else 2))
        return FIX + max(64, size(o) * (0.5 if q == "V" and narrow(o, *ins[:1]) else 1))

    def op(q, fn, outs, ins, kind=None):
        reads = [r for i in ins for r in i[1]]
        writes = [r for o in outs for r in o[1]]

        def emit():
            sync(q, reads, writes)
            call = fn()
            cnt[q] += 1
            n = cnt[q]
            call.then_inc(semof(q), 1)
            snap[(q, n)] = dict(clk[q])
            snap[(q, n)][q] = n - 1
            note(q, n, reads, writes)
        plan.append((q, cycles(q, outs[0], ins, kind), 0, reads, writes, emit, kind if q == "P" else None,
                     "scatter" if kind == "scatter" else "gather" if ins and len(ins[0][1]) > 1 else None))

    def sc(x):
        return x[0] if isinstance(x, tuple) else x

    def tl(*xs):
        return [x for x in xs if isinstance(x, tuple)]

    def tt(o, a, b, f): op("V", lambda: eng["V"].tensor_tensor(o[0], a[0], b[0], f), [o], [a, b], "two")
    def ts(o, a, s1, s2, f0, f1=None):
        if f1 is None:
            op("V", lambda: eng["V"].tensor_scalar(o[0], a[0], sc(s1), None, f0), [o], [a] + tl(s1))
        else:
            op("V", lambda: eng["V"].tensor_scalar(o[0], a[0], sc(s1), sc(s2), f0, f1), [o], [a] + tl(s1, s2))
    def cp(o, a): op("V", lambda: eng["V"].tensor_copy(o[0], a[0]), [o], [a])
    def scat(q, tab, off, a):
        if q == "V":
            op("V", lambda: eng["V"].tensor_copy(tab[0].indirect(off[0]), a[0]), [tab], [a, off], "scatter")
        else:
            op("S", lambda: eng["S"].activation(tab[0].indirect(off[0]), a[0], F.Silu), [tab], [a, off], "scatter")
    def scan(o, a, b, i, f0, f1): op("V", lambda: eng["V"].tensor_tensor_scan(o[0], a[0], b[0], i, f0, f1), [o], [a, b])
    def fill(o, c): op("V", lambda: eng["V"].memset(o[0], c), [o], [])
    def act(o, a, f=F.Copy, scale=1.0, bias=0.0, total=None):
        if total is None:
            op("S", lambda: eng["S"].activation(o[0], a[0], f, bias=sc(bias), scale=sc(scale)), [o], [a] + tl(bias, scale), "load" if f == F.Silu else None)
        else:
            op("S", lambda: eng["S"].activation(o[0], a[0], f, bias=sc(bias), scale=sc(scale), accum_out=total[0]), [o, total], [a] + tl(bias, scale))
    def mm(o, l, r, st=True, sp=True, late=False):
        op("P", lambda: eng["P"].matmul(o[0], l[0], r[0], st, sp), [o if st and sp else B(o[1][0][0])], [l, r], None if st or sp or late else "free")
    def iota(o, pat, base, cm, whole=False):
        if whole:
            op("G", lambda: g.iota(o[0], pat, base, cm), [o], [])
        else:
            op("G", lambda: g.iota(o[0], pat, base, cm, allow_small_or_imprecise_dtypes=True), [o], [])
    def asel(o, a, pat, cop, fv, base, cm): op("G", lambda: g.affine_select(o[0], a[0], pat, cop, fv, base, cm), [o], [a])

    def dma(q, sem, out, in_, outs, ins):
        reads, writes = [r for i in ins for r in i[1]], [r for o in outs for r in o[1]]

        def emit():
            sync(q, reads, writes)
            eng[q].dma_start(out, in_).then_inc(T.sem[sem], 16)
            snap[(sem, 16)] = dict(clk[q])
            note(sem, 16, reads, writes)
        plan.append((q, 100, LAG + LW * sum(size(x) for x in outs), reads, writes, emit, None, None))

    def arrive(sem, n, b):
        def emit():
            snap[(sem, n)] = {}
            note(sem, n, [], b[1])
        plan.append((sem, 0, 0, [], b[1], emit, sends[sem], None))

    def send(core, dst, topo, o, i, rsem):
        def emit():
            sync("G", i[1], [])
            rid, pid = topo.addr(dst, core)
            g.remote_dma(o[0], i[0], T.sem[rsem], T.sem.sent, pid, rid, topo.mask(core, dst))
        sends[rsem] = len(plan)
        plan.append(("G", CALL if len(sends) > 1 else FIRST, FAR + 3 * size(i), i[1], [], emit, None, "send"))
        return len(topo.engines(core, dst))

    def part(t, what):
        parts.append((len(plan), t, what))

    def issue():
        if not ORDER:
            names = [(t, (what, i - a)) for (a, t, what), b in zip(parts, parts[1:] + [(len(plan),)]) for i in range(a, b[0])]
            ORDER.extend(order([x + (y,) for x, y in zip(plan, names)]))
        for i in ORDER:
            plan[i][5]()

    return dict(B=B, I=I, tt=tt, ts=ts, cp=cp, scat=scat, scan=scan, fill=fill, act=act, mm=mm, iota=iota, asel=asel, dma=dma,
                arrive=arrive, send=send, part=part, issue=issue, cnt=cnt)


def needs(plan):
    pred, acc, bank = [], {}, {}
    for i, (q, cost, lag, reads, writes, emit, after) in enumerate(x[:7] for x in plan):
        p, free = {}, after == "free"
        for regs, w in ((reads, False), ([] if free else writes, True)):
            for reg in regs:
                for (j, old, rw) in acc.get(reg[0], ()):
                    if (w or rw) and meet(reg, old):
                        d = (0 if q == "P" else OWN) if plan[j][0] == q else CROSS
                        p[j] = max(p.get(j, 0), d + plan[j][2])
        if q in ("P", "Y"):
            b = writes[0][0] if q == "P" else q
            for j in bank.get(b, [])[:1 if free else None]:
                p.setdefault(j, 0)
            bank[b] = bank[b] + [i] if free else [i]
        elif after is not None:
            p[after] = plan[after][2]
        pred.append(p)
        for reg in [] if free else writes:
            acc[reg[0]] = [x for x in acc.get(reg[0], []) if not covers(reg, x[1])] + [(i, reg, True)]
        for reg in reads:
            acc.setdefault(reg[0], []).append((i, reg, False))
    return pred


def order(plan):
    need, lumps, of = needs(plan), [], []
    for i, x in enumerate(plan):
        l = lumps[-1] if lumps else [i]
        y = plan[l[-1]]
        if lumps and x[0] == y[0] == "P" and (x[4][0][0], x[3][0][0], x[3][1][0]) == (y[4][0][0], y[3][0][0], y[3][1][0]) \
                and sum(plan[j][1] for j in l) + x[1] <= LUMP and {j for j in need[i] if plan[j][0] != "P"} <= {j for k in l for j in need[k]}:
            l.append(i)
        else:
            lumps.append([i])
        of.append(len(lumps) - 1)
    n = len(lumps)
    Q, C, lag = [plan[l[0]][0] for l in lumps], [sum(plan[j][1] for j in l) for l in lumps], [plan[l[0]][2] for l in lumps]
    pred, succ = [{} for _ in lumps], [{} for _ in lumps]
    for i, p in enumerate(need):
        for j, d in p.items():
            if of[j] != of[i]:
                pred[of[i]][of[j]] = succ[of[j]][of[i]] = max(pred[of[i]].get(of[j], 0), d)
    banks = [sorted({8 * int(r[0][2]) for j in l for r in plan[j][3] + plan[j][4] if r[0].startswith("pb")}) for l in lumps]
    qi = ["GPSVY".index(q) if len(q) == 1 else -1 for q in Q]

    def run(pred, succ, urge, head, tail, look):
        left, ready = [len(p) for p in pred], {}
        for i in range(n):
            if not left[i]:
                ready.setdefault(Q[i], {})[i] = head[i]
        free, end, used, out = {}, [0] * n, [-CROSS] * 64, []
        while len(out) < n:
            st = [{i: max([s, free.get(q, 0)] + [used[r] + CROSS for b in banks[i] for r in range(b, b + 5) if r != b + qi[i]]) for i, s in r.items()}
                  for q, r in ready.items() if r]
            st = min(st, key=lambda x: min(x.values()))
            s = min(st.values())
            i = max((j for j in st if st[j] <= s), key=lambda j: urge[j])
            i = max([j for j in st if st[j] < s + min(C[i], look) and urge[j] - urge[i] > st[j] - s] or [i], key=lambda j: urge[j] - st[j])
            end[i] = free[Q[i]] = st[i] + C[i]
            for b in banks[i]:
                used[b + qi[i]] = end[i]
            del ready[Q[i]][i]
            out.append(i)
            for k in succ[i]:
                left[k] -= 1
                if not left[k]:
                    ready.setdefault(Q[k], {})[k] = max([head[k]] + [end[j] + d for j, d in pred[k].items()])
        return max(end[i] + tail[i] for i in range(n)), out, end

    none = [0] * n
    soon = max(range(n), key=lambda i: C[i] if Q[i] == "S" else 0)
    best = cur = run(pred, succ, [-i for i in range(n)], none, lag, 0)
    for t in range(ROUNDS):
        back = run(succ, pred, cur[2], lag, none, 150 * (t % 4))[2]
        back[soon] += max(back)
        new = run(pred, succ, back, none, lag, 150 * (t % 4))
        cur, best = new if new[0] < 1.01 * cur[0] else cur, min(best, new)
    cases = []
    for wait, f in CASES:
        k = [f.get(plan[l[0]][7], 1) for l in lumps]
        late = [lag[i] * (k[i] if k[i] != 1 else wait) for i in range(n)]
        cases.append(([60 + (C[i] - 60) * k[i] for i in range(n)], late, CROSS * wait,
                      [[(j, (d - lag[j]) * wait + late[j]) for j, d in p.items()] for p in pred]))

    def replay(case, o, a, end, why, kept, limit):
        C, lag, CROSS, P = case
        free, used, top, last = kept[a // 40]
        free, used, end, why, kept = free[:], used[:], end[:], why[:], kept[:a // 40 + 1]
        for x in range(a // 40 * 40, n):
            if x == 40 * len(kept):
                kept.append((free[:], used[:], top, last))
            i = o[x]
            q, s, w, swap = qi[i], 0, -1, True
            if q >= 0:
                w, free[q] = free[q], i
                s = end[w] if w >= 0 else 0
            for j, d in P[i]:
                if end[j] + d >= s:
                    s, w, swap = end[j] + d, j, False
            for b in banks[i]:
                for r in range(b, b + 5):
                    j = used[r]
                    if j >= 0 and r != b + q and end[j] + CROSS > s:
                        s, w, swap = end[j] + CROSS, j, True
                used[b + q] = i
            end[i], why[i] = s + C[i], (w, swap)
            if end[i] + lag[i] > top:
                top, last = end[i] + lag[i], i
                if top > limit:
                    return None
        return top, last, end, why, kept

    def steps(why, i):
        runs, out = [[]], []
        while i >= 0:
            runs[-1].insert(0, i)
            if not why[i][1]:
                runs.append([])
            i = why[i][0]
        for r in runs:
            out += [(r[0], v, 0) for v in r[1:]] + [(u, r[-1], 1) for u in r[:-1]] + [(u, v, 0) for u, v in zip(r[1:], r[2:])]
            out += [(u, v, x) for u, v in zip(r, r[2:]) for x in (0, 1)]
        return out

    def shift(o, a, b, back):
        s = {o[a] if back else o[b]}
        for x in range(a + 1, b + 1) if back else range(b - 1, a - 1, -1):
            if not s.isdisjoint((pred if back else succ)[o[x]]):
                s.add(o[x])
        if o[a] in s and o[b] in s:
            return None
        return o[:a] + sorted(o[a:b + 1], key=lambda i: (i in s) == bool(back)) + o[b + 1:]

    name = [plan[l[0]][8] for l in lumps]
    twin = {x: i for i, x in enumerate(name)}
    at = [best[2][i] - C[i] for i in range(n)]
    head = [at[twin[(t, ("rings", 0))]] for t in range(HOPS)]
    r = min(range(1, HOPS - 1), key=lambda t: head[t + 1] - head[t])
    at = [at[twin[(r, x)]] + (t - r) * (head[r + 1] - head[r]) if (r, x) in twin else at[i] - head[t] + head[r] + (t - r) * (head[r + 1] - head[r])
          for i, (t, x) in enumerate(name)]
    o, left, ready = [], [len(p) for p in pred], {i for i in range(n) if not pred[i]}
    while ready:
        o.append(min(ready, key=lambda i: at[i]))
        ready.remove(o[-1])
        for k in succ[o[-1]]:
            left[k] -= 1
            if not left[k]:
                ready.add(k)
    now = [replay(c, o, 0, none, none, [([-1] * 5, [-1] * 64, 0, -1)], 1e18) for c in cases]
    best, todo, seed = (sum(x[0] for x in now), o), [], 1
    for step in range(STEPS):
        if not todo:
            todo, pos = [s for x in now for s in steps(x[3], x[1])], {i: x for x, i in enumerate(o)}
            if step >= ALIKE * STEPS:
                todo = [s for s in todo if name[s[1]][0] >= HOPS - 2 or (step % 8 == 0 and name[s[1]][0] == 0)] or todo
        seed = (seed * 1103515245 + 12345) % 2 ** 31
        u, v, back = todo.pop(seed // 8 % len(todo))
        new, room, r, spans = shift(o, pos[u], pos[v], back), SLACK * (1 - step / STEPS) * (seed % 1024) / 1024, [], [(pos[u], pos[v])]
        if new and step < ALIKE * STEPS:
            for d in range(1 - HOPS, HOPS):
                a, b = (pos.get(twin.get((name[x][0] + d, name[x][1])), -1) for x in (u, v))
                if 0 <= a < b and all(b < y or z < a for y, z in spans):
                    new = shift(new, a, b, back) or new
                    spans.append((a, b))
            room *= len(spans)
        for c, x in zip(cases, now):
            r.append(new and replay(c, new, min(spans)[0], x[2], x[3], x[4], x[0] + room + (SLACK if len(r) < len(now) - 1 else 0)))
            if not r[-1]:
                break
            room += x[0] - r[-1][0]
        else:
            o, todo, now = new, [], r
            best = min(best, (sum(x[0] for x in now), o))
    return [j for i in best[1] for j in lumps[i]]


def rank_program(g, core, T, topo):
    rank = T.rank_of(core)
    if rank is None:
        return
    K = make(g, T)
    B, I, tt, ts, cp, scat, scan, fill, act, mm, iota, asel, dma, part = (K[k] for k in (
        "B", "I", "tt", "ts", "cp", "scat", "scan", "fill", "act", "mm", "iota", "asel", "dma", "part"))
    nxt = T.cores[(rank + 3) % len(T.cores)]
    prv_eng = len(topo.engines(T.cores[(rank + 1) % len(T.cores)], core))
    ET, FT, FU, XS = B("ET", SP, SP + 2048), B("FT"), B("FU"), B("XS")

    def lin(name, o, a, bias):
        if name in ONS:
            act(o, a, bias=bias)
        else:
            ts(o, a, bias, None, A.add)

    def lst(t, c, kind, a=0, b=None):
        w = CHUNK[c][1] // 16
        o = 128 * t + {"vm": 32 * c, "v": 56 + 16 * c - w, "vf": 56 + 16 * c - w, "f": 56 + 16 * c, "fm": 80 + 32 * c}[kind]
        return B("LT", o + a, o + ((2 * w if kind == "vf" else w) if b is None else b))

    def msg(buf, t, c, j, j1=None):
        p0, n = CHUNK[c]
        o = 384 * t + 2 * p0
        return B(buf, o + n * j, o + n * (j + 1 if j1 is None else j1))

    def parts(m, t):
        if m[0] == "L":
            return lst(t + 1, int(m[1]), "v"), lst(t, int(m[1]), "f")
        if m[0] == "D":
            c, b = (int(m[1]), CHUNK[int(m[1])][1] // 4) if m[1:] else (0, 48)
            return lst(t + 1, c, "vm", 0, b), lst(t, c, "fm", 0, b)
        a, b = {"M0": (0, NA), "Z0": (NA, 2 * NA), "M1": (2 * NA, 384), "Z": (NA, 384), "P1": (2 * NA, 192 + NA), "Z1": (192 + NA, 384), "ZP": (NA, 192 + NA)}[m]
        return B("MM", 384 * (t + 1) + a, 384 * (t + 1) + b), B("MO", 384 * t + a, 384 * t + b)

    def col(name, c, h=None):
        p0, n = CHUNK[c]
        if h is None:
            return B(name, p0, p0 + n)
        return B(name, 2 * p0, 2 * p0 + 2 * n) if h == 2 else B(name, 2 * p0 + h * n, 2 * p0 + h * n + n)

    def W(c, n, a=0, b=128, st=1):
        return B(n, a, b, st, 0, CHUNK[c][1])

    def dedupe(c, t, kind):
        for b in range(CHUNK[c][1] // 64 - 1, -1, -1):
            s, (bk, d, e) = str(2 * c + b), BANK["same"][2 * c + b]

            def R(n, a, z, st=1):
                return B(n, a, z, st, 64 * b, 64 * b + 64)
            wf, wm = R("WF%d" % c, 0, 128), R("WF%d" % c, 128, 256)
            mm(B(bk, d, d + 160), wf, R("PERM", 0, 160), True, False)
            mm(B(bk, d, d + 160), wm, R("SEG", 0, 160), False, False)
            mm(B(bk, e, e + 49, 48), wm, R("GBs", 4 * b, 4 * b + 4, 2), False, False)
            mm(B(bk, e + 16, e + 97, 80), wm, R("GBs", 4 * b + 1, 4 * b + 4, 2), False, True)
            tt(B("eq" + s), B(bk, d, d + 160), B("MK"), A.is_equal)
            scan(B("dup" + s), B("eq" + s), B(bk, e, e + 160), 0.0, A.max, A.min)
            ts(lst(t, c, kind, 16 * b, 16 * b + 16), I(B("dup" + s), B("LE", 0, 1)), 4096.0, None, A.mult)

    def marks(q, tab, val, v0, t, c, kind):
        p0, n = CHUNK[c]
        for b in range(n // 64 - 1, -1, -1):
            scat(q, B(tab), lst(t, c, kind, 16 * b, 16 * b + 4), B(val, v0 + p0 + 64 * b, v0 + p0 + 64 * b + 64))

    def row(c, o, t):
        n = CHUNK[c][1]
        ps = B(BANK["row"][c], 0, n)
        mm(ps, W(c, "NS%d" % c), W(c, "ID", 0, n))
        act(o, ps, F.Identity, scale=B("qr"), bias=B("QS", t + 1, t + 2))

    dma("Y", "ld0", T.v0s[:], T.v0[:], [B("v0s")], [])
    dma("Y", "ld3", T.ET[:, SP:SP + 2048], T.en[:], [ET], [])
    dma("S", "ld1", T.z0s[:], T.z0[:], [B("z0s")], [])
    dma("S", "ld2", T.wts[:], T.wt[:], [B("wts")], [])
    dma("Y", "ld4", T.XS[:], T.xs[:], [B("XS")], [])

    def q(i):
        return B("EQD", i, i + 1)

    def mul(o, a, s1, s2=None):
        if s2 is None:
            ts(o, a, s1, None, A.mult)
        else:
            ts(o, a, s1, s2, A.mult, A.mult)

    for n, v in (("o256", 1.0), ("WNa", 128 * U), ("NS0", 0.0), ("NS1", 0.0), ("NF1", 0.0)):
        fill(B(n), v)
    fill(B("pb6", 256, 272), 0.0); fill(B("FT", 1024, FV), 2048.0)
    for a in range(FV, 2112, 544):
        iota(B("FT", a, min(2112, a + 544)), [[0, min(2112, a + 544) - a]], 2048, 0)
    for a in range(0, 1024, 256):
        act(B("FT", a, a + 256), B("o256"), F.Copy if a else F.Silu, scale=2048.0)
    for n, v in (("onef", 1), ("C32", 32), ("RSA", -15 * 2 ** 20), ("RSB", -15 * 2 ** 20), ("RSC", -15 * 2 ** 20)):
        if n in ONG:
            iota(B(n), [[0, PLACE[n][2]]], v, 0)
        else:
            act(B(n), B("o256", 0, PLACE[n][2]), scale=float(v))
    for a in (0, 192):
        act(B("RSP", a, a + 192), B("o256", 0, 192), scale=1.0e6)
    iota(B("qI"), [[0, 1]], 0, 1, True)
    iota(B("CI"), [[0, 16], [1, 16]], 0, 0)
    iota(B("LI"), [[1, 12]], 0, 0)
    iota(B("RSi"), [[-16, 24]], -16 - 4096, 0)
    iota(B("THR"), [[0, 2], [2048, 8]], int(BAR), 0)
    for j in range(4):
        iota(B("FU", 528 * j, 528 * j + 528), [[0, 528]], 2048, 0)
    iota(B("CJ"), [[1, 64]], 0, 0)
    for t in range(HOPS):
        iota(B("VV", 192 * t, 192 * t + 192), [[2, 192]], 1664 - 384 * t - 1, 0)
        iota(B("VAL", 192 * t, 192 * t + 192), [[2, 192]], 1664 - 384 * t, 0)
    iota(B("qp"), [[0, 1]], -2, -4)
    for c in (0, 1):
        act(B("NS%d" % c, 1, 128, 16), B("o256", 0, 8), scale=CC)
        for i in (2, 3):
            act(B("NS%d" % c, i, 128, 16), B("o256", 0, 8), F.Identity, scale=-4.0 * CHUNK[c][0], bias=B("qp"))
    asel(B("BDt"), B("o256", 0, 128), [[-16, 8], [0, 16]], A.is_ge, 0.0, 0, 1)
    asel(B("BD"), B("BDt"), [[16, 8], [0, 16]], A.is_ge, 0.0, 15, -1)
    asel(B("ID"), B("o256", 0, 128), [[-1, 128]], A.is_equal, 0.0, 0, 1)
    asel(B("D15t"), B("o256", 0, 128), [[-1, 128]], A.is_equal, 0.0, 15, 1)
    for h in (0, 1):
        asel(B("SE2", 128 * h, 128 * h + 128), B("onef"), [[-1, 8], [-16, 8], [8 - 16 * (1 - h), 2]], A.is_equal, 0.0, -8 * h, 1)
    asel(B("E2t"), B("o256", 0, 64), [[-2, 64]], A.is_ge, 0.0, 0, 1)
    asel(B("E2"), B("E2t"), [[2, 64]], A.is_ge, 0.0, 1, -1)
    iota(B("ODt"), [[0, 8], [1, 2], [0, 8]], 0, 0)
    asel(B("GBt"), B("o256", 0, 8), [[-16, 8]], A.is_ge, 0.0, 0, 1)
    asel(B("GBf"), B("GBt"), [[16, 8]], A.is_ge, 0.0, 15, -1)
    act(B("GB"), B("GBf")); tt(B("GB4"), B("GBf", 0, 4), B("GBf", 4, 8), A.add)
    asel(B("WNb"), B("WNa"), [[0, 48], [-16, 8]], A.is_ge, 0.0, 0, 1)
    asel(B("WNa"), B("WNb"), [[0, 48], [16, 8]], A.is_ge, 0.0, 15, -1)
    asel(B("WN"), B("WNa"), [[-1, 16], [0, 3], [-16, 8]], A.not_equal, 2.0 ** 26, 0, 1)
    ts(B("qJ"), B("qI"), 15, None, A.bitwise_and); cp(B("qi"), B("qJ")); ts(B("qK"), B("qJ"), 1, None, A.bitwise_and)
    ts(B("qL"), B("qI"), 63, None, A.bitwise_and)
    ts(B("EQD"), B("CI"), B("qi"), None, A.is_equal)
    for n, a, s, b in (("wtf", B("wts"), 1.0, 0.0), ("qa", B("qi"), 2048.0, -2048 * (15.5 + T0)), ("qe", B("qK"), -1.0, 1.0), ("qs1", B("qi"), 1.0, 1.0), ("qb", B("qi"), 1 / 4096, 0.5),
                       ("q64", B("qL"), 1.0, 1.0), ("qx", q(1), 32.0, 15.0), ("GB4", B("GB4"), -1.0, 0.0),
                       ("qr", q(1), -31 / 32, 1.0), ("qg", B("qi"), U / HI, -1.0), ("qc", q(1), T0 - CC / 32, 0.0)):
        act(B(n), a, scale=s, bias=b)
    for n, a, s, b in (("qy", q(1), 2048.0, q(0)), ("qv", q(3), 4096.0, q(0)), ("qf", q(2), 4096.0, q(0)), ("q23", q(2), 1.0, q(3)),
                       ("qd", q(2), -4096.0, B("qc")), ("qs", q(3), -3328.0, B("qd")), ("qw", q(2), 80.0, B("qx")), ("qu", q(3), 144.0, B("qw"))):
        act(B(n), a, F.Identity, scale=s, bias=b)
    ts(B("qo"), B("qK"), q(15), None, A.subtract); act(B("q23"), B("q23"), scale=768.0)
    ts(B("QS"), B("LI", 0, 6), B("q23"), B("qs"), A.mult, A.add)
    ts(B("ODD"), B("ODt"), B("qe"), 2.0 ** 45, A.is_equal, A.mult)
    cp(B("LD"), B("LI"))
    cp(B("LE", 0, 1), B("qu")); ts(B("CK"), B("CJ"), B("qi"), None, A.subtract)
    for a in range(4):
        o, n = 8 * a * (a + 1), 16 * a + 16
        ts(B("MK", o, o + n), B("CK", 0, n), 16.0 * a + 1, 4096.0, A.is_ge, A.mult)
        ts(B("PERM", o, o + n), B("CJ", 0, n), B("q64"), None, A.is_equal)
        ts(B("SEG", o, o + n), B("CJ", 0, n), 0.5, B("GB4", a, a + 1), A.is_ge, A.mult)
        act(B("CD", o, o + n), B("o256", 0, n), F.Identity, scale=a / 256, bias=B("qb"))
    for bk, d, e in BANK["same"]:
        act(B(bk, e, e + 160), B("CD"))
    act(B("RSP", 0, 384, 16), B("RSi"), F.Identity, bias=B("qi"))
    act(B("RSB", 0, 128, 16), B("THR", 0, 8)); act(B("RSC", 0, 128, 16), B("THR", 0, 8), bias=CC)
    for n, a, v in (("IDb", "ID", 1.0), ("NIb", "ID", -1.0), ("NID", "ID", -1.0), ("I4K", "ID", 4096.0), ("W4K", "ID", -4096.0), ("I8b", "ID", 8192.0), ("I4b", "ID", 4096.0), ("WP", "ID", -65536.0),
                    ("WPd", "ID", B("qg")), ("BDv", "BD", B("qv")), ("BDf", "BD", B("qf")), ("WY", "BD", B("qy")), ("D15", "D15t", q(0)), ("E2b", "E2", 1 / 64)):
        mul(B(n), B(a), v)
    for n, i, v in (("WT", 1, 2048.0), ("W64", 1, -64.0), ("Y15", 0, 16.0), ("WPb", 0, -70.0)):
        mul(B(n), B("BD"), q(i), v)
    tt(B("WH", 0, 128), B("WPb"), B("WPd"), A.add); cp(B("WH", 128, 256), B("WH", 0, 128)); cp(B("WH", 256, 384), B("WH", 0, 128))
    for n, v in (("WX", 1 / 4), ("WR", -1 / 8), ("WA", 1 / 8)):
        act(B(n), B("WNa", 0, 24), scale=v)
    act(B("WD"), B("GB"), scale=B("wtf")); act(B("GBs"), B("GBf"), scale=1 / 4096)
    for c in (0, 1):
        if KS[c] < 16 // WD:
            for j in range(3):
                mul(B("WZ%d" % c, 128 * j, 128 * j + 128), B("BD"), -16 * U)
            if KS[c]:
                asel(B("WZ%d" % c), B("WZ%d" % c), [[0, 24 * WD], [1, 16 // WD]], A.is_ge, 0.0, -KS[c], 0)
    for t in range(HOPS - 1):
        act(B("BT", t, t + 1), q(15), scale=2048.0 * (9 + t))
    for n, a, v in (("DE", "ID", "qe"), ("DO", "ID", "qo"), ("YW", "BD", "qs1"), ("YE", "YW", "qe"), ("YO", "YW", "qo")):
        act(B(n), B(a), scale=B(v))

    cp(B("v0f"), B("v0s"))
    tt(B("LM"), I(B("v0f"), B("LD")), B("EQD", 0, 192), A.mult)
    for c in (0, 1):
        p0, n = CHUNK[c]
        cp(lst(0, c, "v"), B("v0s", p0 // 16, (p0 + n) // 16))
        bk = BANK["lst"][c]
        mm(W(c, bk, 256, 384), col("LM", c), B("BD")); mm(W(c, bk, 384, 512), col("LM", c), B("ID"))
        act(W(c, "WF%d" % c, 0, 256), W(c, bk, 256, 512))
        act(W(c, "NS%d" % c, 0, 128, 16), W(c, "WF%d" % c, 0, 128, 16))
        row(c, msg("MM", 0, c, 0), -1)
        cp(msg("MM", 0, c, 1), col("z0s", c))
        dedupe(c, 0, "vm")

    sent = 0
    for t in range(HOPS):
        last = t == HOPS - 1
        part(t, "arrivals")
        if t > 0:
            for m in SENDS:
                K["arrive"]("a%s%d" % (m, t), prv_eng, parts(m, t - 1)[0])

        def bc(name, c, k, st=16):
            return B(name, 16 * CHUNK[c][0] + k, 16 * (CHUNK[c][0] + CHUNK[c][1]), st)

        def bp(name, c, p, j, m=MP):
            p0, n = CHUNK[c]
            return B(name, 16 * (p0 + p) + j, 16 * (p0 + min(n, p + m)), 16 // WD)

        def halves(c):
            return range(CHUNK[c][0] // 64, (CHUNK[c][0] + CHUNK[c][1]) // 64)

        def key(c, k):
            return W(c, "pb%d" % (2 + c), k, 384, 16)

        def ring(c):
            p0, n = CHUNK[c]
            for p in range(0, n, RP):
                ts(B("RJ", p0 + p, p0 + min(n, p + RP)), I(ET, lst(t, c, "v", p // 16, min(n, p + RP) // 16)), 2047, None, A.bitwise_and)
                cp(B("RL", p0 + p, p0 + min(n, p + RP)), B("RJ", p0 + p, p0 + min(n, p + RP)))

        def rings(q, a, b):
            for p in range(a, b, PC):
                o, i = B("X", 16 * p, 16 * min(b, p + PC)), I(ET, B("RL", p, min(b, p + PC)))
                if q == "V":
                    ts(o, i, B0, None, A.add)
                else:
                    act(o, i, bias=B0)

        def records(q, a, b):
            for p in range(a, b, PC):
                (cp if q == "V" else act)(B("R", 16 * p, 16 * min(b, p + PC)), I(XS, B("AL", p, min(b, p + PC))))

        def pick(c):
            for h in halves(c):
                bk = BANK["pick"][h]
                sb, nm = (B(x, 128 * h, 128 * h + 128) for x in ("sbh", "nmh"))
                mm(B(bk, 0, 128), B("IDb"), B("ODD"), True, False)
                for k in range(8):
                    i = (k + t) % 16
                    mm(B(bk, k, 128, 8), B("X", 1024 * h + k, 1024 * h + 1024, 8), B("SE2", 16 * i, 16 * i + 16), False, False)
                mm(B(bk, 0, 128), B("NIb"), B("ODD"), False, True)
                lin("sb", sb, B(bk, 0, 128), -511.5)
                tt(nm, B(bk, 0, 128), sb, A.subtract)
                o = B(BANK["names"][h], 128, 192)
                if t > 0:
                    mm(o, B("WP"), B("PEN", 64 * h, 64 * h + 64), True, False)
                mm(o, nm, B("E2"), t == 0, True)
                cp(B("AL", 64 * h, 64 * h + 64), o)
                lin("hi", B("hi", 64 * h, 64 * h + 64), o, HI - 511.5)

        def older(c):
            n, bk = CHUNK[c][1], BANK["thr"][c]
            a = 512 - WD * n
            if t > 0:
                for m in range(WD):
                    mm(B(bk, a + m, 512, WD), B("WT"), msg("MM", t, c, 0))
                if "pen" in ONS:
                    act(col("PEN", c), B(bk, a, 512, WD), F.Relu, bias=B("qa"))
                else:
                    ts(col("PEN", c), B(bk, a, 512, WD), B("qa"), 0.0, A.add, A.max)
            zsum = KS[c] < 16 // WD
            if zsum:
                mm(W(c, "pb%d" % (2 + c), 0, 384), msg("MM", t, c, 1), B("WZ%d" % c), True, False)
            for j in range(16 // WD):
                for p in range(0, n, MP):
                    if t > 0:
                        tt(bp("M", c, p, j), bp("X", c, p, j), B(bk, a + WD * p, a + WD * min(n, p + MP)), A.is_lt)
                    else:
                        ts(bp("M", c, p, j), bp("X", c, p, j), 2048 * T0, None, A.is_lt)
                for k in range(j, 16, 16 // WD):
                    i = (k + t) % 16
                    mm(key(c, k), bc("M", c, k), B("WN", 24 * i, 24 * i + 24), k == 0 and not zsum, False)

        def entry(c, name, a, w, stop=False):
            for h in halves(c):
                mm(B("pb%d" % (2 + c), a, a + 128, 1, 64 * (h % 2), 64 * (h % 2) + 64), B(w), B(name, 128 * h, 128 * h + 128), False, stop)

        def sizes(c):
            p0, n = CHUNK[c]
            kk, J, z = W(c, "pb%d" % (2 + c), 0, 384), 16 // WD, msg("MM", t, c, 1)
            bk, a = BANK["zz"][c], 512 - WD * n
            ks, m, sums = [k for k in range(16) if k % J < KS[c]], 512 // n, []
            mm(kk, col("hi", c), B("WH"), False, False, KS[c] == J)
            entry(c, "sbh", 256, "E2b")
            if KS[c] == J:
                entry(c, "nmh", 0, "E2")
            else:
                for j in range(WD):
                    mm(B(bk, a + j, 512, WD), B("ID"), z)
            for k in range(16):
                if k not in ks:
                    mm(key(c, k), bc("R", c, k), B("WR"), False, False)
            for x in range(max(J - KS[c], -(-len(ks) // m))):
                part, db = ks[m * x:m * x + m], BANK["diff"][(x + c * KS[0]) % 2]
                for j, k in enumerate(part):
                    mm(B(db, j * n, j * n + n), B("NID"), z, j == 0, False)
                for j, k in enumerate(part):
                    mm(B(db, j * n, j * n + n), B("IDb"), bc("R", c, k), False, k == part[-1])
                o = 16 * p0 + m * x * n
                if part:
                    act(B("AB", o, o + len(part) * n), B(db, 0, len(part) * n), F.Abs)
                if KS[c] + x < J:
                    for p in range(0, n, XP):
                        tt(bp("MX", c, p, KS[c] + x, XP), bp("R", c, p, KS[c] + x, XP), B(bk, a + WD * p, a + WD * min(n, p + XP)), A.max)
                    sums += [(k, bc("MX", c, k), "WX") for k in range(KS[c] + x, 16, J)]
                sums += [(k, B("AB", o + j * n, o + j * n + n), "WA") for j, k in enumerate(part)]
            for k, d, w in sums:
                mm(key(c, k), d, B(w), False, KS[c] == J and k == sums[-1][0])
            if KS[c] < J:
                entry(c, "nmh", 0, "E2", True)

        def fused(c):
            p0, n = CHUNK[c]
            mm(W(c, "pb%d" % (2 + c), 0, 384), col("hi", c), B("WH"), False, False, True)
            entry(c, "sbh", 256, "E2b"); entry(c, "nmh", 0, "E2")
            for k in range(16):
                asel(bc("MX", c, k), msg("MM", t, c, 1), [[0, n]], A.is_equal, 0.0, 0, 0)
            for p in range(p0, p0 + n, FUSE):
                tt(B("R", 16 * p, 16 * (p + FUSE)), I(XS, B("AL", p, p + FUSE)), B("MX", 16 * p, 16 * (p + FUSE)), A.subtract)
                act(B("AB", 16 * p, 16 * (p + FUSE)), B("R", 16 * p, 16 * (p + FUSE)), F.Abs)
            for k in range(16):
                mm(key(c, k), bc("AB", c, k), B("WA"), False, k == 15)

        def hash_():
            for c in (0, 1):
                mm(W(c, "pb6", 256 + 8 * c, 264 + 8 * c), msg("MM", t, c, 1), B("WD"))
            cp(B("ui"), B("pb6", 256, 272))
            ts(B("ua"), B("ui"), 2047, None, A.bitwise_and)
            act(B("uc"), B("ua"), F.Square, bias=592.0)
            if t > 0:
                act(B("Ax"), B("pb6", 272, 273), scale=-1.0, bias=4080 - 17 * 65536.0)
                act(B("Ay"), B("pb6", 272, 273), F.Identity, bias=B("Ax"))
                ts(B("ud"), B("uc"), B("Ay"), -592.0 ** 2, A.add, A.add)
            else:
                ts(B("ud"), B("uc"), -592.0 ** 2, None, A.add)
            ts(B("ue"), B("ud"), 5, 2047, A.arith_shift_right, A.bitwise_and)
            tt(B("RSA", 0, 256, 16), B("THR"), B("ue"), A.add)

        def least(c):
            s, kk = str(c), "pb%d" % (2 + c)
            ma, mb, mc = (W(c, x + s, 15, 128, 16) for x in ("Ma", "Mb", "Mc"))
            wide = I(B("NF" + s), B("LD", 0, 8))
            scan(W(c, "Ma" + s), W(c, "RSA", 128 * c, 128 * c + 128), W(c, kk), 0.0, A.max, A.min)
            scan(W(c, "Mb" + s), W(c, "RSB"), W(c, kk, 128, 256), 0.0, A.max, A.min)
            tt(W(c, "NF" + s, 0, 8), ma, mb, A.subtract)
            act(B("WF" + s, 0, 128), wide)
            tt(B("WF" + s, 128, 256), wide, B("EQD", 0, 128), A.mult)
            scan(W(c, "Mc" + s), W(c, "RSC"), W(c, kk, 256, 384), 0.0, A.max, A.min)
            if "ns" in ONS:
                act(W(c, "NS" + s, 0, 128, 16), W(c, "NF" + s, 0, 8))
            else:
                tt(W(c, "NS" + s, 0, 128, 16), ma, mb, A.subtract)
            tt(W(c, "NS" + s, 1, 128, 16), mc, mb, A.subtract)
            o = B(BANK["lst"][c], 240, 240 + CHUNK[c][1] // 16)
            mm(o, W(c, "WF" + s, 128, 256), W(c, "GB", 0, CHUNK[c][1] // 16))
            cp(lst(t, c, "f"), o)
            row(c, msg("MO", t, c, 0), t)

        def zproc(c):
            n, (bk, a, b) = CHUNK[c][1], BANK["zp"][c]
            p1, p2 = B(bk, a, a + n), B(bk, b, b + n)
            act(col("XF", c), I(XS, lst(t, c, "f")))
            mm(p1, B("W64"), msg("MO", t, c, 0), True, False)
            mm(p1, B("ID"), col("XF", c), False, True)
            act(col("R1", c), p1, F.Relu, bias=64 * T0)
            mm(p2, B("ID"), msg("MM", t, c, 1), True, False)
            mm(p2, B("NID"), col("R1", c), False, True)
            act(col("ZL", c) if last else msg("MO", t, c, 1), p2, F.Abs)

        def meetings(c):
            p0, n = CHUNK[c]
            wo, we, w15 = ("YO", "YE", "Y15") if last else ("DO", "DE", "D15")
            bk = BANK["new"][c]
            for h, (own, oth, new) in enumerate((("Rv", "Rf", "MO"), ("Rf", "Rv", "MM"))):
                o = B(bk, n * h, n * h + n)
                mm(o, B(w15), msg(new, t, c, 0), h == 0, False)
                mm(o, B(wo), col(own, c), False, False)
                mm(o, B(we), col(oth, c), False, h == 1)
            act(col("NN", c, 2), B(bk, 0, 2 * n), F.Identity, bias=16 * 2048.0 * (9 + t) if last else B("BT", t, t + 1))
            tt(col("PRE", c), I(FU if c else FT, lst(t, c, "f")), B("VAL", 192 * t + p0, 192 * t + p0 + n), A.min)
            marks(MQ[c], "FU" if c else "FT", "PRE", 0, t, c, "fm")
            for q, h, kind in {"S": [("S", 2, "vf")], "V": [("V", 2, "vf")], "SV": [("S", 0, "v"), ("V", 1, "f")]}[LQ[c]]:
                if q == "S":
                    act(col("AV", c, h), I(FU if c else FT, lst(t, c, kind)))
                else:
                    tt(col("AV", c, h), I(FU if c else FT, lst(t, c, kind)), B("EQD", 0, len(kind) * n), A.add)
            if c:
                top = 1664.0 - 384 * t + 2 * NA
                if "gv" in ONS:
                    act(B("GV"), I(FT, lst(t, c, "vf")), F.Relu, scale=-1.0, bias=top)
                else:
                    ts(B("GV"), I(FT, lst(t, c, "vf")), top, 4096.0, A.is_lt, A.mult)

        def stand(cs):
            bk, a, b = "pb%d" % (2 + cs[0]), 2 * CHUNK[cs[0]][0], 2 * sum(CHUNK[cs[-1]])
            terms = [(c, h, "I8b" if LQ[c] == "S" else "I4b", B("EQD", 0, CHUNK[c][1])) for c in cs if LQ[c] != "V" for h in (0, 1)]
            terms += [(c, h, w, msg(m, t, c, 0)) for h, (w, m) in enumerate((("BDv", "MM"), ("BDf", "MO"))) for c in cs]
            for c in cs:
                if c:
                    terms += [(c, h, "W4K" if "gv" in ONS else "NID", B("GV", 64 * x, 64 * x + 64)) for x in (0, 1) for h in (0, 1)]
                terms += [(c, h, "I4K", col("AV", c, x)) for x in (0, 1) for h in (0, 1)]
            for x, (c, h, w, r) in enumerate(terms):
                mm(col(bk, c, h), B(w), r, x == 0, x == len(terms) - 1)
            scan(B("ysa", a, b), B("RSP", a, b), B(bk, a, b), 1.0e6, A.min, A.max)
            pos = "PO3" if t == HOPS - 2 else "POS"
            ts(B(pos, a // 16, b // 16), B("ysa", a + 15, b, 16), SP + 4096.0, None, A.add)
            if APART == 2:
                a = 0 if b == 384 else b
            if a < b:
                scat("V", B("YS" if last else "ET"), B(pos, a // 16, b // 16), B("NN", a, b))

        def ysum(when):
            part(t, "sums %d" % when)
            for a in range(0, 2048, 512):
                if (t, when) == (HOPS - 1 if YT[a // 256] >= YN else HOPS - 2, 0):
                    asel(B("EF", a, a + 512), B("ET", SP + a, SP + a + 512), [[0, 512]], A.is_equal, 0.0, 0, 0)
            if (t, when) == YN:
                for a in range(0, 384, YS):
                    scat("V", B("YS"), B("PO3", a // 16, (a + YS) // 16), B("NY", a, a + YS))
            for j in range(8):
                if YT[j] == (t, when):
                    for y in (0, 128):
                        mm(B("pb6", y, y + 128), B("YW"), B("EF", 256 * j + y, 256 * j + y + 128))
                    act(B("YS", SP + 256 * j, SP + 256 * j + 256), B("pb6", 0, 256))

        part(t, "rings")
        ring(0); ring(1)
        for h in range(3):
            rings("V", 64 * h, 64 * h + EV[h]); rings("S", 64 * h + EV[h], 64 * h + 64)
        ysum(0)
        part(t, "candidates" if t else "first candidates")
        for c in (0, 1):
            act(col("Rv", c), I(ET, lst(t, c, "v")))
            older(c)
        pick(0); pick(1)
        hash_()
        part(t, "records")
        marks(MV[0], "FT", "VV", 192 * t, t, 0, "vm"); marks(MV[1], "FU", "VV", 192 * t, t, 1, "vm")
        for h in range(2 if FUSE else 3):
            records("V", 64 * h, 64 * h + RV[h]); records("S", 64 * h + RV[h], 64 * h + 64)
        sizes(0); (fused if FUSE else sizes)(1)
        ysum(1)
        part(t, "least")
        for c in (0, 1):
            least(c); dedupe(c, t, "fm"); zproc(c)
            act(col("Rf", c), I(ET, lst(t, c, "f")))
        part(t, "sends")
        if not last:
            for m in SENDS:
                sent += K["send"](core, nxt, topo, *parts(m, t), "a%s%d" % (m, t + 1))
        part(t, "meetings")
        meetings(0); meetings(1)
        for cs in ((0,), (1,)) if APART else ((0, 1),):
            stand(cs)
        part(t, "new sums")
        if t == HOPS - 2:
            for a in range(0, 384, 128):
                mm(B(BANK["ny"], a, a + 128), B("YW"), B("NN", a, a + 128))
            act(B("NY"), B(BANK["ny"], 0, 384))
        part(t, "failures")
        if not last:
            for c in (0, 1):
                act(W(c, "FC", 8 * c, 8 * c + 8), W(c, "NS%d" % c, 1, 128, 16), F.Relu, scale=-1 / 32, bias=1 + CC / 32, total=W(c, "FA", c, c + 1))
            for c in (0, 1):
                mm(B("pb6", 272, 273), W(c, "C32"), W(c, "FA", c, c + 1), c == 0, c == 1)
            ysum(2)

    t = HOPS - 1
    part(t, "end")
    dma("S", "st0", T.yz[:], T.ZL[:], [], [B("ZL")])
    for c in (0, 1):
        mm(col("pb4", c), B("WY"), msg("MO", t, c, 0))
    act(B("YP"), B("pb4", 0, 192), bias=-2048 * T0)
    dma("S", "st1", T.yp[:], T.YP[0:128:16, :], [], [B("YP")])
    dma("Y", "st2", T.ys[:], T.YS[0:128:16, SP:SP + 2048], [], [B("YS")])

    K["issue"]()
    for q_ in ("V", "S", "P", "G"):
        g.wait_ge(T.sem["c" + q_], K["cnt"][q_])
    for j in range(5):
        g.wait_ge(T.sem["ld%d" % j], 16)
    for j in range(3):
        g.wait_ge(T.sem["st%d" % j], 16)
    g.wait_ge(T.sem.sent, sent)
